import numpy as np
import ml_dtypes


def mxq(x, axis, fmt="e4m3"):
    dtype, down = {"e4m3": (ml_dtypes.float8_e4m3fn, 7), "e5m2": (ml_dtypes.float8_e5m2, 14)}[fmt]
    v = np.moveaxis(np.asarray(x, np.float32).astype(ml_dtypes.bfloat16).astype(np.float64), axis, -1)
    blocks = v.reshape(v.shape[:-1] + (-1, 32))
    amax = np.abs(blocks).max(-1, keepdims=True)
    byte = np.maximum(np.where(amax > 0, np.frexp(amax)[1] - 1 + 127, 0) - down, 1)
    scale = np.exp2(byte - 127.0)
    codes = (blocks / scale).astype(np.float32).astype(dtype).astype(np.float64)
    return np.moveaxis((codes * scale).reshape(v.shape), -1, axis)


WIDE = False


def mx_kscale(k):
    if not WIDE:
        return np.ones(k)
    levels = np.array([10, -10, 5, -5, 0])
    if k % 512:
        return np.exp2(np.random.permutation(np.resize(levels, k // 32))).repeat(32)
    a = np.empty((k // 512, 16))
    for p in range(k // 512):
        a[p, :8] = np.random.permutation(np.resize(levels, 8))
        for g in range(8):
            far = levels[np.abs(levels - a[p, g]) >= 10]
            a[p, g + 8] = far[np.random.randint(len(far))]
    return np.exp2(a.ravel()).repeat(32)


def f64(x):
    return np.asarray(x).astype(np.float64)


def striped(idx):
    return np.tile(idx.reshape(-1, 16).T, (8, 1)).astype(np.uint16)


def unstriped(offs):
    return offs[:16].T.reshape(-1).astype(np.int64)


E2M1 = np.array([0.0, 0.5, 1.0, 1.5, 2.0, 3.0, 4.0, 6.0, -0.0, -0.5, -1.0, -1.5, -2.0, -3.0, -4.0, -6.0])


def pack_weight(w, fmt):
    k, n = w.shape
    w = f64(np.asarray(w, np.float32).astype(ml_dtypes.bfloat16)).reshape(k // 32, 32, n)
    amax = np.abs(w).max(1)
    if fmt == "e4m3":
        byte = np.frexp(amax)[1] - 1 + 127 - 7
    else:
        mant, ex = np.frexp(amax / 6.0)
        byte = np.where(mant > 0.5, ex, ex - 1) + 127
    byte = np.clip(np.where(amax > 0, byte, 1), 1, 254)
    scaled = (w * np.exp2(127.0 - byte)[:, None, :]).reshape(k, n).astype(np.float32)
    by_word = np.ascontiguousarray(scaled.reshape(k // 512, 128, 4, n).transpose(0, 1, 3, 2))
    if fmt == "e4m3":
        words = by_word.astype(ml_dtypes.float8_e4m3fn).view(np.uint8)
    else:
        c = by_word.astype(ml_dtypes.float4_e2m1fn).view(np.uint8) & 0xF
        words = (c[..., 0::2] | (c[..., 1::2] << 4)).reshape(k // 512, 128, 2 * n)
    return np.ascontiguousarray(words), np.ascontiguousarray(byte.astype(np.uint8).reshape(k // 512, 16, n))


def unpack_weight(words, scales, fmt):
    g, _, n = scales.shape
    words = np.ascontiguousarray(words).reshape(g, 128, n, -1)
    if fmt == "e4m3":
        vals = words.view(ml_dtypes.float8_e4m3fn).astype(np.float64)
    else:
        nib = np.empty((g, 128, n, 4), np.uint8)
        nib[..., 0::2] = words & 0xF
        nib[..., 1::2] = words >> 4
        vals = E2M1[nib]
    vals = vals * np.repeat(np.exp2(scales.astype(np.float64) - 127.0), 8, axis=1)[..., None]
    return vals.transpose(0, 1, 3, 2).reshape(g * 512, n)


def gelu(v):
    return 0.5 * v * (1.0 + np.tanh(np.sqrt(2.0 / np.pi) * (v + 0.044715 * v**3)))


K, T, S, T2, P, H, N = 512, 2048, 1024, 2048, 1024, 1024, 512

def setup_inputs():
    n = np.random.standard_normal
    s = mx_kscale(K)[:, None]
    u = mx_kscale(H)[:, None]
    tab_words, tab_scales = pack_weight(n((K, T)) * s, "e4m3")
    w1_words, w1_scales = pack_weight(n((K, H)) / np.sqrt(K) / s, "e2m1")
    w2 = n((K, H)) / np.sqrt(K) / s
    w3_words, w3_scales = pack_weight(n((K, H)) / np.sqrt(K) / s * u.T, "e4m3")
    w4 = n((H, N)) / np.sqrt(H) / u
    return {
        "tab_words": tab_words, "tab_scales": tab_scales,
        "offs": striped(np.random.permutation(T)[:S]),
        "w1_words": w1_words, "w1_scales": w1_scales,
        "w2": w2.astype(np.float32),
        "w3_words": w3_words, "w3_scales": w3_scales,
        "wgs": np.exp(0.3 * n((128, S))).astype(np.float32),
        "offs2": striped(np.random.permutation(T2)[:S]),
        "offs3": striped(np.random.permutation(T2)[:P]),
        "ctx": (n((H, P)) * u).astype(np.float32),
        "w4": w4.astype(np.float32),
    }

def reference(tab_words, tab_scales, offs, w1_words, w1_scales, w2, w3_words, w3_scales, wgs, offs2, offs3, ctx, w4):
    v = unpack_weight(tab_words, tab_scales, "e4m3")[:, unstriped(offs)]
    d = np.maximum(unpack_weight(w1_words, w1_scales, "e2m1").T @ v, 0.0)
    q = (mxq(f64(w2), 0, "e4m3").T @ v) + d
    gate = q / (1.0 + np.exp(-q))
    h = (unpack_weight(w3_words, w3_scales, "e4m3").T @ v) * gate
    page = np.zeros((H, T2))
    page[:, unstriped(offs2)] = np.tile(f64(wgs), (H // 128, 1)) * h
    x = page[:, unstriped(offs3)]
    z = np.abs(x) + f64(ctx)
    out = mxq(f64(w4), 0, "e4m3").T @ mxq(z, 0, "e4m3")
    return out

@@ -1,0 +1,291 @@
+from contextlib import ExitStack
+
+import concourse.mybir as mybir
+from concourse.masks import make_identity
+
+K, T, S, T2, PM, H, N = 512, 2048, 1024, 2048, 1024, 1024, 512
+FLOPS = 2 * (3 * K * H * S + H * N * PM)
+
+F32 = mybir.dt.float32
+BF16 = mybir.dt.bfloat16
+I32 = mybir.dt.int32
+U32 = mybir.dt.uint32
+U16 = mybir.dt.uint16
+U8 = mybir.dt.uint8
+FP8X4 = mybir.dt.float8_e4m3fn_x4
+FP4X4 = mybir.dt.float4_e2m1fn_x4
+ALU = mybir.AluOpType
+ACT = mybir.ActivationFunctionType
+
+P = 128
+PACK = 4
+BANK = 512
+GROUPS = ((0, 0, 256), (0, 256, 256), (0, 512, 512), (1, 0, 512), (1, 512, 512))
+LAST_CHUNK = 256
+
+
+def tile_list_byte_patch_slots_kernel(
+    tc, tab_words, tab_scales, offs, w1_words, w1_scales, w2, w3_words, w3_scales, wgs, offs2, offs3, ctx, w4, out
+):
+    nc = tc.nc
+    with ExitStack() as stack:
+        keep = stack.enter_context(tc.tile_pool(name="keep", bufs=1))
+        ring = stack.enter_context(tc.tile_pool(name="ring", bufs=2))
+        psum = stack.enter_context(tc.psum_pool(name="psum", bufs=2))
+
+        list1 = keep.tile([P, S // 16], U16, name="list1")
+        list2 = keep.tile([P, S // 16], U16, name="list2")
+        list3 = keep.tile([P, PM // 16], U16, name="list3")
+        tab_w = ring.tile([P, T], I32, name="tab_w", tag="table_then_ctx", bufs=1)
+        tab_s = keep.tile([P, T], U8, name="tab_s", align_bytes=64)
+        v_w = keep.tile([P, S], U32, name="v_w", align_bytes=64)
+        v_s = keep.tile([P, S], U8, name="v_s", align_bytes=64)
+        w1_w = keep.tile([P, 2 * H], U8, name="w1_w", align_bytes=64)
+        w1_s = keep.tile([P, H], U8, name="w1_s", align_bytes=64)
+        w3_raw_w = ring.tile([P, H], I32, name="w3_raw_w", tag="raw", bufs=1)
+        w3_raw_s = keep.tile([P, H], U8, name="w3_raw_s", align_bytes=64)
+        w3_w = keep.tile([P, H], I32, name="w3_w", align_bytes=64)
+        w3_s = keep.tile([P, H], U8, name="w3_s", align_bytes=64)
+        w2_w = [keep.tile([P, BANK], U32, name=f"w2_w{a}", align_bytes=64) for a in range(2)]
+        w2_s = [keep.tile([P, BANK], U8, name=f"w2_s{a}", align_bytes=64) for a in range(2)]
+        w4_w = [keep.tile([P, N], U32, name=f"w4_w{a}", align_bytes=64) for a in range(2)]
+        w4_s = [keep.tile([P, N], U8, name=f"w4_s{a}", align_bytes=64) for a in range(2)]
+        z_w = [keep.tile([P, PM], U32, name=f"z_w{a}", align_bytes=64) for a in range(2)]
+        z_s = [keep.tile([P, PM], U8, name=f"z_s{a}", align_bytes=64) for a in range(2)]
+        slot_w = [keep.tile([P, PACK, BANK], F32, name="slot_w0")]
+        pages = [keep.tile([P, T2], F32, name=f"page{t}") for t in range(PACK)]
+        ident = keep.tile([P, P], F32, name="ident")
+
+        def load_scales(queue, plane, rows):
+            for q in range(4):
+                queue.dma_start(out=plane[32 * q : 32 * q + 4, :].bitcast(I32), in_=rows[0, 4 * q : 4 * q + 4, :].bitcast(I32))
+
+        def load_slot_weights(j0, width):
+            rows = wgs.rearrange("(m t) j -> m t j", t=PACK)
+            half, c0 = divmod(j0, BANK)
+            for q in range(4):
+                nc.sync.dma_start(out=slot_w[half][32 * q : 32 * q + 32, :, c0 : c0 + width], in_=rows[:, :, j0 : j0 + width])
+
+        def load_weight(rows, tag="raw"):
+            raw = ring.tile([P, PACK, BANK], F32, name="raw", tag=tag, bufs=1)
+            nc.sync.dma_start(out=raw[:], in_=rows.rearrange("(p t) c -> p t c", t=PACK))
+            return raw
+
+        def load_ctx(a):
+            own = ring.tile([P, PACK, PM], F32, name="own", tag="table_then_ctx", bufs=1)
+            nc.sync.dma_start(out=own[:], in_=ctx[BANK * a : BANK * (a + 1), :].rearrange("(p t) m -> p t m", t=PACK))
+            return own
+
+        def interleave(copy, planes, width, pieces=1):
+            woven = ring.tile([P, width, PACK], BF16, name="woven", align_bytes=64)
+            step = width // pieces
+            for c0 in range(0, width, step):
+                copy(
+                    out=woven[:, c0 : c0 + step, :].rearrange("p (c i) t -> p c t i", i=4),
+                    in_=planes[:, :, c0 : c0 + step].rearrange("p t (c i) -> p c t i", i=4),
+                )
+            return woven
+
+        def quantize(woven, words, scales):
+            nc.vector.quantize_mx(out=words.bitcast(FP8X4), scales=scales, in_=woven[:].rearrange("p c t -> p (c t)"))
+
+        def gather_table(j0, width):
+            picks = list1[:, j0 // 16 : (j0 + width) // 16]
+            nc.vector.tensor_copy(out=v_w[:, j0 : j0 + width], in_=tab_w[:].bitcast(U32).indirect(picks))
+            nc.vector.tensor_copy(out=v_s[:, j0 : j0 + width], in_=tab_s[:].indirect(picks))
+
+        def reorder_w3(a):
+            cols = slice(BANK * a, BANK * (a + 1))
+            nc.vector.tensor_copy(
+                out=w3_w[:, cols].rearrange("p (t b i) -> p b t i", t=PACK, i=4),
+                in_=w3_raw_w[:, cols].rearrange("p (b i t) -> p b t i", t=PACK, i=4),
+            )
+            nc.vector.tensor_copy(
+                out=w3_s[:, cols].rearrange("p (t b i) -> p b t i", t=PACK, i=16),
+                in_=w3_raw_s[:, cols].rearrange("p (b i t) -> p b t i", t=PACK, i=16),
+            )
+
+        relu_t, second_t = {}, {}
+
+        def token_major(e):
+            a, jt = divmod(e, S // P)
+            tokens = slice(P * jt, P * (jt + 1))
+            bank1 = psum.tile([P, BANK], F32, name="bank1", tag="first")
+            nc.tensor.matmul_mx(
+                out=bank1[:],
+                lhsT=v_w[:, tokens].bitcast(FP8X4),
+                lhsT_scale=v_s[:, tokens],
+                rhs=w1_w[:, 2 * BANK * a : 2 * BANK * (a + 1)].bitcast(FP4X4),
+                rhs_scale=w1_s[:, BANK * a : BANK * (a + 1)],
+                start=True,
+                stop=True,
+            )
+            bank2 = psum.tile([P, BANK], F32, name="bank2", tag="second")
+            nc.tensor.matmul_mx(
+                out=bank2[:],
+                lhsT=v_w[:, tokens].bitcast(FP8X4),
+                lhsT_scale=v_s[:, tokens],
+                rhs=w2_w[a][:].bitcast(FP8X4),
+                rhs_scale=w2_s[a][:],
+                start=True,
+                stop=True,
+            )
+            d = ring.tile([P, PACK, P], F32, name="d", bufs=8)
+            nc.scalar.activation(out=d[:], in_=bank1[:].rearrange("j (m t) -> j t m", t=PACK), func=ACT.Relu)
+            s2 = ring.tile([P, PACK, P], F32, name="s2", bufs=8)
+            nc.scalar.copy(out=s2[:], in_=bank2[:].rearrange("j (m t) -> j t m", t=PACK))
+            relu_t[e], second_t[e] = d, s2
+
+        units = [(a, j0, width, t) for a, j0, width in GROUPS for t in range(PACK)]
+        states = {}
+
+        def make_state(u):
+            a, j0, width, t = units[u]
+            q = psum.tile([P, BANK], F32, name="q", tag="sum")
+            for i in range(width // P):
+                e = a * (S // P) + j0 // P + i
+                cols = slice(P * i, P * (i + 1))
+                nc.tensor.matmul(q[:, cols], lhsT=relu_t[e][:, t, :], rhs=ident[:], is_transpose=True, start=True, stop=False)
+                nc.tensor.matmul(q[:, cols], lhsT=second_t[e][:, t, :], rhs=ident[:], is_transpose=True, start=False, stop=True)
+            third = psum.tile([P, BANK], F32, name="third", tag="third")
+            rows = slice(BANK * a + P * t, BANK * a + P * (t + 1))
+            nc.tensor.matmul_mx(
+                out=third[:, :width],
+                lhsT=w3_w[:, rows].bitcast(FP8X4),
+                lhsT_scale=w3_s[:, rows],
+                rhs=v_w[:, j0 : j0 + width].bitcast(FP8X4),
+                rhs_scale=v_s[:, j0 : j0 + width],
+                start=True,
+                stop=True,
+            )
+            gate = ring.tile([P, BANK], F32, name="gate")
+            nc.scalar.activation(out=gate[:, :width], in_=q[:, :width], func=ACT.Silu)
+            h = ring.tile([P, BANK], F32, name="h", bufs=3)
+            nc.vector.tensor_tensor(out=h[:, :width], in0=third[:, :width], in1=gate[:, :width], op=ALU.mult)
+            states[u] = h
+
+        def put_state(u):
+            a, j0, width, t = units[u]
+            size = ring.tile([P, BANK], F32, name="size", bufs=3)
+            nc.scalar.activation(out=size[:, :width], in_=states[u][:, :width], func=ACT.Abs)
+            nc.vector.tensor_tensor(
+                out=pages[t][:].indirect(list2[:, j0 // 16 : (j0 + width) // 16]),
+                in0=size[:, :width],
+                in1=slot_w[j0 // BANK][:, t, j0 % BANK : j0 % BANK + width],
+                op=ALU.mult,
+            )
+
+        def fetch(own, m0, width):
+            z = ring.tile([P, PACK, width], F32, name="z")
+            for t in range(PACK):
+                nc.vector.tensor_tensor(
+                    out=z[:, t, :],
+                    in0=pages[t][:].indirect(list3[:, m0 // 16 : (m0 + width) // 16]),
+                    in1=own[:, t, m0 : m0 + width],
+                    op=ALU.add,
+                )
+            return z
+
+        def last_pass(acc, a, nt, m0, width):
+            nc.tensor.matmul_mx(
+                out=acc,
+                lhsT=w4_w[a][:, P * nt : P * (nt + 1)].bitcast(FP8X4),
+                lhsT_scale=w4_s[a][:, P * nt : P * (nt + 1)],
+                rhs=z_w[a][:, m0 : m0 + width].bitcast(FP8X4),
+                rhs_scale=z_s[a][:, m0 : m0 + width],
+                start=(a == 0),
+                stop=(a == 1),
+            )
+
+        out_rows = out.rearrange("(nt p) m -> p nt m", p=P)
+
+        for plane in (tab_s, w1_s, w3_raw_s):
+            nc.gpsimd.memset(plane[:].bitcast(I32), 0)
+        make_identity(nc, ident[:])
+        load_scales(nc.gpsimd, w1_s, w1_scales)
+        load_scales(nc.gpsimd, w3_raw_s, w3_scales)
+        nc.sync.dma_start(list1[:], offs)
+        raw = load_weight(w2[:, 0:BANK], "w2_then_slots")
+        nc.sync.dma_start(out=tab_w[:], in_=tab_words[0].rearrange("p c i -> p (c i)").bitcast(I32))
+        load_scales(nc.sync, tab_s, tab_scales)
+        nc.sync.dma_start(out=w1_w[:].bitcast(I32), in_=w1_words[0].bitcast(I32))
+        nc.sync.dma_start(out=w3_raw_w[:], in_=w3_words[0].rearrange("p c i -> p (c i)").bitcast(I32))
+        nc.sync.dma_start(list2[:], offs2)
+        load_slot_weights(0, 256)
+        load_slot_weights(256, 256)
+        nc.sync.dma_start(list3[:], offs3)
+
+        quantize(interleave(nc.vector.tensor_copy, raw, BANK), w2_w[0][:], w2_s[0][:])
+        gather_table(0, 256)
+        for t in range(PACK):
+            nc.vector.memset(pages[t][:].bitcast(I32), 0)
+        token_major(0)
+        token_major(1)
+        gather_table(256, 256)
+        reorder_w3(0)
+        slot_w.append(ring.tile([P, PACK, BANK], F32, name="slot_w1", tag="w2_then_slots", bufs=1))
+        load_slot_weights(BANK, BANK)
+        make_state(0)
+        gather_table(512, 512)
+        reorder_w3(1)
+        raw = load_weight(w2[:, BANK : 2 * BANK])
+        own = load_ctx(0)
+
+        picked = []
+        woven_z = []
+        for u in range(len(units)):
+            if u + 1 < len(units):
+                make_state(u + 1)
+            put_state(u)
+            if u < 6:
+                token_major(u + 2)
+            elif u == 6:
+                quantize(interleave(nc.scalar.copy, raw, BANK, 2), w2_w[1][:], w2_s[1][:])
+                raw = load_weight(w4[0:BANK, :])
+            elif u < 15:
+                token_major(u + 1)
+            if u == 11:
+                picked = [fetch(own, m0, BANK) for m0 in (0, BANK)]
+                own = load_ctx(1)
+                quantize(interleave(nc.scalar.copy, raw, BANK, 2), w4_w[0][:], w4_s[0][:])
+                raw = load_weight(w4[BANK : 2 * BANK, :])
+            if u in (12, 14):
+                woven_z.append(interleave(nc.scalar.copy, picked[(u - 12) // 2], BANK, 2))
+            if u in (13, 15):
+                half = slice(BANK * ((u - 13) // 2), BANK * ((u - 13) // 2 + 1))
+                quantize(woven_z[(u - 13) // 2], z_w[0][:, half], z_s[0][:, half])
+            if u == 16:
+                quantize(interleave(nc.scalar.copy, raw, BANK, 2), w4_w[1][:], w4_s[1][:])
+
+        width = LAST_CHUNK
+        starts = list(range(0, PM, width))
+        open_acc = [psum.tile([P, BANK], F32, name=f"open{nt}", tag=("sum", "third")[nt % 2]) for nt in range(4)]
+        for nt in range(4):
+            last_pass(open_acc[nt][:, :width], 0, nt, starts[-1], width)
+
+        def finish(m0, z):
+            cols = slice(m0, m0 + width)
+            quantize(interleave(nc.scalar.copy, z, width), z_w[1][:, cols], z_s[1][:, cols])
+            result = ring.tile([P, 4, width], F32, name="result", bufs=3)
+            for pair in range(2):
+                acc = psum.tile([P, 2, width], F32, name="acc", tag=("first", "second")[pair])
+                for i in range(2):
+                    for a in range(2):
+                        last_pass(acc[:, i, :], a, 2 * pair + i, m0, width)
+                nc.scalar.copy(out=result[:, 2 * pair : 2 * pair + 2, :], in_=acc[:])
+            nc.sync.dma_start(out=out_rows[:, :, cols], in_=result[:])
+
+        z = fetch(own, starts[0], width)
+        for m0 in starts[:-1]:
+            z_next = fetch(own, m0 + width, width)
+            finish(m0, z)
+            z = z_next
+        cols = slice(starts[-1], PM)
+        quantize(interleave(nc.vector.tensor_copy, z, width), z_w[1][:, cols], z_s[1][:, cols])
+        for nt in range(4):
+            last_pass(open_acc[nt][:, :width], 1, nt, starts[-1], width)
+        for pair, copy in enumerate((nc.scalar.copy, nc.vector.tensor_copy)):
+            result = ring.tile([P, 2, width], F32, name="tail", bufs=2)
+            for i in range(2):
+                copy(out=result[:, i, :], in_=open_acc[2 * pair + i][:, :width])
+            nc.sync.dma_start(out=out_rows[:, 2 * pair : 2 * pair + 2, cols], in_=result[:])

@@ -31,6 +31,7 @@ def tile_list_byte_patch_slots_kernel(
     with ExitStack() as stack:
         keep = stack.enter_context(tc.tile_pool(name="keep", bufs=1))
         ring = stack.enter_context(tc.tile_pool(name="ring", bufs=2))
+        shared = stack.enter_context(tc.tile_pool(name="shared", bufs=1))
         psum = stack.enter_context(tc.psum_pool(name="psum", bufs=2))
 
         list1 = keep.tile([P, S // 16], U16, name="list1")
@@ -38,8 +39,23 @@ def tile_list_byte_patch_slots_kernel(
         list3 = keep.tile([P, PM // 16], U16, name="list3")
         tab_w = ring.tile([P, T], I32, name="tab_w", tag="table_then_ctx", bufs=1)
         tab_s = keep.tile([P, T], U8, name="tab_s", align_bytes=64)
-        v_w = keep.tile([P, S], U32, name="v_w", align_bytes=64)
-        v_s = keep.tile([P, S], U8, name="v_s", align_bytes=64)
+        first_woven = shared.tile([P, BANK, PACK], BF16, name="first_woven", align_bytes=64, offset=0)
+        v_w = {
+            0: keep.tile([P, 256], U32, name="v_w0", align_bytes=64),
+            256: shared.tile([P, 256], U32, name="v_w1", align_bytes=64, offset=0),
+            512: shared.tile([P, 512], U32, name="v_w2", align_bytes=64, offset=1024),
+        }
+        v_s = {
+            0: keep.tile([P, 256], U8, name="v_s0", align_bytes=64),
+            256: shared.tile([P, 256], U8, name="v_s1", align_bytes=64, offset=3072),
+            512: shared.tile([P, 512], U8, name="v_s2", align_bytes=64, offset=3328),
+        }
+
+        def picked_columns(j0, width):
+            start = max(s for s in v_w if s <= j0)
+            cols = slice(j0 - start, j0 - start + width)
+            return v_w[start][:, cols].bitcast(FP8X4), v_s[start][:, cols]
+
         w1_w = keep.tile([P, 2 * H], U8, name="w1_w", align_bytes=64)
         w1_s = keep.tile([P, H], U8, name="w1_s", align_bytes=64)
         w3_raw_w = ring.tile([P, H], I32, name="w3_raw_w", tag="raw", bufs=1)
@@ -76,8 +92,9 @@ def tile_list_byte_patch_slots_kernel(
             nc.sync.dma_start(out=own[:], in_=ctx[BANK * a : BANK * (a + 1), :].rearrange("(p t) m -> p t m", t=PACK))
             return own
 
-        def interleave(copy, planes, width, pieces=1):
-            woven = ring.tile([P, width, PACK], BF16, name="woven", align_bytes=64)
+        def interleave(copy, planes, width, pieces=1, woven=None):
+            if woven is None:
+                woven = ring.tile([P, width, PACK], BF16, name="woven", bufs=3, align_bytes=64)
             step = width // pieces
             for c0 in range(0, width, step):
                 copy(
@@ -91,8 +108,8 @@ def tile_list_byte_patch_slots_kernel(
 
         def gather_table(j0, width):
             picks = list1[:, j0 // 16 : (j0 + width) // 16]
-            nc.vector.tensor_copy(out=v_w[:, j0 : j0 + width], in_=tab_w[:].bitcast(U32).indirect(picks))
-            nc.vector.tensor_copy(out=v_s[:, j0 : j0 + width], in_=tab_s[:].indirect(picks))
+            nc.vector.tensor_copy(out=v_w[j0][:], in_=tab_w[:].bitcast(U32).indirect(picks))
+            nc.vector.tensor_copy(out=v_s[j0][:], in_=tab_s[:].indirect(picks))
 
         def reorder_w3(a):
             cols = slice(BANK * a, BANK * (a + 1))
@@ -109,12 +126,12 @@ def tile_list_byte_patch_slots_kernel(
 
         def token_major(e):
             a, jt = divmod(e, S // P)
-            tokens = slice(P * jt, P * (jt + 1))
+            words, scales = picked_columns(P * jt, P)
             bank1 = psum.tile([P, BANK], F32, name="bank1", tag="first")
             nc.tensor.matmul_mx(
                 out=bank1[:],
-                lhsT=v_w[:, tokens].bitcast(FP8X4),
-                lhsT_scale=v_s[:, tokens],
+                lhsT=words,
+                lhsT_scale=scales,
                 rhs=w1_w[:, 2 * BANK * a : 2 * BANK * (a + 1)].bitcast(FP4X4),
                 rhs_scale=w1_s[:, BANK * a : BANK * (a + 1)],
                 start=True,
@@ -123,8 +140,8 @@ def tile_list_byte_patch_slots_kernel(
             bank2 = psum.tile([P, BANK], F32, name="bank2", tag="second")
             nc.tensor.matmul_mx(
                 out=bank2[:],
-                lhsT=v_w[:, tokens].bitcast(FP8X4),
-                lhsT_scale=v_s[:, tokens],
+                lhsT=words,
+                lhsT_scale=scales,
                 rhs=w2_w[a][:].bitcast(FP8X4),
                 rhs_scale=w2_s[a][:],
                 start=True,
@@ -149,34 +166,42 @@ def tile_list_byte_patch_slots_kernel(
                 nc.tensor.matmul(q[:, cols], lhsT=second_t[e][:, t, :], rhs=ident[:], is_transpose=True, start=False, stop=True)
             third = psum.tile([P, BANK], F32, name="third", tag="third")
             rows = slice(BANK * a + P * t, BANK * a + P * (t + 1))
-            nc.tensor.matmul_mx(
-                out=third[:, :width],
-                lhsT=w3_w[:, rows].bitcast(FP8X4),
-                lhsT_scale=w3_s[:, rows],
-                rhs=v_w[:, j0 : j0 + width].bitcast(FP8X4),
-                rhs_scale=v_s[:, j0 : j0 + width],
-                start=True,
-                stop=True,
-            )
+            step = 256 if j0 < BANK else width
+            for c0 in range(0, width, step):
+                words, scales = picked_columns(j0 + c0, step)
+                nc.tensor.matmul_mx(
+                    out=third[:, c0 : c0 + step],
+                    lhsT=w3_w[:, rows].bitcast(FP8X4),
+                    lhsT_scale=w3_s[:, rows],
+                    rhs=words,
+                    rhs_scale=scales,
+                    start=True,
+                    stop=True,
+                )
             gate = ring.tile([P, BANK], F32, name="gate")
             nc.scalar.activation(out=gate[:, :width], in_=q[:, :width], func=ACT.Silu)
+            gate_size = ring.tile([P, BANK], F32, name="gate_size")
+            nc.scalar.activation(out=gate_size[:, :width], in_=gate[:, :width], func=ACT.Abs)
+            third_size = ring.tile([P, BANK], F32, name="third_size")
+            nc.scalar.activation(out=third_size[:, :width], in_=third[:, :width], func=ACT.Abs)
+            engine = nc.gpsimd
+            weighted = ring.tile([P, BANK], F32, name="weighted")
+            engine.tensor_tensor(
+                out=weighted[:, :width],
+                in0=gate_size[:, :width],
+                in1=slot_w[j0 // BANK][:, t, j0 % BANK : j0 % BANK + width],
+                op=ALU.mult,
+            )
             h = ring.tile([P, BANK], F32, name="h", bufs=3)
-            nc.vector.tensor_tensor(out=h[:, :width], in0=third[:, :width], in1=gate[:, :width], op=ALU.mult)
+            engine.tensor_tensor(out=h[:, :width], in0=weighted[:, :width], in1=third_size[:, :width], op=ALU.mult)
             states[u] = h
 
         def put_state(u):
             a, j0, width, t = units[u]
-            size = ring.tile([P, BANK], F32, name="size", bufs=3)
-            nc.scalar.activation(out=size[:, :width], in_=states[u][:, :width], func=ACT.Abs)
-            nc.vector.tensor_tensor(
-                out=pages[t][:].indirect(list2[:, j0 // 16 : (j0 + width) // 16]),
-                in0=size[:, :width],
-                in1=slot_w[j0 // BANK][:, t, j0 % BANK : j0 % BANK + width],
-                op=ALU.mult,
-            )
+            nc.vector.tensor_copy(out=pages[t][:].indirect(list2[:, j0 // 16 : (j0 + width) // 16]), in_=states[u][:, :width])
 
         def fetch(own, m0, width):
-            z = ring.tile([P, PACK, width], F32, name="z")
+            z = ring.tile([P, PACK, width], F32, name=f"z{width}", bufs=2)
             for t in range(PACK):
                 nc.vector.tensor_tensor(
                     out=z[:, t, :],
@@ -199,25 +224,29 @@ def tile_list_byte_patch_slots_kernel(
 
         out_rows = out.rearrange("(nt p) m -> p nt m", p=P)
 
-        for plane in (tab_s, w1_s, w3_raw_s):
+        for plane in (tab_s, w3_raw_s):
             nc.gpsimd.memset(plane[:].bitcast(I32), 0)
         make_identity(nc, ident[:])
-        load_scales(nc.gpsimd, w1_s, w1_scales)
-        load_scales(nc.gpsimd, w3_raw_s, w3_scales)
-        nc.sync.dma_start(list1[:], offs)
-        raw = load_weight(w2[:, 0:BANK], "w2_then_slots")
-        nc.sync.dma_start(out=tab_w[:], in_=tab_words[0].rearrange("p c i -> p (c i)").bitcast(I32))
-        load_scales(nc.sync, tab_s, tab_scales)
+        nc.gpsimd.memset(pages[PACK - 1][:].bitcast(I32), 0)
+        for tile, names in ((list1, offs), (list2, offs2), (list3, offs3)):
+            nc.sync.dma_start(tile[:], names)
+        table = tab_words[0].rearrange("p c i -> p (c i)").bitcast(I32)
+        for c0 in range(0, T, BANK):
+            nc.sync.dma_start(out=tab_w[:, c0 : c0 + BANK], in_=table[:, c0 : c0 + BANK])
         nc.sync.dma_start(out=w1_w[:].bitcast(I32), in_=w1_words[0].bitcast(I32))
+        load_scales(nc.sync, tab_s, tab_scales)
+        raw = load_weight(w2[:, 0:BANK], "w2_then_slots")
+        load_scales(nc.sync, w1_s, w1_scales)
         nc.sync.dma_start(out=w3_raw_w[:], in_=w3_words[0].rearrange("p c i -> p (c i)").bitcast(I32))
-        nc.sync.dma_start(list2[:], offs2)
+        load_scales(nc.sync, w3_raw_s, w3_scales)
         load_slot_weights(0, 256)
         load_slot_weights(256, 256)
-        nc.sync.dma_start(list3[:], offs3)
 
-        quantize(interleave(nc.vector.tensor_copy, raw, BANK), w2_w[0][:], w2_s[0][:])
+        warm = keep.tile([P, 1], F32, name="warm")
+        nc.scalar.activation(out=warm[:], in_=ident[:, 0:1], func=ACT.Silu)
         gather_table(0, 256)
-        for t in range(PACK):
+        quantize(interleave(nc.vector.tensor_copy, raw, BANK, woven=first_woven), w2_w[0][:], w2_s[0][:])
+        for t in range(PACK - 1):
             nc.vector.memset(pages[t][:].bitcast(I32), 0)
         token_major(0)
         token_major(1)
@@ -263,9 +292,11 @@ def tile_list_byte_patch_slots_kernel(
         for nt in range(4):
             last_pass(open_acc[nt][:, :width], 0, nt, starts[-1], width)
 
-        def finish(m0, z):
+        def weave(m0, z):
             cols = slice(m0, m0 + width)
             quantize(interleave(nc.scalar.copy, z, width), z_w[1][:, cols], z_s[1][:, cols])
+
+        def finish(m0):
             result = ring.tile([P, 4, width], F32, name="result", bufs=3)
             for pair in range(2):
                 acc = psum.tile([P, 2, width], F32, name="acc", tag=("first", "second")[pair])
@@ -273,13 +304,15 @@ def tile_list_byte_patch_slots_kernel(
                     for a in range(2):
                         last_pass(acc[:, i, :], a, 2 * pair + i, m0, width)
                 nc.scalar.copy(out=result[:, 2 * pair : 2 * pair + 2, :], in_=acc[:])
-            nc.sync.dma_start(out=out_rows[:, :, cols], in_=result[:])
+            nc.sync.dma_start(out=out_rows[:, :, m0 : m0 + width], in_=result[:])
 
         z = fetch(own, starts[0], width)
-        for m0 in starts[:-1]:
-            z_next = fetch(own, m0 + width, width)
-            finish(m0, z)
-            z = z_next
+        for c, m0 in enumerate(starts[:-1]):
+            weave(m0, z)
+            z = fetch(own, m0 + width, width)
+            if c > 0:
+                finish(m0 - width)
+        finish(starts[-2])
         cols = slice(starts[-1], PM)
         quantize(interleave(nc.vector.tensor_copy, z, width), z_w[1][:, cols], z_s[1][:, cols])
         for nt in range(4):

@@ -20,7 +20,6 @@ ACT = mybir.ActivationFunctionType
 P = 128
 PACK = 4
 BANK = 512
-GROUPS = ((0, 0, 256), (0, 256, 256), (0, 512, 512), (1, 0, 512), (1, 512, 512))
 LAST_CHUNK = 256
 
 
@@ -39,16 +38,15 @@ def tile_list_byte_patch_slots_kernel(
         list3 = keep.tile([P, PM // 16], U16, name="list3")
         tab_w = ring.tile([P, T], I32, name="tab_w", tag="table_then_ctx", bufs=1)
         tab_s = keep.tile([P, T], U8, name="tab_s", align_bytes=64)
-        first_woven = shared.tile([P, BANK, PACK], BF16, name="first_woven", align_bytes=64, offset=0)
         v_w = {
             0: keep.tile([P, 256], U32, name="v_w0", align_bytes=64),
-            256: shared.tile([P, 256], U32, name="v_w1", align_bytes=64, offset=0),
-            512: shared.tile([P, 512], U32, name="v_w2", align_bytes=64, offset=1024),
+            256: keep.tile([P, 256], U32, name="v_w1", align_bytes=64),
+            512: shared.tile([P, 512], U32, name="v_w2", align_bytes=64, offset=0),
         }
         v_s = {
             0: keep.tile([P, 256], U8, name="v_s0", align_bytes=64),
-            256: shared.tile([P, 256], U8, name="v_s1", align_bytes=64, offset=3072),
-            512: shared.tile([P, 512], U8, name="v_s2", align_bytes=64, offset=3328),
+            256: keep.tile([P, 256], U8, name="v_s1", align_bytes=64),
+            512: shared.tile([P, 512], U8, name="v_s2", align_bytes=64, offset=4 * H),
         }
 
         def picked_columns(j0, width):
@@ -58,8 +56,8 @@ def tile_list_byte_patch_slots_kernel(
 
         w1_w = keep.tile([P, 2 * H], U8, name="w1_w", align_bytes=64)
         w1_s = keep.tile([P, H], U8, name="w1_s", align_bytes=64)
-        w3_raw_w = ring.tile([P, H], I32, name="w3_raw_w", tag="raw", bufs=1)
-        w3_raw_s = keep.tile([P, H], U8, name="w3_raw_s", align_bytes=64)
+        w3_raw_w = shared.tile([P, H], I32, name="w3_raw_w", align_bytes=64, offset=0)
+        w3_raw_s = shared.tile([P, H], U8, name="w3_raw_s", align_bytes=64, offset=4 * H)
         w3_w = keep.tile([P, H], I32, name="w3_w", align_bytes=64)
         w3_s = keep.tile([P, H], U8, name="w3_s", align_bytes=64)
         w2_w = [keep.tile([P, BANK], U32, name=f"w2_w{a}", align_bytes=64) for a in range(2)]
@@ -68,7 +66,7 @@ def tile_list_byte_patch_slots_kernel(
         w4_s = [keep.tile([P, N], U8, name=f"w4_s{a}", align_bytes=64) for a in range(2)]
         z_w = [keep.tile([P, PM], U32, name=f"z_w{a}", align_bytes=64) for a in range(2)]
         z_s = [keep.tile([P, PM], U8, name=f"z_s{a}", align_bytes=64) for a in range(2)]
-        slot_w = [keep.tile([P, PACK, BANK], F32, name="slot_w0")]
+        slot_w = {j0: keep.tile([P, PACK, 256], F32, name=f"slot_w{j0}") for j0 in (0, 256)}
         pages = [keep.tile([P, T2], F32, name=f"page{t}") for t in range(PACK)]
         ident = keep.tile([P, P], F32, name="ident")
 
@@ -78,13 +76,14 @@ def tile_list_byte_patch_slots_kernel(
 
         def load_slot_weights(j0, width):
             rows = wgs.rearrange("(m t) j -> m t j", t=PACK)
-            half, c0 = divmod(j0, BANK)
             for q in range(4):
-                nc.sync.dma_start(out=slot_w[half][32 * q : 32 * q + 32, :, c0 : c0 + width], in_=rows[:, :, j0 : j0 + width])
+                nc.sync.dma_start(out=slot_w[j0][32 * q : 32 * q + 32, :, :], in_=rows[:, :, j0 : j0 + width])
 
-        def load_weight(rows, tag="raw"):
+        def load_weight(rows, tag="raw", pieces=1):
             raw = ring.tile([P, PACK, BANK], F32, name="raw", tag=tag, bufs=1)
-            nc.sync.dma_start(out=raw[:], in_=rows.rearrange("(p t) c -> p t c", t=PACK))
+            step = BANK // pieces
+            for c0 in range(0, BANK, step):
+                nc.sync.dma_start(out=raw[:, :, c0 : c0 + step], in_=rows.rearrange("(p t) c -> p t c", t=PACK)[:, :, c0 : c0 + step])
             return raw
 
         def load_ctx(a):
@@ -92,19 +91,20 @@ def tile_list_byte_patch_slots_kernel(
             nc.sync.dma_start(out=own[:], in_=ctx[BANK * a : BANK * (a + 1), :].rearrange("(p t) m -> p t m", t=PACK))
             return own
 
-        def interleave(copy, planes, width, pieces=1, woven=None):
-            if woven is None:
-                woven = ring.tile([P, width, PACK], BF16, name="woven", bufs=3, align_bytes=64)
-            step = width // pieces
-            for c0 in range(0, width, step):
-                copy(
-                    out=woven[:, c0 : c0 + step, :].rearrange("p (c i) t -> p c t i", i=4),
-                    in_=planes[:, :, c0 : c0 + step].rearrange("p t (c i) -> p c t i", i=4),
-                )
-            return woven
+        def new_woven(width):
+            return ring.tile([P, width, PACK], BF16, name="woven", bufs=3, align_bytes=64)
+
+        def interleave(copy, woven, planes):
+            copy(out=woven.rearrange("p (c i) t -> p c t i", i=4), in_=planes.rearrange("p t (c i) -> p c t i", i=4))
 
         def quantize(woven, words, scales):
-            nc.vector.quantize_mx(out=words.bitcast(FP8X4), scales=scales, in_=woven[:].rearrange("p c t -> p (c t)"))
+            nc.vector.quantize_mx(out=words.bitcast(FP8X4), scales=scales, in_=woven.rearrange("p c t -> p (c t)"))
+
+        def prepare_weight(raw, words, scales):
+            woven = new_woven(BANK)
+            for c0 in (0, 256):
+                interleave(nc.scalar.copy, woven[:, c0 : c0 + 256, :], raw[:, :, c0 : c0 + 256])
+            quantize(woven[:], words[:], scales[:])
 
         def gather_table(j0, width):
             picks = list1[:, j0 // 16 : (j0 + width) // 16]
@@ -148,29 +148,38 @@ def tile_list_byte_patch_slots_kernel(
                 stop=True,
             )
             d = ring.tile([P, PACK, P], F32, name="d", bufs=8)
-            nc.scalar.activation(out=d[:], in_=bank1[:].rearrange("j (m t) -> j t m", t=PACK), func=ACT.Relu)
             s2 = ring.tile([P, PACK, P], F32, name="s2", bufs=8)
-            nc.scalar.copy(out=s2[:], in_=bank2[:].rearrange("j (m t) -> j t m", t=PACK))
+            by_slice1, by_slice2 = (bank[:].rearrange("j (m t) -> j t m", t=PACK) for bank in (bank1, bank2))
+            if e in (2, 3):
+                nc.vector.tensor_scalar_max(d[:], by_slice1, 0.0)
+                nc.vector.tensor_copy(out=s2[:], in_=by_slice2)
+            else:
+                nc.scalar.activation(out=d[:], in_=by_slice1, func=ACT.Relu)
+                nc.scalar.copy(out=s2[:], in_=by_slice2)
             relu_t[e], second_t[e] = d, s2
 
-        units = [(a, j0, width, t) for a, j0, width in GROUPS for t in range(PACK)]
+        units = [(0, j0, 256, t0) for j0 in range(0, S, 256) for t0 in (0, 2)]
+        units += [(1, j0, 256, t0) for j0 in (0, 256) for t0 in (0, 2)]
+        units += [(1, BANK, BANK, t0) for t0 in range(PACK)]
         states = {}
 
-        def make_state(u):
-            a, j0, width, t = units[u]
+        def make_state(u, weighted):
+            a, j0, width, t0 = units[u]
+            slices = range(t0, t0 + BANK // width)
+            start = min(j0, BANK)
             q = psum.tile([P, BANK], F32, name="q", tag="sum")
-            for i in range(width // P):
-                e = a * (S // P) + j0 // P + i
-                cols = slice(P * i, P * (i + 1))
-                nc.tensor.matmul(q[:, cols], lhsT=relu_t[e][:, t, :], rhs=ident[:], is_transpose=True, start=True, stop=False)
-                nc.tensor.matmul(q[:, cols], lhsT=second_t[e][:, t, :], rhs=ident[:], is_transpose=True, start=False, stop=True)
+            for t in slices:
+                for i in range(width // P):
+                    e = a * (S // P) + j0 // P + i
+                    c0 = (t - t0) * width + P * i
+                    nc.tensor.matmul(q[:, c0 : c0 + P], lhsT=relu_t[e][:, t, :], rhs=ident[:], is_transpose=True, start=True, stop=False)
+                    nc.tensor.matmul(q[:, c0 : c0 + P], lhsT=second_t[e][:, t, :], rhs=ident[:], is_transpose=True, start=False, stop=True)
             third = psum.tile([P, BANK], F32, name="third", tag="third")
-            rows = slice(BANK * a + P * t, BANK * a + P * (t + 1))
-            step = 256 if j0 < BANK else width
-            for c0 in range(0, width, step):
-                words, scales = picked_columns(j0 + c0, step)
+            words, scales = picked_columns(j0, width)
+            for t in slices:
+                rows = slice(BANK * a + P * t, BANK * a + P * (t + 1))
                 nc.tensor.matmul_mx(
-                    out=third[:, c0 : c0 + step],
+                    out=third[:, (t - t0) * width : (t - t0 + 1) * width],
                     lhsT=w3_w[:, rows].bitcast(FP8X4),
                     lhsT_scale=w3_s[:, rows],
                     rhs=words,
@@ -179,29 +188,33 @@ def tile_list_byte_patch_slots_kernel(
                     stop=True,
                 )
             gate = ring.tile([P, BANK], F32, name="gate")
-            nc.scalar.activation(out=gate[:, :width], in_=q[:, :width], func=ACT.Silu)
+            nc.scalar.activation(out=gate[:], in_=q[:], func=ACT.Silu)
             gate_size = ring.tile([P, BANK], F32, name="gate_size")
-            nc.scalar.activation(out=gate_size[:, :width], in_=gate[:, :width], func=ACT.Abs)
+            nc.scalar.activation(out=gate_size[:], in_=gate[:], func=ACT.Abs)
             third_size = ring.tile([P, BANK], F32, name="third_size")
-            nc.scalar.activation(out=third_size[:, :width], in_=third[:, :width], func=ACT.Abs)
-            engine = nc.gpsimd
-            weighted = ring.tile([P, BANK], F32, name="weighted")
-            engine.tensor_tensor(
-                out=weighted[:, :width],
-                in0=gate_size[:, :width],
-                in1=slot_w[j0 // BANK][:, t, j0 % BANK : j0 % BANK + width],
+            nc.scalar.activation(out=third_size[:], in_=third[:], func=ACT.Abs)
+            nc.gpsimd.tensor_tensor(
+                out=weighted[:].rearrange("p (t j) -> p t j", j=width),
+                in0=gate_size[:].rearrange("p (t j) -> p t j", j=width),
+                in1=slot_w[start][:, t0 : t0 + len(slices), j0 - start : j0 - start + width],
                 op=ALU.mult,
             )
-            h = ring.tile([P, BANK], F32, name="h", bufs=3)
-            engine.tensor_tensor(out=h[:, :width], in0=weighted[:, :width], in1=third_size[:, :width], op=ALU.mult)
+            h = ring.tile([P, BANK], F32, name="h")
+            nc.gpsimd.tensor_tensor(out=h[:], in0=weighted[:], in1=third_size[:], op=ALU.mult)
             states[u] = h
 
-        def put_state(u):
-            a, j0, width, t = units[u]
-            nc.vector.tensor_copy(out=pages[t][:].indirect(list2[:, j0 // 16 : (j0 + width) // 16]), in_=states[u][:, :width])
+        def new_weighted():
+            return ring.tile([P, BANK], F32, name="weighted", bufs=1)
 
-        def fetch(own, m0, width):
-            z = ring.tile([P, PACK, width], F32, name=f"z{width}", bufs=2)
+        def put_state(u):
+            a, j0, width, t0 = units[u]
+            for i in range(BANK // width):
+                nc.vector.tensor_copy(
+                    out=pages[t0 + i][:].indirect(list2[:, j0 // 16 : (j0 + width) // 16]),
+                    in_=states[u][:, i * width : (i + 1) * width],
+                )
+
+        def fetch(z, own, m0, width):
             for t in range(PACK):
                 nc.vector.tensor_tensor(
                     out=z[:, t, :],
@@ -209,7 +222,6 @@ def tile_list_byte_patch_slots_kernel(
                     in1=own[:, t, m0 : m0 + width],
                     op=ALU.add,
                 )
-            return z
 
         def last_pass(acc, a, nt, m0, width):
             nc.tensor.matmul_mx(
@@ -227,16 +239,16 @@ def tile_list_byte_patch_slots_kernel(
         for plane in (tab_s, w3_raw_s):
             nc.gpsimd.memset(plane[:].bitcast(I32), 0)
         make_identity(nc, ident[:])
-        nc.gpsimd.memset(pages[PACK - 1][:].bitcast(I32), 0)
-        for tile, names in ((list1, offs), (list2, offs2), (list3, offs3)):
-            nc.sync.dma_start(tile[:], names)
-        table = tab_words[0].rearrange("p c i -> p (c i)").bitcast(I32)
-        for c0 in range(0, T, BANK):
-            nc.sync.dma_start(out=tab_w[:, c0 : c0 + BANK], in_=table[:, c0 : c0 + BANK])
-        nc.sync.dma_start(out=w1_w[:].bitcast(I32), in_=w1_words[0].bitcast(I32))
-        load_scales(nc.sync, tab_s, tab_scales)
-        raw = load_weight(w2[:, 0:BANK], "w2_then_slots")
+        for t in (2, 3):
+            nc.gpsimd.memset(pages[t][:].bitcast(I32), 0)
+        nc.sync.dma_start(list1[:], offs)
         load_scales(nc.sync, w1_s, w1_scales)
+        nc.sync.dma_start(list2[:], offs2)
+        nc.sync.dma_start(list3[:], offs3)
+        nc.sync.dma_start(out=tab_w[:], in_=tab_words[0].rearrange("p c i -> p (c i)").bitcast(I32))
+        load_scales(nc.sync, tab_s, tab_scales)
+        nc.sync.dma_start(out=w1_w[:].bitcast(I32), in_=w1_words[0].bitcast(I32))
+        raw = load_weight(w2[:, 0:BANK], "w2_then_slots", 2)
         nc.sync.dma_start(out=w3_raw_w[:], in_=w3_words[0].rearrange("p c i -> p (c i)").bitcast(I32))
         load_scales(nc.sync, w3_raw_s, w3_scales)
         load_slot_weights(0, 256)
@@ -245,46 +257,68 @@ def tile_list_byte_patch_slots_kernel(
         warm = keep.tile([P, 1], F32, name="warm")
         nc.scalar.activation(out=warm[:], in_=ident[:, 0:1], func=ACT.Silu)
         gather_table(0, 256)
-        quantize(interleave(nc.vector.tensor_copy, raw, BANK, woven=first_woven), w2_w[0][:], w2_s[0][:])
-        for t in range(PACK - 1):
+        first_woven = new_woven(BANK)
+        for c0 in (0, 256):
+            cols = slice(c0, c0 + 256)
+            interleave(nc.vector.tensor_copy, first_woven[:, cols, :], raw[:, :, cols])
+        for c0 in (0, 256):
+            cols = slice(c0, c0 + 256)
+            quantize(first_woven[:, cols, :], w2_w[0][:, cols], w2_s[0][:, cols])
+        for t in (0, 1):
             nc.vector.memset(pages[t][:].bitcast(I32), 0)
         token_major(0)
         token_major(1)
         gather_table(256, 256)
         reorder_w3(0)
-        slot_w.append(ring.tile([P, PACK, BANK], F32, name="slot_w1", tag="w2_then_slots", bufs=1))
-        load_slot_weights(BANK, BANK)
-        make_state(0)
-        gather_table(512, 512)
         reorder_w3(1)
+        slot_w[BANK] = ring.tile([P, PACK, BANK], F32, name="slot_w_late", tag="w2_then_slots", bufs=1)
+        load_slot_weights(BANK, BANK)
+        make_state(0, new_weighted())
+        token_major(2)
+        token_major(3)
+        gather_table(512, 512)
         raw = load_weight(w2[:, BANK : 2 * BANK])
         own = load_ctx(0)
 
-        picked = []
-        woven_z = []
-        for u in range(len(units)):
-            if u + 1 < len(units):
-                make_state(u + 1)
+        for u in range(7):
+            make_state(u + 1, new_weighted())
             put_state(u)
-            if u < 6:
-                token_major(u + 2)
-            elif u == 6:
-                quantize(interleave(nc.scalar.copy, raw, BANK, 2), w2_w[1][:], w2_s[1][:])
+            if u < 4:
+                token_major(u + 4)
+            elif u == 4:
+                prepare_weight(raw, w2_w[1], w2_s[1])
                 raw = load_weight(w4[0:BANK, :])
-            elif u < 15:
-                token_major(u + 1)
-            if u == 11:
-                picked = [fetch(own, m0, BANK) for m0 in (0, BANK)]
-                own = load_ctx(1)
-                quantize(interleave(nc.scalar.copy, raw, BANK, 2), w4_w[0][:], w4_s[0][:])
-                raw = load_weight(w4[BANK : 2 * BANK, :])
-            if u in (12, 14):
-                woven_z.append(interleave(nc.scalar.copy, picked[(u - 12) // 2], BANK, 2))
-            if u in (13, 15):
-                half = slice(BANK * ((u - 13) // 2), BANK * ((u - 13) // 2 + 1))
-                quantize(woven_z[(u - 13) // 2], z_w[0][:, half], z_s[0][:, half])
-            if u == 16:
-                quantize(interleave(nc.scalar.copy, raw, BANK, 2), w4_w[1][:], w4_s[1][:])
+            else:
+                token_major(u + 3)
+        make_state(8, new_weighted())
+        put_state(7)
+        z0 = ring.tile([P, PACK, PM], F32, name="z0", bufs=1)
+        fetch(z0, own, 0, PM)
+        token_major(10)
+        token_major(11)
+        make_state(9, ring.tile([P, BANK], F32, name="weighted_after_fetch", tag="table_then_ctx", bufs=1))
+        own = load_ctx(1)
+        put_state(8)
+        token_major(12)
+        token_major(13)
+        prepare_weight(raw, w4_w[0], w4_s[0])
+        raw = load_weight(w4[BANK : 2 * BANK, :])
+        woven_z = []
+        for u in range(9, 15):
+            make_state(u + 1, new_weighted())
+            put_state(u)
+            if u < 11:
+                token_major(u + 5)
+            else:
+                c0 = 256 * (u - 11)
+                if c0 % BANK == 0:
+                    woven_z.append(new_woven(BANK))
+                interleave(nc.scalar.copy, woven_z[-1][:, c0 % BANK : c0 % BANK + 256, :], z0[:, :, c0 : c0 + 256])
+            if u == 13:
+                quantize(woven_z[0][:], z_w[0][:, 0:BANK], z_s[0][:, 0:BANK])
+        put_state(15)
+        quantize(woven_z[1][:], z_w[0][:, BANK:PM], z_s[0][:, BANK:PM])
+        prepare_weight(raw, w4_w[1], w4_s[1])
 
         width = LAST_CHUNK
         starts = list(range(0, PM, width))
@@ -294,7 +328,9 @@ def tile_list_byte_patch_slots_kernel(
 
         def weave(m0, z):
             cols = slice(m0, m0 + width)
-            quantize(interleave(nc.scalar.copy, z, width), z_w[1][:, cols], z_s[1][:, cols])
+            woven = new_woven(width)
+            interleave(nc.scalar.copy, woven[:], z[:])
+            quantize(woven[:], z_w[1][:, cols], z_s[1][:, cols])
 
         def finish(m0):
             result = ring.tile([P, 4, width], F32, name="result", bufs=3)
@@ -306,15 +342,22 @@ def tile_list_byte_patch_slots_kernel(
                 nc.scalar.copy(out=result[:, 2 * pair : 2 * pair + 2, :], in_=acc[:])
             nc.sync.dma_start(out=out_rows[:, :, m0 : m0 + width], in_=result[:])
 
-        z = fetch(own, starts[0], width)
+        def fetch_chunk(m0):
+            z = ring.tile([P, PACK, width], F32, name="z")
+            fetch(z, own, m0, width)
+            return z
+
+        z = fetch_chunk(starts[0])
         for c, m0 in enumerate(starts[:-1]):
             weave(m0, z)
-            z = fetch(own, m0 + width, width)
+            z = fetch_chunk(m0 + width)
             if c > 0:
                 finish(m0 - width)
         finish(starts[-2])
         cols = slice(starts[-1], PM)
-        quantize(interleave(nc.vector.tensor_copy, z, width), z_w[1][:, cols], z_s[1][:, cols])
+        woven = new_woven(width)
+        interleave(nc.vector.tensor_copy, woven[:], z[:])
+        quantize(woven[:], z_w[1][:, cols], z_s[1][:, cols])
         for nt in range(4):
             last_pass(open_acc[nt][:, :width], 1, nt, starts[-1], width)
         for pair, copy in enumerate((nc.scalar.copy, nc.vector.tensor_copy)):

@@ -21,6 +21,9 @@ P = 128
 PACK = 4
 BANK = 512
 LAST_CHUNK = 256
+KIB = 1024
+AT_Z0 = 5 * KIB
+AT_LATE = 21 * KIB
 
 
 def tile_list_byte_patch_slots_kernel(
@@ -62,9 +65,12 @@ def tile_list_byte_patch_slots_kernel(
         w3_s = keep.tile([P, H], U8, name="w3_s", align_bytes=64)
         w2_w = [keep.tile([P, BANK], U32, name=f"w2_w{a}", align_bytes=64) for a in range(2)]
         w2_s = [keep.tile([P, BANK], U8, name=f"w2_s{a}", align_bytes=64) for a in range(2)]
-        w4_w = [keep.tile([P, N], U32, name=f"w4_w{a}", align_bytes=64) for a in range(2)]
+        w4_w = [shared.tile([P, N], U32, name=f"w4_w{a}", align_bytes=64, offset=AT_LATE + (16 + 2 * a) * KIB) for a in range(2)]
         w4_s = [keep.tile([P, N], U8, name=f"w4_s{a}", align_bytes=64) for a in range(2)]
-        z_w = [keep.tile([P, PM], U32, name=f"z_w{a}", align_bytes=64) for a in range(2)]
+        z_w = [
+            shared.tile([P, PM], U32, name="z_w0", align_bytes=64, offset=AT_LATE + 12 * KIB),
+            keep.tile([P, PM], U32, name="z_w1", align_bytes=64),
+        ]
         z_s = [keep.tile([P, PM], U8, name=f"z_s{a}", align_bytes=64) for a in range(2)]
         slot_w = {j0: keep.tile([P, PACK, 256], F32, name=f"slot_w{j0}") for j0 in (0, 256)}
         pages = [keep.tile([P, T2], F32, name=f"page{t}") for t in range(PACK)]
@@ -92,7 +98,7 @@ def tile_list_byte_patch_slots_kernel(
             return own
 
         def new_woven(width):
-            return ring.tile([P, width, PACK], BF16, name="woven", bufs=3, align_bytes=64)
+            return ring.tile([P, width, PACK], BF16, name="woven", bufs=5, align_bytes=64)
 
         def interleave(copy, woven, planes):
             copy(out=woven.rearrange("p (c i) t -> p c t i", i=4), in_=planes.rearrange("p t (c i) -> p c t i", i=4))
@@ -100,11 +106,11 @@ def tile_list_byte_patch_slots_kernel(
         def quantize(woven, words, scales):
             nc.vector.quantize_mx(out=words.bitcast(FP8X4), scales=scales, in_=woven.rearrange("p c t -> p (c t)"))
 
-        def prepare_weight(raw, words, scales):
+        def weave_weight(raw):
             woven = new_woven(BANK)
             for c0 in (0, 256):
                 interleave(nc.scalar.copy, woven[:, c0 : c0 + 256, :], raw[:, :, c0 : c0 + 256])
-            quantize(woven[:], words[:], scales[:])
+            return woven
 
         def gather_table(j0, width):
             picks = list1[:, j0 // 16 : (j0 + width) // 16]
@@ -189,22 +195,27 @@ def tile_list_byte_patch_slots_kernel(
                 )
             gate = ring.tile([P, BANK], F32, name="gate")
             nc.scalar.activation(out=gate[:], in_=q[:], func=ACT.Silu)
-            gate_size = ring.tile([P, BANK], F32, name="gate_size")
+            gate_size = ring.tile([P, BANK], F32, name="gate_size", bufs=3)
             nc.scalar.activation(out=gate_size[:], in_=gate[:], func=ACT.Abs)
-            third_size = ring.tile([P, BANK], F32, name="third_size")
+            third_size = ring.tile([P, BANK], F32, name="third_size", bufs=3)
             nc.scalar.activation(out=third_size[:], in_=third[:], func=ACT.Abs)
-            nc.gpsimd.tensor_tensor(
-                out=weighted[:].rearrange("p (t j) -> p t j", j=width),
+            engine = nc.vector if u == 0 else nc.gpsimd
+            engine.tensor_tensor(
+                out=weighted.rearrange("p (t j) -> p t j", j=width),
                 in0=gate_size[:].rearrange("p (t j) -> p t j", j=width),
                 in1=slot_w[start][:, t0 : t0 + len(slices), j0 - start : j0 - start + width],
                 op=ALU.mult,
             )
-            h = ring.tile([P, BANK], F32, name="h")
-            nc.gpsimd.tensor_tensor(out=h[:], in0=weighted[:], in1=third_size[:], op=ALU.mult)
+            if u == 7:
+                h = shared.tile([P, BANK], F32, name="last_h", offset=AT_Z0)
+            else:
+                h = ring.tile([P, BANK], F32, name="h", bufs=3)
+            engine.tensor_tensor(out=h[:], in0=weighted, in1=third_size[:], op=ALU.mult)
             states[u] = h
 
-        def new_weighted():
-            return ring.tile([P, BANK], F32, name="weighted", bufs=1)
+        def new_weighted(u):
+            columns = 5 * KIB if u == len(units) - 1 else BANK
+            return shared.tile([P, columns], F32, name=f"weighted{u}", offset=AT_LATE)[:, 0:BANK]
 
         def put_state(u):
             a, j0, width, t0 = units[u]
@@ -273,7 +284,7 @@ def tile_list_byte_patch_slots_kernel(
         reorder_w3(1)
         slot_w[BANK] = ring.tile([P, PACK, BANK], F32, name="slot_w_late", tag="w2_then_slots", bufs=1)
         load_slot_weights(BANK, BANK)
-        make_state(0, new_weighted())
+        make_state(0, new_weighted(0))
         token_major(2)
         token_major(3)
         gather_table(512, 512)
@@ -281,31 +292,31 @@ def tile_list_byte_patch_slots_kernel(
         own = load_ctx(0)
 
         for u in range(7):
-            make_state(u + 1, new_weighted())
+            make_state(u + 1, new_weighted(u + 1))
             put_state(u)
             if u < 4:
                 token_major(u + 4)
             elif u == 4:
-                prepare_weight(raw, w2_w[1], w2_s[1])
+                quantize(weave_weight(raw)[:], w2_w[1][:], w2_s[1][:])
                 raw = load_weight(w4[0:BANK, :])
             else:
                 token_major(u + 3)
-        make_state(8, new_weighted())
+        make_state(8, new_weighted(8))
         put_state(7)
-        z0 = ring.tile([P, PACK, PM], F32, name="z0", bufs=1)
+        z0 = shared.tile([P, PACK, PM], F32, name="z0", offset=AT_Z0)
         fetch(z0, own, 0, PM)
         token_major(10)
         token_major(11)
-        make_state(9, ring.tile([P, BANK], F32, name="weighted_after_fetch", tag="table_then_ctx", bufs=1))
+        make_state(9, ring.tile([P, BANK], F32, name="weighted_after_fetch", tag="table_then_ctx", bufs=1)[:])
         own = load_ctx(1)
         put_state(8)
         token_major(12)
         token_major(13)
-        prepare_weight(raw, w4_w[0], w4_s[0])
+        woven_w4 = weave_weight(raw)
         raw = load_weight(w4[BANK : 2 * BANK, :])
         woven_z = []
         for u in range(9, 15):
-            make_state(u + 1, new_weighted())
+            make_state(u + 1, new_weighted(u + 1))
             put_state(u)
             if u < 11:
                 token_major(u + 5)
@@ -314,11 +325,12 @@ def tile_list_byte_patch_slots_kernel(
                 if c0 % BANK == 0:
                     woven_z.append(new_woven(BANK))
                 interleave(nc.scalar.copy, woven_z[-1][:, c0 % BANK : c0 % BANK + 256, :], z0[:, :, c0 : c0 + 256])
-            if u == 13:
-                quantize(woven_z[0][:], z_w[0][:, 0:BANK], z_s[0][:, 0:BANK])
         put_state(15)
-        quantize(woven_z[1][:], z_w[0][:, BANK:PM], z_s[0][:, BANK:PM])
-        prepare_weight(raw, w4_w[1], w4_s[1])
+        quantize(woven_w4[:], w4_w[0][:], w4_s[0][:])
+        for half in range(2):
+            cols = slice(BANK * half, BANK * (half + 1))
+            quantize(woven_z[half][:], z_w[0][:, cols], z_s[0][:, cols])
+        quantize(weave_weight(raw)[:], w4_w[1][:], w4_s[1][:])
 
         width = LAST_CHUNK
         starts = list(range(0, PM, width))
@@ -326,10 +338,10 @@ def tile_list_byte_patch_slots_kernel(
         for nt in range(4):
             last_pass(open_acc[nt][:, :width], 0, nt, starts[-1], width)
 
-        def weave(m0, z):
+        def weave(copy, m0, z):
             cols = slice(m0, m0 + width)
             woven = new_woven(width)
-            interleave(nc.scalar.copy, woven[:], z[:])
+            interleave(copy, woven[:], z)
             quantize(woven[:], z_w[1][:, cols], z_s[1][:, cols])
 
         def finish(m0):
@@ -342,22 +354,21 @@ def tile_list_byte_patch_slots_kernel(
                 nc.scalar.copy(out=result[:, 2 * pair : 2 * pair + 2, :], in_=acc[:])
             nc.sync.dma_start(out=out_rows[:, :, m0 : m0 + width], in_=result[:])
 
-        def fetch_chunk(m0):
-            z = ring.tile([P, PACK, width], F32, name="z")
-            fetch(z, own, m0, width)
+        def fetch_late(m0, columns, at):
+            z = shared.tile([P, PACK, columns], F32, name=f"z_late{m0}", offset=AT_LATE + at)
+            fetch(z, own, m0, columns)
             return z
 
-        z = fetch_chunk(starts[0])
-        for c, m0 in enumerate(starts[:-1]):
-            weave(m0, z)
-            z = fetch_chunk(m0 + width)
-            if c > 0:
-                finish(m0 - width)
-        finish(starts[-2])
+        z_first = fetch_late(0, BANK, 0)
+        z_third = fetch_late(BANK, width, 8 * KIB)
+        weave(nc.scalar.copy, 0, z_first[:, :, 0:width])
+        weave(nc.scalar.copy, width, z_first[:, :, width:BANK])
+        z_last = fetch_late(starts[-1], width, 0)
+        weave(nc.scalar.copy, BANK, z_third[:])
+        for m0 in starts[:-1]:
+            finish(m0)
+        weave(nc.vector.tensor_copy, starts[-1], z_last[:])
         cols = slice(starts[-1], PM)
-        woven = new_woven(width)
-        interleave(nc.vector.tensor_copy, woven[:], z[:])
-        quantize(woven[:], z_w[1][:, cols], z_s[1][:, cols])
         for nt in range(4):
             last_pass(open_acc[nt][:, :width], 1, nt, starts[-1], width)
         for pair, copy in enumerate((nc.scalar.copy, nc.vector.tensor_copy)):

@@ -20,10 +20,20 @@ ACT = mybir.ActivationFunctionType
 P = 128
 PACK = 4
 BANK = 512
-LAST_CHUNK = 256
+QUARTER = 256
 KIB = 1024
-AT_Z0 = 5 * KIB
-AT_LATE = 21 * KIB
+AT_RAW = (106 * KIB, 82 * KIB)
+AT_CTX = 90 * KIB
+AT_FIRST_WOVEN = 16 * KIB
+AT_FIRST_STATES = 24 * KIB
+AT_WEIGHTED = 26 * KIB
+AT_SECOND_WOVEN = 28 * KIB
+AT_LATE_WEIGHTED = 32 * KIB
+AT_Z0_WOVEN = 38 * KIB
+AT_W2_LATE = 46 * KIB
+AT_Z = 48 * KIB
+AT_LATE_CODES = 64 * KIB
+AT_TABLE = 74 * KIB
 
 
 def tile_list_byte_patch_slots_kernel(
@@ -36,69 +46,70 @@ def tile_list_byte_patch_slots_kernel(
         shared = stack.enter_context(tc.tile_pool(name="shared", bufs=1))
         psum = stack.enter_context(tc.psum_pool(name="psum", bufs=2))
 
+        def at(offset, name, shape, dtype):
+            return shared.tile(shape, dtype, name=name, align_bytes=64, offset=offset)
+
         list1 = keep.tile([P, S // 16], U16, name="list1")
         list2 = keep.tile([P, S // 16], U16, name="list2")
         list3 = keep.tile([P, PM // 16], U16, name="list3")
-        tab_w = ring.tile([P, T], I32, name="tab_w", tag="table_then_ctx", bufs=1)
-        tab_s = keep.tile([P, T], U8, name="tab_s", align_bytes=64)
-        v_w = {
-            0: keep.tile([P, 256], U32, name="v_w0", align_bytes=64),
-            256: keep.tile([P, 256], U32, name="v_w1", align_bytes=64),
-            512: shared.tile([P, 512], U32, name="v_w2", align_bytes=64, offset=0),
-        }
-        v_s = {
-            0: keep.tile([P, 256], U8, name="v_s0", align_bytes=64),
-            256: keep.tile([P, 256], U8, name="v_s1", align_bytes=64),
-            512: shared.tile([P, 512], U8, name="v_s2", align_bytes=64, offset=4 * H),
-        }
-
-        def picked_columns(j0, width):
-            start = max(s for s in v_w if s <= j0)
-            cols = slice(j0 - start, j0 - start + width)
-            return v_w[start][:, cols].bitcast(FP8X4), v_s[start][:, cols]
-
+        tab_w = at(AT_TABLE, "tab_w", [P, T], I32)
+        tab_s = at(AT_CTX, "tab_s", [P, T], U8)
+        v_w = [
+            keep.tile([P, QUARTER], U32, name="v_w0", align_bytes=64),
+            at(AT_FIRST_WOVEN + 4 * KIB, "v_w1", [P, QUARTER], U32),
+            at(AT_FIRST_WOVEN + 5 * KIB, "v_w2", [P, QUARTER], U32),
+            at(AT_FIRST_STATES + KIB, "v_w3", [P, QUARTER], U32),
+        ]
+        v_s = [
+            keep.tile([P, QUARTER], U8, name="v_s0", align_bytes=64),
+            at(AT_FIRST_WOVEN + 6 * KIB, "v_s1", [P, QUARTER], U8),
+            at(AT_FIRST_WOVEN + 7 * KIB, "v_s2", [P, QUARTER], U8),
+            at(AT_FIRST_STATES, "v_s3", [P, QUARTER], U8),
+        ]
         w1_w = keep.tile([P, 2 * H], U8, name="w1_w", align_bytes=64)
         w1_s = keep.tile([P, H], U8, name="w1_s", align_bytes=64)
-        w3_raw_w = shared.tile([P, H], I32, name="w3_raw_w", align_bytes=64, offset=0)
-        w3_raw_s = shared.tile([P, H], U8, name="w3_raw_s", align_bytes=64, offset=4 * H)
-        w3_w = keep.tile([P, H], I32, name="w3_w", align_bytes=64)
-        w3_s = keep.tile([P, H], U8, name="w3_s", align_bytes=64)
-        w2_w = [keep.tile([P, BANK], U32, name=f"w2_w{a}", align_bytes=64) for a in range(2)]
+        w3_raw_w = [at(AT_RAW[1], "w3_raw_w0", [P, BANK], I32), at(8 * KIB, "w3_raw_w1", [P, BANK], I32)]
+        w3_raw_s = at(AT_RAW[1] + 4 * KIB, "w3_raw_s", [P, H], U8)
+        w3_w = [at(AT_FIRST_WOVEN + 2 * KIB * a, f"w3_w{a}", [P, BANK], I32) for a in range(2)]
+        w3_s = [keep.tile([P, BANK], U8, name=f"w3_s{a}", align_bytes=64) for a in range(2)]
+        w2_w = [keep.tile([P, BANK], U32, name="w2_w0", align_bytes=64), at(AT_W2_LATE, "w2_w1", [P, BANK], U32)]
         w2_s = [keep.tile([P, BANK], U8, name=f"w2_s{a}", align_bytes=64) for a in range(2)]
-        w4_w = [shared.tile([P, N], U32, name=f"w4_w{a}", align_bytes=64, offset=AT_LATE + (16 + 2 * a) * KIB) for a in range(2)]
+        w4_w = [at(AT_LATE_CODES + 2 * KIB * a, f"w4_w{a}", [P, N], U32) for a in range(2)]
         w4_s = [keep.tile([P, N], U8, name=f"w4_s{a}", align_bytes=64) for a in range(2)]
-        z_w = [
-            shared.tile([P, PM], U32, name="z_w0", align_bytes=64, offset=AT_LATE + 12 * KIB),
-            keep.tile([P, PM], U32, name="z_w1", align_bytes=64),
-        ]
+        z0_w = [at(AT_LATE_CODES + (4, 6, 7, 8)[i] * KIB, f"z0_w{i}", [P, QUARTER], U32) for i in range(4)]
+        z1_w = keep.tile([P, PM], U32, name="z1_w", align_bytes=64)
         z_s = [keep.tile([P, PM], U8, name=f"z_s{a}", align_bytes=64) for a in range(2)]
-        slot_w = {j0: keep.tile([P, PACK, 256], F32, name=f"slot_w{j0}") for j0 in (0, 256)}
+        slot_w = {
+            0: keep.tile([P, PACK, QUARTER], F32, name="slot_w0"),
+            256: at(4 * KIB, "slot_w256", [P, PACK, QUARTER], F32),
+            512: at(AT_TABLE, "slot_w512", [P, PACK, BANK], F32),
+        }
         pages = [keep.tile([P, T2], F32, name=f"page{t}") for t in range(PACK)]
         ident = keep.tile([P, P], F32, name="ident")
 
-        def load_scales(queue, plane, rows):
-            for q in range(4):
-                queue.dma_start(out=plane[32 * q : 32 * q + 4, :].bitcast(I32), in_=rows[0, 4 * q : 4 * q + 4, :].bitcast(I32))
+        def load_scales(plane, rows, quadrants=range(4)):
+            for q in quadrants:
+                nc.sync.dma_start(out=plane[32 * q : 32 * q + 4, :].bitcast(I32), in_=rows[0, 4 * q : 4 * q + 4, :].bitcast(I32))
 
-        def load_slot_weights(j0, width):
+        def load_slot_weights(j0):
             rows = wgs.rearrange("(m t) j -> m t j", t=PACK)
+            width = slot_w[j0].shape[2]
             for q in range(4):
                 nc.sync.dma_start(out=slot_w[j0][32 * q : 32 * q + 32, :, :], in_=rows[:, :, j0 : j0 + width])
 
-        def load_weight(rows, tag="raw", pieces=1):
-            raw = ring.tile([P, PACK, BANK], F32, name="raw", tag=tag, bufs=1)
-            step = BANK // pieces
-            for c0 in range(0, BANK, step):
-                nc.sync.dma_start(out=raw[:, :, c0 : c0 + step], in_=rows.rearrange("(p t) c -> p t c", t=PACK)[:, :, c0 : c0 + step])
+        def load_weight(name, offset, rows):
+            raw = at(offset, name, [P, PACK, rows.shape[1]], F32)
+            nc.sync.dma_start(out=raw[:], in_=rows.rearrange("(p t) c -> p t c", t=PACK))
             return raw
 
+        def load_w3_words(a):
+            words = w3_words[0].rearrange("p c i -> p (c i)").bitcast(I32)
+            nc.sync.dma_start(out=w3_raw_w[a][:], in_=words[:, BANK * a : BANK * (a + 1)])
+
         def load_ctx(a):
-            own = ring.tile([P, PACK, PM], F32, name="own", tag="table_then_ctx", bufs=1)
+            own = at(AT_CTX, f"own{a}", [P, PACK, PM], F32)
             nc.sync.dma_start(out=own[:], in_=ctx[BANK * a : BANK * (a + 1), :].rearrange("(p t) m -> p t m", t=PACK))
             return own
-
-        def new_woven(width):
-            return ring.tile([P, width, PACK], BF16, name="woven", bufs=5, align_bytes=64)
 
         def interleave(copy, woven, planes):
             copy(out=woven.rearrange("p (c i) t -> p c t i", i=4), in_=planes.rearrange("p t (c i) -> p c t i", i=4))
@@ -106,273 +117,287 @@ def tile_list_byte_patch_slots_kernel(
         def quantize(woven, words, scales):
             nc.vector.quantize_mx(out=words.bitcast(FP8X4), scales=scales, in_=woven.rearrange("p c t -> p (c t)"))
 
-        def weave_weight(raw):
-            woven = new_woven(BANK)
-            for c0 in (0, 256):
-                interleave(nc.scalar.copy, woven[:, c0 : c0 + 256, :], raw[:, :, c0 : c0 + 256])
-            return woven
+        def gather_table(quarter):
+            picks = list1[:, 16 * quarter : 16 * (quarter + 1)]
+            nc.vector.tensor_copy(out=v_w[quarter][:], in_=tab_w[:].bitcast(U32).indirect(picks))
+            nc.vector.tensor_copy(out=v_s[quarter][:], in_=tab_s[:].indirect(picks))
 
-        def gather_table(j0, width):
-            picks = list1[:, j0 // 16 : (j0 + width) // 16]
-            nc.vector.tensor_copy(out=v_w[j0][:], in_=tab_w[:].bitcast(U32).indirect(picks))
-            nc.vector.tensor_copy(out=v_s[j0][:], in_=tab_s[:].indirect(picks))
-
-        def reorder_w3(a):
+        def reorder_w3(a, t0, count):
             cols = slice(BANK * a, BANK * (a + 1))
-            nc.vector.tensor_copy(
-                out=w3_w[:, cols].rearrange("p (t b i) -> p b t i", t=PACK, i=4),
-                in_=w3_raw_w[:, cols].rearrange("p (b i t) -> p b t i", t=PACK, i=4),
-            )
-            nc.vector.tensor_copy(
-                out=w3_s[:, cols].rearrange("p (t b i) -> p b t i", t=PACK, i=16),
-                in_=w3_raw_s[:, cols].rearrange("p (b i t) -> p b t i", t=PACK, i=16),
-            )
+            for dst, src in ((w3_w[a], w3_raw_w[a][:]), (w3_s[a], w3_raw_s[:, cols])):
+                nc.gpsimd.tensor_copy(
+                    out=dst[:].rearrange("p (t m) -> p t m", t=PACK)[:, t0 : t0 + count, :],
+                    in_=src.rearrange("p (m t) -> p t m", t=PACK)[:, t0 : t0 + count, :],
+                )
 
         relu_t, second_t = {}, {}
 
+        def token_product(e, tag, words, scales):
+            jt = e % (S // P)
+            cols = slice(P * (jt % 2), P * (jt % 2 + 1))
+            bank = psum.tile([P, BANK], F32, name="bank", tag=tag)
+            nc.tensor.matmul_mx(
+                out=bank[:],
+                lhsT=v_w[jt // 2][:, cols].bitcast(FP8X4),
+                lhsT_scale=v_s[jt // 2][:, cols],
+                rhs=words,
+                rhs_scale=scales,
+                start=True,
+                stop=True,
+            )
+            return bank[:].rearrange("j (m t) -> j t m", t=PACK)
+
+        def first_product(e):
+            a = e // (S // P)
+            words = w1_w[:, 2 * BANK * a : 2 * BANK * (a + 1)].bitcast(FP4X4)
+            by_slice = token_product(e, "first", words, w1_s[:, BANK * a : BANK * (a + 1)])
+            relu_t[e] = ring.tile([P, PACK, P], F32, name="d", tag="d", bufs=8, align_bytes=64)
+            nc.scalar.activation(out=relu_t[e][:], in_=by_slice, func=ACT.Relu)
+
+        def second_product(e):
+            a = e // (S // P)
+            by_slice = token_product(e, "second", w2_w[a][:].bitcast(FP8X4), w2_s[a][:])
+            second_t[e] = ring.tile([P, PACK, P], F32, name="s2", tag="s2", bufs=8, align_bytes=64)
+            nc.scalar.copy(out=second_t[e][:], in_=by_slice)
+
         def token_major(e):
-            a, jt = divmod(e, S // P)
-            words, scales = picked_columns(P * jt, P)
-            bank1 = psum.tile([P, BANK], F32, name="bank1", tag="first")
-            nc.tensor.matmul_mx(
-                out=bank1[:],
-                lhsT=words,
-                lhsT_scale=scales,
-                rhs=w1_w[:, 2 * BANK * a : 2 * BANK * (a + 1)].bitcast(FP4X4),
-                rhs_scale=w1_s[:, BANK * a : BANK * (a + 1)],
-                start=True,
-                stop=True,
-            )
-            bank2 = psum.tile([P, BANK], F32, name="bank2", tag="second")
-            nc.tensor.matmul_mx(
-                out=bank2[:],
-                lhsT=words,
-                lhsT_scale=scales,
-                rhs=w2_w[a][:].bitcast(FP8X4),
-                rhs_scale=w2_s[a][:],
-                start=True,
-                stop=True,
-            )
-            d = ring.tile([P, PACK, P], F32, name="d", bufs=8)
-            s2 = ring.tile([P, PACK, P], F32, name="s2", bufs=8)
-            by_slice1, by_slice2 = (bank[:].rearrange("j (m t) -> j t m", t=PACK) for bank in (bank1, bank2))
-            if e in (2, 3):
-                nc.vector.tensor_scalar_max(d[:], by_slice1, 0.0)
-                nc.vector.tensor_copy(out=s2[:], in_=by_slice2)
-            else:
-                nc.scalar.activation(out=d[:], in_=by_slice1, func=ACT.Relu)
-                nc.scalar.copy(out=s2[:], in_=by_slice2)
-            relu_t[e], second_t[e] = d, s2
+            first_product(e)
+            second_product(e)
 
-        units = [(0, j0, 256, t0) for j0 in range(0, S, 256) for t0 in (0, 2)]
-        units += [(1, j0, 256, t0) for j0 in (0, 256) for t0 in (0, 2)]
-        units += [(1, BANK, BANK, t0) for t0 in range(PACK)]
-        states = {}
-
-        def make_state(u, weighted):
-            a, j0, width, t0 = units[u]
-            slices = range(t0, t0 + BANK // width)
+        def make_state(unit, weighted, h, third_size=None, tags=("third", "sum")):
+            a, j0, width, t0, count = unit
+            total = width * count
             start = min(j0, BANK)
-            q = psum.tile([P, BANK], F32, name="q", tag="sum")
-            for t in slices:
-                for i in range(width // P):
-                    e = a * (S // P) + j0 // P + i
-                    c0 = (t - t0) * width + P * i
-                    nc.tensor.matmul(q[:, c0 : c0 + P], lhsT=relu_t[e][:, t, :], rhs=ident[:], is_transpose=True, start=True, stop=False)
-                    nc.tensor.matmul(q[:, c0 : c0 + P], lhsT=second_t[e][:, t, :], rhs=ident[:], is_transpose=True, start=False, stop=True)
-            third = psum.tile([P, BANK], F32, name="third", tag="third")
-            words, scales = picked_columns(j0, width)
-            for t in slices:
-                rows = slice(BANK * a + P * t, BANK * a + P * (t + 1))
+            third = psum.tile([P, total], F32, name="third", tag=tags[0])
+            for i in range(total // QUARTER):
+                t, quarter = t0 + QUARTER * i // width, (j0 + QUARTER * i % width) // QUARTER
                 nc.tensor.matmul_mx(
-                    out=third[:, (t - t0) * width : (t - t0 + 1) * width],
-                    lhsT=w3_w[:, rows].bitcast(FP8X4),
-                    lhsT_scale=w3_s[:, rows],
-                    rhs=words,
-                    rhs_scale=scales,
+                    out=third[:, QUARTER * i : QUARTER * (i + 1)],
+                    lhsT=w3_w[a][:, P * t : P * (t + 1)].bitcast(FP8X4),
+                    lhsT_scale=w3_s[a][:, P * t : P * (t + 1)],
+                    rhs=v_w[quarter][:].bitcast(FP8X4),
+                    rhs_scale=v_s[quarter][:],
                     start=True,
                     stop=True,
                 )
-            gate = ring.tile([P, BANK], F32, name="gate")
+            q = psum.tile([P, total], F32, name="q", tag=tags[1])
+            for i in range(total // P):
+                t, e = t0 + P * i // width, a * (S // P) + (j0 + P * i % width) // P
+                cols = slice(P * i, P * (i + 1))
+                nc.tensor.matmul(q[:, cols], lhsT=relu_t[e][:, t, :], rhs=ident[:], is_transpose=True, start=True, stop=False)
+                nc.tensor.matmul(q[:, cols], lhsT=second_t[e][:, t, :], rhs=ident[:], is_transpose=True, start=False, stop=True)
+            if third_size is None:
+                third_size = ring.tile([P, total], F32, name="third_size", bufs=3)[:]
+            nc.scalar.activation(out=third_size, in_=third[:], func=ACT.Abs)
+            gate = ring.tile([P, total], F32, name="gate")
             nc.scalar.activation(out=gate[:], in_=q[:], func=ACT.Silu)
-            gate_size = ring.tile([P, BANK], F32, name="gate_size", bufs=3)
+            gate_size = ring.tile([P, total], F32, name="gate_size", bufs=3)
             nc.scalar.activation(out=gate_size[:], in_=gate[:], func=ACT.Abs)
-            third_size = ring.tile([P, BANK], F32, name="third_size", bufs=3)
-            nc.scalar.activation(out=third_size[:], in_=third[:], func=ACT.Abs)
-            engine = nc.vector if u == 0 else nc.gpsimd
-            engine.tensor_tensor(
+            nc.gpsimd.tensor_tensor(
                 out=weighted.rearrange("p (t j) -> p t j", j=width),
-                in0=gate_size[:].rearrange("p (t j) -> p t j", j=width),
-                in1=slot_w[start][:, t0 : t0 + len(slices), j0 - start : j0 - start + width],
+                in0=third_size.rearrange("p (t j) -> p t j", j=width),
+                in1=slot_w[start][:, t0 : t0 + count, j0 - start : j0 - start + width],
                 op=ALU.mult,
             )
-            if u == 7:
-                h = shared.tile([P, BANK], F32, name="last_h", offset=AT_Z0)
-            else:
-                h = ring.tile([P, BANK], F32, name="h", bufs=3)
-            engine.tensor_tensor(out=h[:], in0=weighted, in1=third_size[:], op=ALU.mult)
-            states[u] = h
+            nc.gpsimd.tensor_tensor(out=h, in0=weighted, in1=gate_size[:], op=ALU.mult)
 
-        def new_weighted(u):
-            columns = 5 * KIB if u == len(units) - 1 else BANK
-            return shared.tile([P, columns], F32, name=f"weighted{u}", offset=AT_LATE)[:, 0:BANK]
-
-        def put_state(u):
-            a, j0, width, t0 = units[u]
-            for i in range(BANK // width):
+        def put_state(unit, h):
+            a, j0, width, t0, count = unit
+            for i in range(count):
                 nc.vector.tensor_copy(
                     out=pages[t0 + i][:].indirect(list2[:, j0 // 16 : (j0 + width) // 16]),
-                    in_=states[u][:, i * width : (i + 1) * width],
+                    in_=h[:, i * width : (i + 1) * width],
                 )
 
-        def fetch(z, own, m0, width):
-            for t in range(PACK):
-                nc.vector.tensor_tensor(
-                    out=z[:, t, :],
-                    in0=pages[t][:].indirect(list3[:, m0 // 16 : (m0 + width) // 16]),
-                    in1=own[:, t, m0 : m0 + width],
-                    op=ALU.add,
-                )
-
-        def last_pass(acc, a, nt, m0, width):
-            nc.tensor.matmul_mx(
-                out=acc,
-                lhsT=w4_w[a][:, P * nt : P * (nt + 1)].bitcast(FP8X4),
-                lhsT_scale=w4_s[a][:, P * nt : P * (nt + 1)],
-                rhs=z_w[a][:, m0 : m0 + width].bitcast(FP8X4),
-                rhs_scale=z_s[a][:, m0 : m0 + width],
-                start=(a == 0),
-                stop=(a == 1),
+        def fetch(z, own, t, m0, width):
+            nc.vector.tensor_tensor(
+                out=z,
+                in0=pages[t][:].indirect(list3[:, m0 // 16 : (m0 + width) // 16]),
+                in1=own[:, t, m0 : m0 + width],
+                op=ALU.add,
             )
+
+        def part_of(offset, name, kib, columns=BANK):
+            return at(offset, name, [P, kib * KIB // 4], F32)[:, 0:columns]
+
+        def ring_state():
+            return ring.tile([P, BANK], F32, name="h", bufs=3)[:]
 
         out_rows = out.rearrange("(nt p) m -> p nt m", p=P)
 
         for plane in (tab_s, w3_raw_s):
             nc.gpsimd.memset(plane[:].bitcast(I32), 0)
         make_identity(nc, ident[:])
-        for t in (2, 3):
-            nc.gpsimd.memset(pages[t][:].bitcast(I32), 0)
-        nc.sync.dma_start(list1[:], offs)
-        load_scales(nc.sync, w1_s, w1_scales)
-        nc.sync.dma_start(list2[:], offs2)
-        nc.sync.dma_start(list3[:], offs3)
-        nc.sync.dma_start(out=tab_w[:], in_=tab_words[0].rearrange("p c i -> p (c i)").bitcast(I32))
-        load_scales(nc.sync, tab_s, tab_scales)
-        nc.sync.dma_start(out=w1_w[:].bitcast(I32), in_=w1_words[0].bitcast(I32))
-        raw = load_weight(w2[:, 0:BANK], "w2_then_slots", 2)
-        nc.sync.dma_start(out=w3_raw_w[:], in_=w3_words[0].rearrange("p c i -> p (c i)").bitcast(I32))
-        load_scales(nc.sync, w3_raw_s, w3_scales)
-        load_slot_weights(0, 256)
-        load_slot_weights(256, 256)
-
+        for t in range(PACK):
+            (nc.vector if t < 2 else nc.gpsimd).memset(pages[t][:].bitcast(I32), 0)
         warm = keep.tile([P, 1], F32, name="warm")
         nc.scalar.activation(out=warm[:], in_=ident[:, 0:1], func=ACT.Silu)
-        gather_table(0, 256)
-        first_woven = new_woven(BANK)
-        for c0 in (0, 256):
-            cols = slice(c0, c0 + 256)
-            interleave(nc.vector.tensor_copy, first_woven[:, cols, :], raw[:, :, cols])
-        for c0 in (0, 256):
-            cols = slice(c0, c0 + 256)
-            quantize(first_woven[:, cols, :], w2_w[0][:, cols], w2_s[0][:, cols])
-        for t in (0, 1):
-            nc.vector.memset(pages[t][:].bitcast(I32), 0)
-        token_major(0)
-        token_major(1)
-        gather_table(256, 256)
-        reorder_w3(0)
-        reorder_w3(1)
-        slot_w[BANK] = ring.tile([P, PACK, BANK], F32, name="slot_w_late", tag="w2_then_slots", bufs=1)
-        load_slot_weights(BANK, BANK)
-        make_state(0, new_weighted(0))
-        token_major(2)
-        token_major(3)
-        gather_table(512, 512)
-        raw = load_weight(w2[:, BANK : 2 * BANK])
+        nc.sync.dma_start(list1[:], offs)
+        load_scales(w1_s, w1_scales, (0, 1))
+        nc.sync.dma_start(out=tab_w[:], in_=tab_words[0].rearrange("p c i -> p (c i)").bitcast(I32))
+        load_scales(tab_s, tab_scales)
+        load_scales(w1_s, w1_scales, (2, 3))
+        raw = at(0, "w2_raw", [P, 5, BANK], F32)[:, 0:PACK, :]
+        nc.sync.dma_start(out=raw, in_=w2[:, 0:BANK].rearrange("(p t) c -> p t c", t=PACK))
+        nc.sync.dma_start(out=w1_w[:].bitcast(I32), in_=w1_words[0].bitcast(I32))
+        load_w3_words(0)
+        load_scales(w3_raw_s, w3_scales)
+        load_slot_weights(0)
+        nc.sync.dma_start(list2[:], offs2)
+        nc.sync.dma_start(list3[:], offs3)
+
+        gather_table(0)
+        woven = at(AT_FIRST_WOVEN, "w2_woven", [P, 2 * BANK, PACK], BF16)
+        for cols, copy in ((slice(0, 192), nc.scalar.copy), (slice(192, BANK), nc.vector.tensor_copy)):
+            interleave(copy, woven[:, cols, :], raw[:, :, cols])
+        quantize(woven[:, 0:BANK, :], w2_w[0][:], w2_s[0][:])
+        load_slot_weights(256)
+        load_w3_words(1)
+        reorder_w3(0, 0, 2)
+        reorder_w3(0, 2, 2)
+        gather_table(1)
+        gather_table(2)
+        first_product(0)
+        first_product(1)
+        second_product(0)
+        second_product(1)
+
+        def weave_halves(woven, raw):
+            for c0 in (0, 256):
+                interleave(nc.scalar.copy, woven[:, c0 : c0 + 256, :], raw[:, :, c0 : c0 + 256])
+
+        singles = [(0, 0, QUARTER, t, 1) for t in range(2)]
+        states = [part_of(AT_FIRST_STATES + KIB * t, f"first_h{t}", 1, QUARTER) for t in range(2)]
+        for t in range(2):
+            make_state(singles[t], part_of(AT_WEIGHTED, f"first_weighted{t}", 2, QUARTER), states[t], tags=("first", "second"))
+        reorder_w3(1, 0, PACK)
+        raw_late = load_weight("w2_raw_late", AT_RAW[1], w2[:, BANK : 2 * BANK])
+        for t in range(2):
+            put_state(singles[t], states[t])
+        gather_table(3)
+        load_slot_weights(512)
         own = load_ctx(0)
 
-        for u in range(7):
-            make_state(u + 1, new_weighted(u + 1))
-            put_state(u)
-            if u < 4:
-                token_major(u + 4)
-            elif u == 4:
-                quantize(weave_weight(raw)[:], w2_w[1][:], w2_s[1][:])
-                raw = load_weight(w4[0:BANK, :])
-            else:
-                token_major(u + 3)
-        make_state(8, new_weighted(8))
-        put_state(7)
-        z0 = shared.tile([P, PACK, PM], F32, name="z0", offset=AT_Z0)
-        fetch(z0, own, 0, PM)
+        pairs = [(a, j0, QUARTER, t0, 2) for a in range(2) for j0 in range(0, S, QUARTER) for t0 in (0, 2)]
+        for u in range(1, 7):
+            h = part_of(AT_W2_LATE, "h_before_w2", 2) if u == 5 else ring_state()
+            make_state(pairs[u], part_of(AT_WEIGHTED, f"weighted{u}", 2), h)
+            put_state(pairs[u], h)
+            if u == 1:
+                token_major(2)
+            if u < 6:
+                token_major(u + 2)
+            if u == 3:
+                woven = at(AT_SECOND_WOVEN, "w2_woven_late", [P, BANK, PACK], BF16)
+                weave_halves(woven, raw_late)
+                raw_w4 = [load_weight(f"w4_raw{a}", (AT_RAW[1], 8 * KIB)[a], w4[BANK * a : BANK * (a + 1), :]) for a in range(2)]
+            if u == 5:
+                quantize(woven[:], w2_w[1][:], w2_s[1][:])
+        z0 = at(AT_Z, "z0", [P, PACK, PM], F32)
+        h_last = ring_state()
+        make_state(pairs[7], part_of(AT_WEIGHTED, "weighted7", 6), h_last)
+        token_major(8)
+        token_major(9)
+        for t in (0, 1):
+            fetch(z0[:, t, :], own, t, 0, PM)
+        h = ring_state()
+        make_state(pairs[8], own[:, 1, 0:BANK], h)
+        put_state(pairs[7], h_last)
+        for t in (2, 3):
+            fetch(z0[:, t, :], own, t, 0, PM)
+        put_state(pairs[8], h)
         token_major(10)
         token_major(11)
-        make_state(9, ring.tile([P, BANK], F32, name="weighted_after_fetch", tag="table_then_ctx", bufs=1)[:])
+        h = ring_state()
+        make_state(pairs[9], own[:, 3, 0:BANK], h, part_of(AT_LATE_WEIGHTED, "third_size9", 6))
+        put_state(pairs[9], h)
         own = load_ctx(1)
-        put_state(8)
-        token_major(12)
-        token_major(13)
-        woven_w4 = weave_weight(raw)
-        raw = load_weight(w4[BANK : 2 * BANK, :])
+        for e in range(12, 16):
+            token_major(e)
+        woven_w4 = [
+            at(AT_SECOND_WOVEN, "w4_woven0", [P, BANK, PACK], BF16),
+            at(AT_LATE_WEIGHTED + 2 * KIB, "w4_woven1", [P, BANK, PACK], BF16),
+        ]
+        late = pairs[10:12] + [(1, BANK, BANK, t, 1) for t in range(PACK)]
         woven_z = []
-        for u in range(9, 15):
-            make_state(u + 1, new_weighted(u + 1))
-            put_state(u)
-            if u < 11:
-                token_major(u + 5)
+        for i, unit in enumerate(late):
+            third_size = part_of(AT_Z0_WOVEN + 2 * KIB * i, f"late_third_size{i}", 2) if i < 4 else None
+            h = part_of(AT_Z, "last_h", 25) if i == len(late) - 1 else ring_state()
+            make_state(unit, part_of(AT_LATE_WEIGHTED, f"late_weighted{i}", 2), h, third_size)
+            put_state(unit, h)
+            if i < 2:
+                weave_halves(woven_w4[i], raw_w4[i])
+            if i < 4:
+                woven_z.append(at(AT_Z0_WOVEN + 2 * KIB * i, f"z0_woven{i}", [P, QUARTER, PACK], BF16))
+                interleave(nc.scalar.copy, woven_z[i][:], z0[:, :, QUARTER * i : QUARTER * (i + 1)])
+
+        chunks = ((0, 256), (256, 256), (512, 256), (768, 128), (896, 128))
+        tags = (("first", "second"), ("first", "second"), ("sum", "third"), ("sum",), ("third", "first"))
+        banks, woven_late = {}, {}
+
+        def last_passes(c, a):
+            m0, width = chunks[c]
+            share = 4 // len(tags[c])
+            words = z1_w[:, m0 : m0 + width] if a else z0_w[m0 // QUARTER][:, m0 % QUARTER : m0 % QUARTER + width]
+            for b, tag in enumerate(tags[c]):
+                if a == 0:
+                    banks[c, b] = psum.tile([P, share, width], F32, name="acc", tag=tag)
+                for i in range(share):
+                    nt = share * b + i
+                    nc.tensor.matmul_mx(
+                        out=banks[c, b][:, i, :],
+                        lhsT=w4_w[a][:, P * nt : P * (nt + 1)].bitcast(FP8X4),
+                        lhsT_scale=w4_s[a][:, P * nt : P * (nt + 1)],
+                        rhs=words.bitcast(FP8X4),
+                        rhs_scale=z_s[a][:, m0 : m0 + width],
+                        start=(a == 0 and i == 0),
+                        stop=(a == 1 and i == share - 1),
+                    )
+
+        def fetch_chunk(c):
+            m0, width = chunks[c]
+            z = at(AT_Z + (4 * KIB if c == 3 else 0), f"z1_{c}", [P, 6 if c == 1 else PACK, width], F32)[:, 0:PACK, :]
+            for t in range(PACK):
+                fetch(z[:, t, :], own, t, m0, width)
+            if c == 0:
+                woven_late[c] = at(AT_LATE_CODES + 6 * KIB, "z1_woven0", [P, 384, PACK], BF16)[:, 0:width, :]
             else:
-                c0 = 256 * (u - 11)
-                if c0 % BANK == 0:
-                    woven_z.append(new_woven(BANK))
-                interleave(nc.scalar.copy, woven_z[-1][:, c0 % BANK : c0 % BANK + 256, :], z0[:, :, c0 : c0 + 256])
-        put_state(15)
-        quantize(woven_w4[:], w4_w[0][:], w4_s[0][:])
-        for half in range(2):
-            cols = slice(BANK * half, BANK * (half + 1))
-            quantize(woven_z[half][:], z_w[0][:, cols], z_s[0][:, cols])
-        quantize(weave_weight(raw)[:], w4_w[1][:], w4_s[1][:])
-
-        width = LAST_CHUNK
-        starts = list(range(0, PM, width))
-        open_acc = [psum.tile([P, BANK], F32, name=f"open{nt}", tag=("sum", "third")[nt % 2]) for nt in range(4)]
-        for nt in range(4):
-            last_pass(open_acc[nt][:, :width], 0, nt, starts[-1], width)
-
-        def weave(copy, m0, z):
-            cols = slice(m0, m0 + width)
-            woven = new_woven(width)
-            interleave(copy, woven[:], z)
-            quantize(woven[:], z_w[1][:, cols], z_s[1][:, cols])
-
-        def finish(m0):
-            result = ring.tile([P, 4, width], F32, name="result", bufs=3)
-            for pair in range(2):
-                acc = psum.tile([P, 2, width], F32, name="acc", tag=("first", "second")[pair])
-                for i in range(2):
-                    for a in range(2):
-                        last_pass(acc[:, i, :], a, 2 * pair + i, m0, width)
-                nc.scalar.copy(out=result[:, 2 * pair : 2 * pair + 2, :], in_=acc[:])
-            nc.sync.dma_start(out=out_rows[:, :, m0 : m0 + width], in_=result[:])
-
-        def fetch_late(m0, columns, at):
-            z = shared.tile([P, PACK, columns], F32, name=f"z_late{m0}", offset=AT_LATE + at)
-            fetch(z, own, m0, columns)
+                woven_late[c] = ring.tile([P, width, PACK], BF16, name="z1_woven", tag="s2", bufs=8, align_bytes=64)[:]
             return z
 
-        z_first = fetch_late(0, BANK, 0)
-        z_third = fetch_late(BANK, width, 8 * KIB)
-        weave(nc.scalar.copy, 0, z_first[:, :, 0:width])
-        weave(nc.scalar.copy, width, z_first[:, :, width:BANK])
-        z_last = fetch_late(starts[-1], width, 0)
-        weave(nc.scalar.copy, BANK, z_third[:])
-        for m0 in starts[:-1]:
-            finish(m0)
-        weave(nc.vector.tensor_copy, starts[-1], z_last[:])
-        cols = slice(starts[-1], PM)
-        for nt in range(4):
-            last_pass(open_acc[nt][:, :width], 1, nt, starts[-1], width)
-        for pair, copy in enumerate((nc.scalar.copy, nc.vector.tensor_copy)):
-            result = ring.tile([P, 2, width], F32, name="tail", bufs=2)
-            for i in range(2):
-                copy(out=result[:, i, :], in_=open_acc[2 * pair + i][:, :width])
-            nc.sync.dma_start(out=out_rows[:, 2 * pair : 2 * pair + 2, cols], in_=result[:])
+        def weave_chunk(c, z, copy):
+            interleave(copy, woven_late[c], z)
+
+        def quantize_z0(i):
+            quantize(woven_z[i][:], z0_w[i][:], z_s[0][:, QUARTER * i : QUARTER * (i + 1)])
+
+        def finish(c):
+            m0, width = chunks[c]
+            quantize(woven_late[c], z1_w[:, m0 : m0 + width], z_s[1][:, m0 : m0 + width])
+            last_passes(c, 1)
+            share = 4 // len(tags[c])
+            for b in range(len(tags[c])):
+                result = ring.tile([P, share, width], F32, name="result", tag="d", bufs=8, align_bytes=64)
+                copy = nc.vector.tensor_copy if (c, b) == (len(chunks) - 1, 1) else nc.scalar.copy
+                copy(out=result[:], in_=banks[c, b][:])
+                nc.sync.dma_start(out=out_rows[:, share * b : share * (b + 1), m0 : m0 + width], in_=result[:])
+
+        weave_chunk(0, fetch_chunk(0), nc.scalar.copy)
+        quantize(woven_w4[0][:], w4_w[0][:], w4_s[0][:])
+        quantize_z0(0)
+        last_passes(0, 0)
+        quantize(woven_w4[1][:], w4_w[1][:], w4_s[1][:])
+        finish(0)
+        weave_chunk(1, fetch_chunk(1), nc.scalar.copy)
+        for i in range(1, 4):
+            quantize_z0(i)
+            last_passes(i, 0)
+        last_passes(4, 0)
+        finish(1)
+        weave_chunk(2, fetch_chunk(2), nc.scalar.copy)
+        weave_chunk(3, fetch_chunk(3), nc.scalar.copy)
+        finish(2)
+        z = fetch_chunk(4)
+        finish(3)
+        weave_chunk(4, z, nc.vector.tensor_copy)
+        finish(4)

@@ -22,13 +22,14 @@ PACK = 4
 BANK = 512
 QUARTER = 256
 KIB = 1024
-AT_RAW = (106 * KIB, 82 * KIB)
+AT_RAW = (8 * KIB, 82 * KIB)
 AT_CTX = 90 * KIB
 AT_FIRST_WOVEN = 16 * KIB
 AT_FIRST_STATES = 24 * KIB
 AT_WEIGHTED = 26 * KIB
 AT_SECOND_WOVEN = 28 * KIB
-AT_LATE_WEIGHTED = 32 * KIB
+AT_LATE_WEIGHTED = 74 * KIB
+AT_ODD_WEIGHTED = 36 * KIB
 AT_Z0_WOVEN = 38 * KIB
 AT_W2_LATE = 46 * KIB
 AT_Z = 48 * KIB
@@ -53,24 +54,24 @@ def tile_list_byte_patch_slots_kernel(
         list2 = keep.tile([P, S // 16], U16, name="list2")
         list3 = keep.tile([P, PM // 16], U16, name="list3")
         tab_w = at(AT_TABLE, "tab_w", [P, T], I32)
-        tab_s = at(AT_CTX, "tab_s", [P, T], U8)
+        tab_s = keep.tile([P, T], U8, name="tab_s", align_bytes=64)
         v_w = [
             keep.tile([P, QUARTER], U32, name="v_w0", align_bytes=64),
-            at(AT_FIRST_WOVEN + 4 * KIB, "v_w1", [P, QUARTER], U32),
+            at(AT_FIRST_STATES, "v_w1", [P, QUARTER], U32),
             at(AT_FIRST_WOVEN + 5 * KIB, "v_w2", [P, QUARTER], U32),
-            at(AT_FIRST_STATES + KIB, "v_w3", [P, QUARTER], U32),
+            at(AT_FIRST_WOVEN + 4 * KIB, "v_w3", [P, QUARTER], U32),
         ]
         v_s = [
             keep.tile([P, QUARTER], U8, name="v_s0", align_bytes=64),
-            at(AT_FIRST_WOVEN + 6 * KIB, "v_s1", [P, QUARTER], U8),
+            at(AT_FIRST_STATES + KIB, "v_s1", [P, QUARTER], U8),
             at(AT_FIRST_WOVEN + 7 * KIB, "v_s2", [P, QUARTER], U8),
-            at(AT_FIRST_STATES, "v_s3", [P, QUARTER], U8),
+            at(AT_FIRST_WOVEN + 6 * KIB, "v_s3", [P, QUARTER], U8),
         ]
-        w1_w = keep.tile([P, 2 * H], U8, name="w1_w", align_bytes=64)
+        w1_w = [keep.tile([P, 2 * BANK], U8, name=f"w1_w{a}", align_bytes=64) for a in range(2)]
         w1_s = keep.tile([P, H], U8, name="w1_s", align_bytes=64)
-        w3_raw_w = [at(AT_RAW[1], "w3_raw_w0", [P, BANK], I32), at(8 * KIB, "w3_raw_w1", [P, BANK], I32)]
+        w3_raw_w = [at(AT_RAW[1], "w3_raw_w0", [P, BANK], I32), at(AT_RAW[1] + 2 * KIB, "w3_raw_w1", [P, BANK], I32)]
         w3_raw_s = at(AT_RAW[1] + 4 * KIB, "w3_raw_s", [P, H], U8)
-        w3_w = [at(AT_FIRST_WOVEN + 2 * KIB * a, f"w3_w{a}", [P, BANK], I32) for a in range(2)]
+        w3_w = [keep.tile([P, BANK], I32, name=f"w3_w{a}", align_bytes=64) for a in range(2)]
         w3_s = [keep.tile([P, BANK], U8, name=f"w3_s{a}", align_bytes=64) for a in range(2)]
         w2_w = [keep.tile([P, BANK], U32, name="w2_w0", align_bytes=64), at(AT_W2_LATE, "w2_w1", [P, BANK], U32)]
         w2_s = [keep.tile([P, BANK], U8, name=f"w2_s{a}", align_bytes=64) for a in range(2)]
@@ -82,8 +83,13 @@ def tile_list_byte_patch_slots_kernel(
         slot_w = {
             0: keep.tile([P, PACK, QUARTER], F32, name="slot_w0"),
             256: at(4 * KIB, "slot_w256", [P, PACK, QUARTER], F32),
-            512: at(AT_TABLE, "slot_w512", [P, PACK, BANK], F32),
+            512: keep.tile([P, PACK, BANK], F32, name="slot_w512"),
         }
+
+        def slot_weights(j0, width):
+            start = min(j0, BANK)
+            return slot_w[start][:, :, j0 - start : j0 - start + width]
+
         pages = [keep.tile([P, T2], F32, name=f"page{t}") for t in range(PACK)]
         ident = keep.tile([P, P], F32, name="ident")
 
@@ -93,9 +99,8 @@ def tile_list_byte_patch_slots_kernel(
 
         def load_slot_weights(j0):
             rows = wgs.rearrange("(m t) j -> m t j", t=PACK)
-            width = slot_w[j0].shape[2]
             for q in range(4):
-                nc.sync.dma_start(out=slot_w[j0][32 * q : 32 * q + 32, :, :], in_=rows[:, :, j0 : j0 + width])
+                nc.sync.dma_start(out=slot_weights(j0, QUARTER)[32 * q : 32 * q + 32], in_=rows[:, :, j0 : j0 + QUARTER])
 
         def load_weight(name, offset, rows):
             raw = at(offset, name, [P, PACK, rows.shape[1]], F32)
@@ -106,9 +111,13 @@ def tile_list_byte_patch_slots_kernel(
             words = w3_words[0].rearrange("p c i -> p (c i)").bitcast(I32)
             nc.sync.dma_start(out=w3_raw_w[a][:], in_=words[:, BANK * a : BANK * (a + 1)])
 
-        def load_ctx(a):
-            own = at(AT_CTX, f"own{a}", [P, PACK, PM], F32)
-            nc.sync.dma_start(out=own[:], in_=ctx[BANK * a : BANK * (a + 1), :].rearrange("(p t) m -> p t m", t=PACK))
+        def load_w1_words(a):
+            nc.sync.dma_start(out=w1_w[a][:].bitcast(I32), in_=w1_words[0, :, 2 * BANK * a : 2 * BANK * (a + 1)].bitcast(I32))
+
+        def load_ctx(a, half):
+            own = at(AT_CTX + 8 * KIB * half, f"own{a}_{half}", [P, 2, PM], F32)
+            rows = ctx[BANK * a : BANK * (a + 1), :].rearrange("(p t) m -> p t m", t=PACK)
+            nc.sync.dma_start(out=own[:], in_=rows[:, 2 * half : 2 * half + 2, :])
             return own
 
         def interleave(copy, woven, planes):
@@ -123,8 +132,7 @@ def tile_list_byte_patch_slots_kernel(
             nc.vector.tensor_copy(out=v_s[quarter][:], in_=tab_s[:].indirect(picks))
 
         def reorder_w3(a, t0, count):
-            cols = slice(BANK * a, BANK * (a + 1))
-            for dst, src in ((w3_w[a], w3_raw_w[a][:]), (w3_s[a], w3_raw_s[:, cols])):
+            for dst, src in ((w3_w[a], w3_raw_w[a][:]), (w3_s[a], w3_raw_s[:, BANK * a : BANK * (a + 1)])):
                 nc.gpsimd.tensor_copy(
                     out=dst[:].rearrange("p (t m) -> p t m", t=PACK)[:, t0 : t0 + count, :],
                     in_=src.rearrange("p (m t) -> p t m", t=PACK)[:, t0 : t0 + count, :],
@@ -149,7 +157,7 @@ def tile_list_byte_patch_slots_kernel(
 
         def first_product(e):
             a = e // (S // P)
-            words = w1_w[:, 2 * BANK * a : 2 * BANK * (a + 1)].bitcast(FP4X4)
+            words = w1_w[a][:].bitcast(FP4X4)
             by_slice = token_product(e, "first", words, w1_s[:, BANK * a : BANK * (a + 1)])
             relu_t[e] = ring.tile([P, PACK, P], F32, name="d", tag="d", bufs=8, align_bytes=64)
             nc.scalar.activation(out=relu_t[e][:], in_=by_slice, func=ACT.Relu)
@@ -164,11 +172,10 @@ def tile_list_byte_patch_slots_kernel(
             first_product(e)
             second_product(e)
 
-        def make_state(unit, weighted, h, third_size=None, tags=("third", "sum")):
+        def make_state(unit, weighted, h, third_size=None, bank=None):
             a, j0, width, t0, count = unit
             total = width * count
-            start = min(j0, BANK)
-            third = psum.tile([P, total], F32, name="third", tag=tags[0])
+            third = bank[:, 0:total] if bank else psum.tile([P, total], F32, name="third")[:]
             for i in range(total // QUARTER):
                 t, quarter = t0 + QUARTER * i // width, (j0 + QUARTER * i % width) // QUARTER
                 nc.tensor.matmul_mx(
@@ -180,23 +187,23 @@ def tile_list_byte_patch_slots_kernel(
                     start=True,
                     stop=True,
                 )
-            q = psum.tile([P, total], F32, name="q", tag=tags[1])
+            if third_size is None:
+                third_size = ring.tile([P, total], F32, name="third_size", bufs=3)[:]
+            nc.scalar.activation(out=third_size, in_=third, func=ACT.Abs)
+            q = bank[:, total : 2 * total] if bank else psum.tile([P, total], F32, name="q", tag="sum")[:]
             for i in range(total // P):
                 t, e = t0 + P * i // width, a * (S // P) + (j0 + P * i % width) // P
                 cols = slice(P * i, P * (i + 1))
                 nc.tensor.matmul(q[:, cols], lhsT=relu_t[e][:, t, :], rhs=ident[:], is_transpose=True, start=True, stop=False)
                 nc.tensor.matmul(q[:, cols], lhsT=second_t[e][:, t, :], rhs=ident[:], is_transpose=True, start=False, stop=True)
-            if third_size is None:
-                third_size = ring.tile([P, total], F32, name="third_size", bufs=3)[:]
-            nc.scalar.activation(out=third_size, in_=third[:], func=ACT.Abs)
             gate = ring.tile([P, total], F32, name="gate")
-            nc.scalar.activation(out=gate[:], in_=q[:], func=ACT.Silu)
+            nc.scalar.activation(out=gate[:], in_=q, func=ACT.Silu)
             gate_size = ring.tile([P, total], F32, name="gate_size", bufs=3)
             nc.scalar.activation(out=gate_size[:], in_=gate[:], func=ACT.Abs)
             nc.gpsimd.tensor_tensor(
                 out=weighted.rearrange("p (t j) -> p t j", j=width),
                 in0=third_size.rearrange("p (t j) -> p t j", j=width),
-                in1=slot_w[start][:, t0 : t0 + count, j0 - start : j0 - start + width],
+                in1=slot_weights(j0, width)[:, t0 : t0 + count, :],
                 op=ALU.mult,
             )
             nc.gpsimd.tensor_tensor(out=h, in0=weighted, in1=gate_size[:], op=ALU.mult)
@@ -213,7 +220,7 @@ def tile_list_byte_patch_slots_kernel(
             nc.vector.tensor_tensor(
                 out=z,
                 in0=pages[t][:].indirect(list3[:, m0 // 16 : (m0 + width) // 16]),
-                in1=own[:, t, m0 : m0 + width],
+                in1=own[t // 2][:, t % 2, m0 : m0 + width],
                 op=ALU.add,
             )
 
@@ -233,30 +240,34 @@ def tile_list_byte_patch_slots_kernel(
         warm = keep.tile([P, 1], F32, name="warm")
         nc.scalar.activation(out=warm[:], in_=ident[:, 0:1], func=ACT.Silu)
         nc.sync.dma_start(list1[:], offs)
-        load_scales(w1_s, w1_scales, (0, 1))
+        load_scales(w1_s, w1_scales)
+        load_scales(tab_s, tab_scales, (0, 1))
         nc.sync.dma_start(out=tab_w[:], in_=tab_words[0].rearrange("p c i -> p (c i)").bitcast(I32))
-        load_scales(tab_s, tab_scales)
-        load_scales(w1_s, w1_scales, (2, 3))
-        raw = at(0, "w2_raw", [P, 5, BANK], F32)[:, 0:PACK, :]
-        nc.sync.dma_start(out=raw, in_=w2[:, 0:BANK].rearrange("(p t) c -> p t c", t=PACK))
-        nc.sync.dma_start(out=w1_w[:].bitcast(I32), in_=w1_words[0].bitcast(I32))
-        load_w3_words(0)
+        load_scales(tab_s, tab_scales, (2, 3))
         load_scales(w3_raw_s, w3_scales)
+        raw = [load_weight("w2_raw0", 0, w2[:, 0:384])]
+        load_w1_words(0)
+        raw.append(load_weight("w2_raw1", 6 * KIB, w2[:, 384:BANK]))
+        load_w3_words(0)
+        load_w3_words(1)
         load_slot_weights(0)
         nc.sync.dma_start(list2[:], offs2)
         nc.sync.dma_start(list3[:], offs3)
 
         gather_table(0)
         woven = at(AT_FIRST_WOVEN, "w2_woven", [P, 2 * BANK, PACK], BF16)
-        for cols, copy in ((slice(0, 192), nc.scalar.copy), (slice(192, BANK), nc.vector.tensor_copy)):
-            interleave(copy, woven[:, cols, :], raw[:, :, cols])
-        quantize(woven[:, 0:BANK, :], w2_w[0][:], w2_s[0][:])
+        interleave(nc.scalar.copy, woven[:, 0:192, :], raw[0][:, :, 0:192])
+        interleave(nc.vector.tensor_copy, woven[:, 192:384, :], raw[0][:, :, 192:384])
+        interleave(nc.vector.tensor_copy, woven[:, 384:BANK, :], raw[1][:])
+        for c0 in (0, 256):
+            quantize(woven[:, c0 : c0 + 256, :], w2_w[0][:, c0 : c0 + 256], w2_s[0][:, c0 : c0 + 256])
         load_slot_weights(256)
-        load_w3_words(1)
+        load_w1_words(1)
         reorder_w3(0, 0, 2)
         reorder_w3(0, 2, 2)
-        gather_table(1)
+        reorder_w3(1, 0, PACK)
         gather_table(2)
+        gather_table(3)
         first_product(0)
         first_product(1)
         second_product(0)
@@ -267,66 +278,70 @@ def tile_list_byte_patch_slots_kernel(
                 interleave(nc.scalar.copy, woven[:, c0 : c0 + 256, :], raw[:, :, c0 : c0 + 256])
 
         singles = [(0, 0, QUARTER, t, 1) for t in range(2)]
-        states = [part_of(AT_FIRST_STATES + KIB * t, f"first_h{t}", 1, QUARTER) for t in range(2)]
+        states = [ring_state()[:, 0:QUARTER] for t in range(2)]
         for t in range(2):
-            make_state(singles[t], part_of(AT_WEIGHTED, f"first_weighted{t}", 2, QUARTER), states[t], tags=("first", "second"))
-        reorder_w3(1, 0, PACK)
-        raw_late = load_weight("w2_raw_late", AT_RAW[1], w2[:, BANK : 2 * BANK])
-        for t in range(2):
+            bank = psum.tile([P, BANK], F32, name="single", tag="sum")
+            third_size = part_of(AT_FIRST_STATES, "first_third_size", 2, QUARTER) if t == 0 else None
+            make_state(singles[t], part_of(AT_WEIGHTED + KIB * t, f"first_weighted{t}", 1, QUARTER), states[t], third_size, bank)
+            if t == 0:
+                gather_table(1)
             put_state(singles[t], states[t])
-        gather_table(3)
-        load_slot_weights(512)
-        own = load_ctx(0)
 
         pairs = [(a, j0, QUARTER, t0, 2) for a in range(2) for j0 in range(0, S, QUARTER) for t0 in (0, 2)]
         for u in range(1, 7):
             h = part_of(AT_W2_LATE, "h_before_w2", 2) if u == 5 else ring_state()
-            make_state(pairs[u], part_of(AT_WEIGHTED, f"weighted{u}", 2), h)
+            make_state(pairs[u], part_of(AT_ODD_WEIGHTED if u % 2 else AT_WEIGHTED, f"weighted{u}", 2), h)
             put_state(pairs[u], h)
             if u == 1:
+                load_slot_weights(512)
+                raw_late = load_weight("w2_raw_late", AT_RAW[0], w2[:, BANK : 2 * BANK])
+                raw_w4 = {1: load_weight("w4_raw1", AT_RAW[1], w4[BANK : 2 * BANK, :])}
+                own = [load_ctx(0, 0)]
+                load_slot_weights(768)
                 token_major(2)
-            if u < 6:
-                token_major(u + 2)
-            if u == 3:
+                token_major(3)
+            if u < 5:
+                token_major(u + 3)
+            if u == 5:
                 woven = at(AT_SECOND_WOVEN, "w2_woven_late", [P, BANK, PACK], BF16)
                 weave_halves(woven, raw_late)
-                raw_w4 = [load_weight(f"w4_raw{a}", (AT_RAW[1], 8 * KIB)[a], w4[BANK * a : BANK * (a + 1), :]) for a in range(2)]
+                raw_w4[0] = load_weight("w4_raw0", AT_RAW[0], w4[0:BANK, :])
+                own.append(load_ctx(0, 1))
             if u == 5:
                 quantize(woven[:], w2_w[1][:], w2_s[1][:])
         z0 = at(AT_Z, "z0", [P, PACK, PM], F32)
         h_last = ring_state()
-        make_state(pairs[7], part_of(AT_WEIGHTED, "weighted7", 6), h_last)
+        make_state(pairs[7], part_of(AT_WEIGHTED, "weighted7", 10), h_last)
         token_major(8)
         token_major(9)
         for t in (0, 1):
             fetch(z0[:, t, :], own, t, 0, PM)
         h = ring_state()
-        make_state(pairs[8], own[:, 1, 0:BANK], h)
+        make_state(pairs[9], own[0][:, 1, 0:BANK], h)
         put_state(pairs[7], h_last)
         for t in (2, 3):
             fetch(z0[:, t, :], own, t, 0, PM)
-        put_state(pairs[8], h)
+        put_state(pairs[9], h)
         token_major(10)
         token_major(11)
+        woven_w4 = [at(AT_SECOND_WOVEN + 4 * KIB * a, f"w4_woven{a}", [P, BANK, PACK], BF16) for a in range(2)]
+        weave_halves(woven_w4[1], raw_w4[1])
         h = ring_state()
-        make_state(pairs[9], own[:, 3, 0:BANK], h, part_of(AT_LATE_WEIGHTED, "third_size9", 6))
-        put_state(pairs[9], h)
-        own = load_ctx(1)
-        for e in range(12, 16):
-            token_major(e)
-        woven_w4 = [
-            at(AT_SECOND_WOVEN, "w4_woven0", [P, BANK, PACK], BF16),
-            at(AT_LATE_WEIGHTED + 2 * KIB, "w4_woven1", [P, BANK, PACK], BF16),
-        ]
+        make_state(pairs[8], own[1][:, 1, 0:BANK], h, part_of(AT_LATE_WEIGHTED, "third_size8", 4))
+        put_state(pairs[8], h)
+        own = [load_ctx(1, half) for half in range(2)]
+        weave_halves(woven_w4[0], raw_w4[0])
+        token_major(12)
+        token_major(13)
         late = pairs[10:12] + [(1, BANK, BANK, t, 1) for t in range(PACK)]
         woven_z = []
         for i, unit in enumerate(late):
             third_size = part_of(AT_Z0_WOVEN + 2 * KIB * i, f"late_third_size{i}", 2) if i < 4 else None
             h = part_of(AT_Z, "last_h", 25) if i == len(late) - 1 else ring_state()
-            make_state(unit, part_of(AT_LATE_WEIGHTED, f"late_weighted{i}", 2), h, third_size)
+            make_state(unit, part_of(AT_LATE_WEIGHTED + 2 * KIB * (i % 2), f"late_weighted{i}", 2), h, third_size)
             put_state(unit, h)
             if i < 2:
-                weave_halves(woven_w4[i], raw_w4[i])
+                token_major(14 + i)
             if i < 4:
                 woven_z.append(at(AT_Z0_WOVEN + 2 * KIB * i, f"z0_woven{i}", [P, QUARTER, PACK], BF16))
                 interleave(nc.scalar.copy, woven_z[i][:], z0[:, :, QUARTER * i : QUARTER * (i + 1)])

@@ -33,7 +33,9 @@ AT_ODD_WEIGHTED = 36 * KIB
 AT_Z0_WOVEN = 38 * KIB
 AT_W2_LATE = 46 * KIB
 AT_Z = 48 * KIB
-AT_LATE_CODES = 64 * KIB
+AT_LATE_CODES = 60 * KIB
+AT_Z0_CODES = 73 * KIB
+AT_W4_CODES = 69 * KIB
 AT_TABLE = 74 * KIB
 
 
@@ -75,9 +77,9 @@ def tile_list_byte_patch_slots_kernel(
         w3_s = [keep.tile([P, BANK], U8, name=f"w3_s{a}", align_bytes=64) for a in range(2)]
         w2_w = [keep.tile([P, BANK], U32, name="w2_w0", align_bytes=64), at(AT_W2_LATE, "w2_w1", [P, BANK], U32)]
         w2_s = [keep.tile([P, BANK], U8, name=f"w2_s{a}", align_bytes=64) for a in range(2)]
-        w4_w = [at(AT_LATE_CODES + 2 * KIB * a, f"w4_w{a}", [P, N], U32) for a in range(2)]
+        w4_w = [at(AT_W4_CODES + 2 * KIB * a, f"w4_w{a}", [P, N], U32) for a in range(2)]
         w4_s = [keep.tile([P, N], U8, name=f"w4_s{a}", align_bytes=64) for a in range(2)]
-        z0_w = [at(AT_LATE_CODES + (4, 6, 7, 8)[i] * KIB, f"z0_w{i}", [P, QUARTER], U32) for i in range(4)]
+        z0_w = [at((AT_Z0_CODES, AT_LATE_CODES + 4 * KIB, AT_LATE_CODES + 5 * KIB, AT_LATE_CODES + 6 * KIB)[i], f"z0_w{i}", [P, QUARTER], U32) for i in range(4)]
         z1_w = keep.tile([P, PM], U32, name="z1_w", align_bytes=64)
         z_s = [keep.tile([P, PM], U8, name=f"z_s{a}", align_bytes=64) for a in range(2)]
         slot_w = {
@@ -337,7 +339,7 @@ def tile_list_byte_patch_slots_kernel(
         woven_z = []
         for i, unit in enumerate(late):
             third_size = part_of(AT_Z0_WOVEN + 2 * KIB * i, f"late_third_size{i}", 2) if i < 4 else None
-            h = part_of(AT_Z, "last_h", 25) if i == len(late) - 1 else ring_state()
+            h = part_of(AT_Z, "last_h", 26) if i == len(late) - 1 else ring_state()
             make_state(unit, part_of(AT_LATE_WEIGHTED + 2 * KIB * (i % 2), f"late_weighted{i}", 2), h, third_size)
             put_state(unit, h)
             if i < 2:
@@ -371,11 +373,11 @@ def tile_list_byte_patch_slots_kernel(
 
         def fetch_chunk(c):
             m0, width = chunks[c]
-            z = at(AT_Z + (4 * KIB if c == 3 else 0), f"z1_{c}", [P, 6 if c == 1 else PACK, width], F32)[:, 0:PACK, :]
+            z = at(AT_Z + (0, 4, 8, 12, 8)[c] * KIB, f"z1_{c}", [P, PACK, width], F32)[:]
             for t in range(PACK):
                 fetch(z[:, t, :], own, t, m0, width)
             if c == 0:
-                woven_late[c] = at(AT_LATE_CODES + 6 * KIB, "z1_woven0", [P, 384, PACK], BF16)[:, 0:width, :]
+                woven_late[c] = at(AT_Z + 8 * KIB, "z1_woven0", [P, 11 * P, PACK], BF16)[:, 0:width, :]
             else:
                 woven_late[c] = ring.tile([P, width, PACK], BF16, name="z1_woven", tag="s2", bufs=8, align_bytes=64)[:]
             return z
@@ -397,13 +399,13 @@ def tile_list_byte_patch_slots_kernel(
                 copy(out=result[:], in_=banks[c, b][:])
                 nc.sync.dma_start(out=out_rows[:, share * b : share * (b + 1), m0 : m0 + width], in_=result[:])
 
-        weave_chunk(0, fetch_chunk(0), nc.scalar.copy)
+        for c in range(2):
+            weave_chunk(c, fetch_chunk(c), nc.scalar.copy)
         quantize(woven_w4[0][:], w4_w[0][:], w4_s[0][:])
         quantize_z0(0)
         last_passes(0, 0)
         quantize(woven_w4[1][:], w4_w[1][:], w4_s[1][:])
         finish(0)
-        weave_chunk(1, fetch_chunk(1), nc.scalar.copy)
         for i in range(1, 4):
             quantize_z0(i)
             last_passes(i, 0)

@@ -20,23 +20,19 @@ ACT = mybir.ActivationFunctionType
 P = 128
 PACK = 4
 BANK = 512
-QUARTER = 256
+GROUP = 256
 KIB = 1024
-AT_RAW = (8 * KIB, 82 * KIB)
-AT_CTX = 90 * KIB
-AT_FIRST_WOVEN = 16 * KIB
-AT_FIRST_STATES = 24 * KIB
-AT_WEIGHTED = 26 * KIB
-AT_SECOND_WOVEN = 28 * KIB
-AT_LATE_WEIGHTED = 74 * KIB
-AT_ODD_WEIGHTED = 36 * KIB
-AT_Z0_WOVEN = 38 * KIB
-AT_W2_LATE = 46 * KIB
-AT_Z = 48 * KIB
-AT_LATE_CODES = 60 * KIB
-AT_Z0_CODES = 73 * KIB
-AT_W4_CODES = 69 * KIB
-AT_TABLE = 74 * KIB
+AT_TABLE = 0
+AT_W2_RAW = 8 * KIB
+AT_W3_RAW = 68 * KIB
+AT_W2_WOVEN = 19 * KIB
+AT_RELU = 24 * KIB
+AT_SECOND = 32 * KIB
+AT_GATE = 40 * KIB
+AT_CTX = 48 * KIB
+AT_W2_LATE = 64 * KIB
+AT_W3_LATE = 72 * KIB
+AT_W2_RAW_LATE = 74 * KIB
 
 
 def tile_list_byte_patch_slots_kernel(
@@ -45,69 +41,52 @@ def tile_list_byte_patch_slots_kernel(
     nc = tc.nc
     with ExitStack() as stack:
         keep = stack.enter_context(tc.tile_pool(name="keep", bufs=1))
-        ring = stack.enter_context(tc.tile_pool(name="ring", bufs=2))
         shared = stack.enter_context(tc.tile_pool(name="shared", bufs=1))
-        psum = stack.enter_context(tc.psum_pool(name="psum", bufs=2))
+        psum = stack.enter_context(tc.psum_pool(name="psum", bufs=1))
 
         def at(offset, name, shape, dtype):
             return shared.tile(shape, dtype, name=name, align_bytes=64, offset=offset)
+
+        def kept(name, shape, dtype):
+            return keep.tile(shape, dtype, name=name, align_bytes=64)
+
+        def in_bank(b, shape):
+            return psum.tile(shape, F32, name="bank", tag=f"bank{b}")
 
         list1 = keep.tile([P, S // 16], U16, name="list1")
         list2 = keep.tile([P, S // 16], U16, name="list2")
         list3 = keep.tile([P, PM // 16], U16, name="list3")
         tab_w = at(AT_TABLE, "tab_w", [P, T], I32)
-        tab_s = keep.tile([P, T], U8, name="tab_s", align_bytes=64)
-        v_w = [
-            keep.tile([P, QUARTER], U32, name="v_w0", align_bytes=64),
-            at(AT_FIRST_STATES, "v_w1", [P, QUARTER], U32),
-            at(AT_FIRST_WOVEN + 5 * KIB, "v_w2", [P, QUARTER], U32),
-            at(AT_FIRST_WOVEN + 4 * KIB, "v_w3", [P, QUARTER], U32),
-        ]
-        v_s = [
-            keep.tile([P, QUARTER], U8, name="v_s0", align_bytes=64),
-            at(AT_FIRST_STATES + KIB, "v_s1", [P, QUARTER], U8),
-            at(AT_FIRST_WOVEN + 7 * KIB, "v_s2", [P, QUARTER], U8),
-            at(AT_FIRST_WOVEN + 6 * KIB, "v_s3", [P, QUARTER], U8),
-        ]
-        w1_w = [keep.tile([P, 2 * BANK], U8, name=f"w1_w{a}", align_bytes=64) for a in range(2)]
-        w1_s = keep.tile([P, H], U8, name="w1_s", align_bytes=64)
-        w3_raw_w = [at(AT_RAW[1], "w3_raw_w0", [P, BANK], I32), at(AT_RAW[1] + 2 * KIB, "w3_raw_w1", [P, BANK], I32)]
-        w3_raw_s = at(AT_RAW[1] + 4 * KIB, "w3_raw_s", [P, H], U8)
-        w3_w = [keep.tile([P, BANK], I32, name=f"w3_w{a}", align_bytes=64) for a in range(2)]
-        w3_s = [keep.tile([P, BANK], U8, name=f"w3_s{a}", align_bytes=64) for a in range(2)]
-        w2_w = [keep.tile([P, BANK], U32, name="w2_w0", align_bytes=64), at(AT_W2_LATE, "w2_w1", [P, BANK], U32)]
-        w2_s = [keep.tile([P, BANK], U8, name=f"w2_s{a}", align_bytes=64) for a in range(2)]
-        w4_w = [at(AT_W4_CODES + 2 * KIB * a, f"w4_w{a}", [P, N], U32) for a in range(2)]
-        w4_s = [keep.tile([P, N], U8, name=f"w4_s{a}", align_bytes=64) for a in range(2)]
-        z0_w = [at((AT_Z0_CODES, AT_LATE_CODES + 4 * KIB, AT_LATE_CODES + 5 * KIB, AT_LATE_CODES + 6 * KIB)[i], f"z0_w{i}", [P, QUARTER], U32) for i in range(4)]
-        z1_w = keep.tile([P, PM], U32, name="z1_w", align_bytes=64)
-        z_s = [keep.tile([P, PM], U8, name=f"z_s{a}", align_bytes=64) for a in range(2)]
-        slot_w = {
-            0: keep.tile([P, PACK, QUARTER], F32, name="slot_w0"),
-            256: at(4 * KIB, "slot_w256", [P, PACK, QUARTER], F32),
-            512: keep.tile([P, PACK, BANK], F32, name="slot_w512"),
-        }
+        tab_s = kept("tab_s", [P, T], U8)
+        w1_w = [kept(f"w1_w{a}", [P, 2 * BANK], U8) for a in range(2)]
+        w1_s = kept("w1_s", [P, H], U8)
+        w3_raw_w = [at(AT_W3_RAW, "w3_raw_w0", [P, BANK], I32), kept("w3_raw_w1", [P, BANK], I32)]
+        w3_raw_s = kept("w3_raw_s", [P, H], U8)
+        w2_w = [kept(f"w2_w{a}", [P, BANK], U32) for a in range(2)]
+        w2_s = [kept(f"w2_s{a}", [P, BANK], U8) for a in range(2)]
+        w4_w = kept("w4_w", [P, 2 * N], U32)
+        w4_s = kept("w4_s", [P, 2 * N], U8)
+        z_w = [kept(f"z_w{a}", [P, PM], U32) for a in range(2)]
+        z_s = [kept(f"z_s{a}", [P, PM], U8) for a in range(2)]
+        slot_w = {j0: kept(f"slot_w{j0}", [P, PACK, width], F32) for j0, width in ((0, 256), (256, 256), (512, 512))}
+        states = [kept(f"states{a}", [P, PACK * S], F32) for a in range(2)]
+        late_ctx = kept("late_ctx", [P, PACK, PM], F32)
+        pages = [kept(f"page{t}", [P, T2], F32) for t in range(PACK)]
+        ident = kept("ident", [P, P], F32)
 
-        def slot_weights(j0, width):
-            start = min(j0, BANK)
-            return slot_w[start][:, :, j0 - start : j0 - start + width]
-
-        pages = [keep.tile([P, T2], F32, name=f"page{t}") for t in range(PACK)]
-        ident = keep.tile([P, P], F32, name="ident")
-
-        def load_scales(plane, rows, quadrants=range(4)):
+        def load_scales(plane, rows, quadrants):
             for q in quadrants:
                 nc.sync.dma_start(out=plane[32 * q : 32 * q + 4, :].bitcast(I32), in_=rows[0, 4 * q : 4 * q + 4, :].bitcast(I32))
 
         def load_slot_weights(j0):
             rows = wgs.rearrange("(m t) j -> m t j", t=PACK)
+            width = slot_w[j0].shape[2]
             for q in range(4):
-                nc.sync.dma_start(out=slot_weights(j0, QUARTER)[32 * q : 32 * q + 32], in_=rows[:, :, j0 : j0 + QUARTER])
+                nc.sync.dma_start(out=slot_w[j0][32 * q : 32 * q + 32], in_=rows[:, :, j0 : j0 + width])
 
-        def load_weight(name, offset, rows):
-            raw = at(offset, name, [P, PACK, rows.shape[1]], F32)
-            nc.sync.dma_start(out=raw[:], in_=rows.rearrange("(p t) c -> p t c", t=PACK))
-            return raw
+        def load_rows(tile, rows):
+            nc.sync.dma_start(out=tile[:], in_=rows.rearrange("(p t) c -> p t c", t=PACK))
+            return tile
 
         def load_w3_words(a):
             words = w3_words[0].rearrange("p c i -> p (c i)").bitcast(I32)
@@ -116,302 +95,272 @@ def tile_list_byte_patch_slots_kernel(
         def load_w1_words(a):
             nc.sync.dma_start(out=w1_w[a][:].bitcast(I32), in_=w1_words[0, :, 2 * BANK * a : 2 * BANK * (a + 1)].bitcast(I32))
 
-        def load_ctx(a, half):
-            own = at(AT_CTX + 8 * KIB * half, f"own{a}_{half}", [P, 2, PM], F32)
-            rows = ctx[BANK * a : BANK * (a + 1), :].rearrange("(p t) m -> p t m", t=PACK)
-            nc.sync.dma_start(out=own[:], in_=rows[:, 2 * half : 2 * half + 2, :])
-            return own
-
         def interleave(copy, woven, planes):
             copy(out=woven.rearrange("p (c i) t -> p c t i", i=4), in_=planes.rearrange("p t (c i) -> p c t i", i=4))
+
+        def weave_on_scalar(woven, planes):
+            for c0 in range(0, woven.shape[1], GROUP):
+                interleave(nc.scalar.copy, woven[:, c0 : c0 + GROUP, :], planes[:, :, c0 : c0 + GROUP])
 
         def quantize(woven, words, scales):
             nc.vector.quantize_mx(out=words.bitcast(FP8X4), scales=scales, in_=woven.rearrange("p c t -> p (c t)"))
 
-        def gather_table(quarter):
-            picks = list1[:, 16 * quarter : 16 * (quarter + 1)]
-            nc.vector.tensor_copy(out=v_w[quarter][:], in_=tab_w[:].bitcast(U32).indirect(picks))
-            nc.vector.tensor_copy(out=v_s[quarter][:], in_=tab_s[:].indirect(picks))
+        v_w, v_s = {}, {}
 
-        def reorder_w3(a, t0, count):
-            for dst, src in ((w3_w[a], w3_raw_w[a][:]), (w3_s[a], w3_raw_s[:, BANK * a : BANK * (a + 1)])):
-                nc.gpsimd.tensor_copy(
-                    out=dst[:].rearrange("p (t m) -> p t m", t=PACK)[:, t0 : t0 + count, :],
-                    in_=src.rearrange("p (m t) -> p t m", t=PACK)[:, t0 : t0 + count, :],
-                )
+        def gather_table(j0, words, scales):
+            width = words.shape[1]
+            picks = list1[:, j0 // 16 : (j0 + width) // 16]
+            nc.vector.tensor_copy(out=words[:], in_=tab_w[:].bitcast(U32).indirect(picks))
+            nc.vector.tensor_copy(out=scales[:], in_=tab_s[:].indirect(picks))
+            for c0 in range(0, width, GROUP):
+                v_w[(j0 + c0) // GROUP] = words[:, c0 : c0 + GROUP]
+                v_s[(j0 + c0) // GROUP] = scales[:, c0 : c0 + GROUP]
 
-        relu_t, second_t = {}, {}
+        def deal_words(copy, dealt, raw):
+            copy(out=dealt.rearrange("p (t c i) -> p c t i", t=PACK, i=4), in_=raw.rearrange("p (c i t) -> p c t i", t=PACK, i=4))
 
-        def token_product(e, tag, words, scales):
-            jt = e % (S // P)
-            cols = slice(P * (jt % 2), P * (jt % 2 + 1))
-            bank = psum.tile([P, BANK], F32, name="bank", tag=tag)
+        relu_t, second_t, second_bank = {}, {}, {}
+
+        def token_product(e, bank, words, scales):
+            g, cols = e % 8 // 2, slice(P * (e % 2), P * (e % 2 + 1))
+            acc = in_bank(bank, [P, BANK])
             nc.tensor.matmul_mx(
-                out=bank[:],
-                lhsT=v_w[jt // 2][:, cols].bitcast(FP8X4),
-                lhsT_scale=v_s[jt // 2][:, cols],
+                out=acc[:],
+                lhsT=v_w[g][:, cols].bitcast(FP8X4),
+                lhsT_scale=v_s[g][:, cols],
                 rhs=words,
                 rhs_scale=scales,
                 start=True,
                 stop=True,
             )
-            return bank[:].rearrange("j (m t) -> j t m", t=PACK)
+            return acc[:].rearrange("j (m t) -> j t m", t=PACK)
 
         def first_product(e):
-            a = e // (S // P)
-            words = w1_w[a][:].bitcast(FP4X4)
-            by_slice = token_product(e, "first", words, w1_s[:, BANK * a : BANK * (a + 1)])
-            relu_t[e] = ring.tile([P, PACK, P], F32, name="d", tag="d", bufs=8, align_bytes=64)
+            a = e // 8
+            by_slice = token_product(e, e % 2, w1_w[a][:].bitcast(FP4X4), w1_s[:, BANK * a : BANK * (a + 1)])
+            relu_t[e] = at((AT_W2_RAW - 4 * KIB if e in (2, 3) else AT_RELU) + 2 * KIB * (e % 4), f"relu{e}", [P, PACK, P], F32)
             nc.scalar.activation(out=relu_t[e][:], in_=by_slice, func=ACT.Relu)
 
         def second_product(e):
-            a = e // (S // P)
-            by_slice = token_product(e, "second", w2_w[a][:].bitcast(FP8X4), w2_s[a][:])
-            second_t[e] = ring.tile([P, PACK, P], F32, name="s2", tag="s2", bufs=8, align_bytes=64)
-            nc.scalar.copy(out=second_t[e][:], in_=by_slice)
+            a = e // 8
+            second_bank[e] = token_product(e, (2, 6)[a] + e % 2, w2_w[a][:].bitcast(FP8X4), w2_s[a][:])
 
-        def token_major(e):
-            first_product(e)
-            second_product(e)
+        def empty_second(e, t0, count, offset):
+            part = at(offset, f"second{e}_{t0}", [P, count, P], F32)
+            nc.scalar.copy(out=part[:], in_=second_bank[e][:, t0 : t0 + count, :])
+            for i in range(count):
+                second_t[e, t0 + i] = part[:, i, :]
 
-        def make_state(unit, weighted, h, third_size=None, bank=None):
-            a, j0, width, t0, count = unit
-            total = width * count
-            third = bank[:, 0:total] if bank else psum.tile([P, total], F32, name="third")[:]
-            for i in range(total // QUARTER):
-                t, quarter = t0 + QUARTER * i // width, (j0 + QUARTER * i % width) // QUARTER
+        def state_of(g, t0, count):
+            start = PACK * GROUP * (g % 4) + GROUP * t0
+            return states[g // 4][:, start : start + GROUP * count]
+
+        def weigh_third(g, t0, count, bank):
+            a, j0 = g // 4, GROUP * (g % 4)
+            third = in_bank(bank, [P, GROUP * count])
+            for i in range(count):
+                cols = slice(P * (t0 + i), P * (t0 + i + 1))
                 nc.tensor.matmul_mx(
-                    out=third[:, QUARTER * i : QUARTER * (i + 1)],
-                    lhsT=w3_w[a][:, P * t : P * (t + 1)].bitcast(FP8X4),
-                    lhsT_scale=w3_s[a][:, P * t : P * (t + 1)],
-                    rhs=v_w[quarter][:].bitcast(FP8X4),
-                    rhs_scale=v_s[quarter][:],
+                    out=third[:, GROUP * i : GROUP * (i + 1)],
+                    lhsT=w3_w[a][:, cols].bitcast(FP8X4),
+                    lhsT_scale=w3_s[:, a, cols],
+                    rhs=v_w[g % 4].bitcast(FP8X4),
+                    rhs_scale=v_s[g % 4],
                     start=True,
                     stop=True,
                 )
-            if third_size is None:
-                third_size = ring.tile([P, total], F32, name="third_size", bufs=3)[:]
-            nc.scalar.activation(out=third_size, in_=third, func=ACT.Abs)
-            q = bank[:, total : 2 * total] if bank else psum.tile([P, total], F32, name="q", tag="sum")[:]
-            for i in range(total // P):
-                t, e = t0 + P * i // width, a * (S // P) + (j0 + P * i % width) // P
-                cols = slice(P * i, P * (i + 1))
+            h = state_of(g, t0, count)
+            nc.scalar.activation(out=h, in_=third[:], func=ACT.Abs)
+            start = min(j0, BANK)
+            by_slice = h.rearrange("p (t j) -> p t j", j=GROUP)
+            weights = slot_w[start][:, t0 : t0 + count, j0 - start : j0 - start + GROUP]
+            nc.gpsimd.tensor_tensor(out=by_slice, in0=by_slice, in1=weights, op=ALU.mult)
+
+        def gate_state(g, t0, count, bank, gate_at):
+            q = in_bank(bank, [P, GROUP * count])
+            for i in range(2 * count):
+                t, e, cols = t0 + i // 2, 2 * g + i % 2, slice(P * i, P * (i + 1))
                 nc.tensor.matmul(q[:, cols], lhsT=relu_t[e][:, t, :], rhs=ident[:], is_transpose=True, start=True, stop=False)
-                nc.tensor.matmul(q[:, cols], lhsT=second_t[e][:, t, :], rhs=ident[:], is_transpose=True, start=False, stop=True)
-            gate = ring.tile([P, total], F32, name="gate")
-            nc.scalar.activation(out=gate[:], in_=q, func=ACT.Silu)
-            gate_size = ring.tile([P, total], F32, name="gate_size", bufs=3)
-            nc.scalar.activation(out=gate_size[:], in_=gate[:], func=ACT.Abs)
-            nc.gpsimd.tensor_tensor(
-                out=weighted.rearrange("p (t j) -> p t j", j=width),
-                in0=third_size.rearrange("p (t j) -> p t j", j=width),
-                in1=slot_weights(j0, width)[:, t0 : t0 + count, :],
-                op=ALU.mult,
-            )
-            nc.gpsimd.tensor_tensor(out=h, in0=weighted, in1=gate_size[:], op=ALU.mult)
+                nc.tensor.matmul(q[:, cols], lhsT=second_t[e, t], rhs=ident[:], is_transpose=True, start=False, stop=True)
+            gate = at(gate_at, f"gate{g}_{t0}", [P, GROUP * count], F32)
+            nc.scalar.activation(out=gate[:], in_=q[:], func=ACT.Silu)
+            nc.scalar.activation(out=gate[:], in_=gate[:], func=ACT.Abs)
+            h = state_of(g, t0, count)
+            nc.gpsimd.tensor_tensor(out=h, in0=h, in1=gate[:], op=ALU.mult)
 
-        def put_state(unit, h):
-            a, j0, width, t0, count = unit
-            for i in range(count):
-                nc.vector.tensor_copy(
-                    out=pages[t0 + i][:].indirect(list2[:, j0 // 16 : (j0 + width) // 16]),
-                    in_=h[:, i * width : (i + 1) * width],
-                )
+        def put_state(g, t0, count):
+            picks = list2[:, GROUP * (g % 4) // 16 : GROUP * (g % 4 + 1) // 16]
+            for t in range(t0, t0 + count):
+                nc.vector.tensor_copy(out=pages[t][:].indirect(picks), in_=state_of(g, t, 1))
 
-        def fetch(z, own, t, m0, width):
-            nc.vector.tensor_tensor(
-                out=z,
-                in0=pages[t][:].indirect(list3[:, m0 // 16 : (m0 + width) // 16]),
-                in1=own[t // 2][:, t % 2, m0 : m0 + width],
-                op=ALU.add,
-            )
-
-        def part_of(offset, name, kib, columns=BANK):
-            return at(offset, name, [P, kib * KIB // 4], F32)[:, 0:columns]
-
-        def ring_state():
-            return ring.tile([P, BANK], F32, name="h", bufs=3)[:]
-
-        out_rows = out.rearrange("(nt p) m -> p nt m", p=P)
-
-        for plane in (tab_s, w3_raw_s):
-            nc.gpsimd.memset(plane[:].bitcast(I32), 0)
+        nc.gpsimd.memset(tab_s[:].bitcast(I32), 0)
+        nc.gpsimd.memset(w3_raw_s[:].bitcast(I32), 0)
         make_identity(nc, ident[:])
-        for t in range(PACK):
-            (nc.vector if t < 2 else nc.gpsimd).memset(pages[t][:].bitcast(I32), 0)
-        warm = keep.tile([P, 1], F32, name="warm")
-        nc.scalar.activation(out=warm[:], in_=ident[:, 0:1], func=ACT.Silu)
+        warm = keep.tile([P, 2], F32, name="warm")
+        nc.vector.memset(warm[:, 0:1], 0.0)
+        nc.scalar.activation(out=warm[:, 1:2], in_=warm[:, 0:1], func=ACT.Silu)
+        for t in range(2):
+            nc.vector.memset(pages[t][:, 0 : S - 1].bitcast(I32), 0)
+            nc.vector.memset(pages[t][:, S - 1 : T2].bitcast(I32), 0)
+        for t in range(2, PACK):
+            nc.gpsimd.memset(pages[t][:].bitcast(I32), 0)
         nc.sync.dma_start(list1[:], offs)
-        load_scales(w1_s, w1_scales)
-        load_scales(tab_s, tab_scales, (0, 1))
+        load_scales(w1_s, w1_scales, range(4))
         nc.sync.dma_start(out=tab_w[:], in_=tab_words[0].rearrange("p c i -> p (c i)").bitcast(I32))
-        load_scales(tab_s, tab_scales, (2, 3))
-        load_scales(w3_raw_s, w3_scales)
-        raw = [load_weight("w2_raw0", 0, w2[:, 0:384])]
         load_w1_words(0)
-        raw.append(load_weight("w2_raw1", 6 * KIB, w2[:, 384:BANK]))
-        load_w3_words(0)
-        load_w3_words(1)
-        load_slot_weights(0)
         nc.sync.dma_start(list2[:], offs2)
-        nc.sync.dma_start(list3[:], offs3)
-
-        gather_table(0)
-        woven = at(AT_FIRST_WOVEN, "w2_woven", [P, 2 * BANK, PACK], BF16)
-        interleave(nc.scalar.copy, woven[:, 0:192, :], raw[0][:, :, 0:192])
-        interleave(nc.vector.tensor_copy, woven[:, 192:384, :], raw[0][:, :, 192:384])
-        interleave(nc.vector.tensor_copy, woven[:, 384:BANK, :], raw[1][:])
-        for c0 in (0, 256):
-            quantize(woven[:, c0 : c0 + 256, :], w2_w[0][:, c0 : c0 + 256], w2_s[0][:, c0 : c0 + 256])
+        load_scales(tab_s, tab_scales, range(4))
+        raw = [load_rows(at(AT_W2_RAW, "w2_raw0", [P, PACK, 384], F32), w2[:, 0:384])]
+        raw.append(load_rows(at(AT_W2_RAW + 6 * KIB, "w2_raw1", [P, PACK, P], F32), w2[:, 384:BANK]))
+        load_scales(w3_raw_s, w3_scales, range(4))
+        load_w3_words(0)
+        load_slot_weights(0)
         load_slot_weights(256)
         load_w1_words(1)
-        reorder_w3(0, 0, 2)
-        reorder_w3(0, 2, 2)
-        reorder_w3(1, 0, PACK)
-        gather_table(2)
-        gather_table(3)
+
+        gather_table(0, kept("v_w0", [P, GROUP], U32), kept("v_s0", [P, GROUP], U8))
         first_product(0)
         first_product(1)
+        gather_table(GROUP, kept("v_w1", [P, GROUP], U32), kept("v_s1", [P, GROUP], U8))
+        woven = at(AT_W2_WOVEN, "w2_woven", [P, BANK, PACK], BF16)
+        interleave(nc.scalar.copy, woven[:, 0:P, :], raw[0][:, :, 0:P])
+        interleave(nc.vector.tensor_copy, woven[:, P:384, :], raw[0][:, :, P:384])
+        interleave(nc.vector.tensor_copy, woven[:, 384:BANK, :], raw[1][:])
+        first_product(2)
+        first_product(3)
+        quantize(woven[:], w2_w[0][:], w2_s[0][:])
+        raw_late = load_rows(at(AT_W2_RAW_LATE, "w2_raw_late", [P, PACK, BANK], F32), w2[:, BANK : 2 * BANK])
+        load_slot_weights(512)
+        load_w3_words(1)
+        nc.sync.dma_start(list3[:], offs3)
+        load_rows(late_ctx, ctx[BANK : 2 * BANK, :])
+
+        w3_s = at(AT_W2_WOVEN + KIB, "w3_s", [P, 2, BANK], U8)
+        nc.vector.tensor_copy(
+            out=w3_s[:].rearrange("p a (t m) -> p a t m", t=PACK),
+            in_=w3_raw_s[:].rearrange("p (a m t) -> p a t m", a=2, t=PACK),
+        )
+        w3_w = [at(AT_W2_WOVEN - KIB, "w3_w0", [P, BANK], I32)]
+        deal_words(nc.vector.tensor_copy, w3_w[0][:], w3_raw_w[0][:])
+        gather_table(2 * GROUP, at(AT_W3_RAW + 3 * BANK, "v_w2", [P, BANK], U32), at(AT_W3_RAW + KIB, "v_s2", [P, BANK], U8))
+        raw_w4 = [load_rows(at(AT_TABLE, "w4_raw0", [P, PACK, N], F32), w4[0:BANK, :])]
+
         second_product(0)
         second_product(1)
+        firsts = (
+            (0, 1, 4, 4, (AT_SECOND + BANK, AT_SECOND + KIB)),
+            (1, 1, 5, 0, (AT_W3_RAW, AT_W3_RAW + BANK)),
+            (2, 2, 6, 1, (AT_SECOND, AT_SECOND + KIB)),
+        )
+        for i, (t0, count, third_bank, sum_bank, offset) in enumerate(firsts):
+            weigh_third(0, t0, count, third_bank)
+            empty_second(0, t0, count, offset[0])
+            empty_second(1, t0, count, offset[1])
+            gate_state(0, t0, count, sum_bank, AT_GATE + 2 * KIB * i)
+            put_state(0, t0, count)
 
-        def weave_halves(woven, raw):
-            for c0 in (0, 256):
-                interleave(nc.scalar.copy, woven[:, c0 : c0 + 256, :], raw[:, :, c0 : c0 + 256])
-
-        singles = [(0, 0, QUARTER, t, 1) for t in range(2)]
-        states = [ring_state()[:, 0:QUARTER] for t in range(2)]
-        for t in range(2):
-            bank = psum.tile([P, BANK], F32, name="single", tag="sum")
-            third_size = part_of(AT_FIRST_STATES, "first_third_size", 2, QUARTER) if t == 0 else None
-            make_state(singles[t], part_of(AT_WEIGHTED + KIB * t, f"first_weighted{t}", 1, QUARTER), states[t], third_size, bank)
-            if t == 0:
-                gather_table(1)
-            put_state(singles[t], states[t])
-
-        pairs = [(a, j0, QUARTER, t0, 2) for a in range(2) for j0 in range(0, S, QUARTER) for t0 in (0, 2)]
-        for u in range(1, 7):
-            h = part_of(AT_W2_LATE, "h_before_w2", 2) if u == 5 else ring_state()
-            make_state(pairs[u], part_of(AT_ODD_WEIGHTED if u % 2 else AT_WEIGHTED, f"weighted{u}", 2), h)
-            put_state(pairs[u], h)
-            if u == 1:
-                load_slot_weights(512)
-                raw_late = load_weight("w2_raw_late", AT_RAW[0], w2[:, BANK : 2 * BANK])
-                raw_w4 = {1: load_weight("w4_raw1", AT_RAW[1], w4[BANK : 2 * BANK, :])}
-                own = [load_ctx(0, 0)]
-                load_slot_weights(768)
-                token_major(2)
-                token_major(3)
-            if u < 5:
-                token_major(u + 3)
-            if u == 5:
-                woven = at(AT_SECOND_WOVEN, "w2_woven_late", [P, BANK, PACK], BF16)
-                weave_halves(woven, raw_late)
-                raw_w4[0] = load_weight("w4_raw0", AT_RAW[0], w4[0:BANK, :])
-                own.append(load_ctx(0, 1))
-            if u == 5:
+        picked = states[0][:].rearrange("p (t m) -> p t m", t=PACK)
+        early_ctx = []
+        for g in range(1, 8):
+            for e in (2 * g, 2 * g + 1):
+                if g > 1:
+                    first_product(e)
+            for e in (2 * g, 2 * g + 1):
+                second_product(e)
+                empty_second(e, 0, PACK, AT_W2_LATE if e == 5 else AT_SECOND + 2 * KIB * (e % 4))
+            for half in range(2):
+                weigh_third(g, 2 * half, 2, 4 + half)
+            for half in range(2):
+                gate_at = AT_GATE + 2 * KIB * ((2 * g + half + 1) % 4)
+                if (g, half) == (1, 0):
+                    gate_at = AT_W3_LATE
+                if half == 1 and g in (5, 6):
+                    gate_at = AT_CTX + 8 * KIB * (g - 5) + 3 * KIB
+                gate_state(g, 2 * half, 2, (6, 2)[g // 4] + half, gate_at)
+                put_state(g, 2 * half, 2)
+                if g == 3:
+                    for t in (2 * half, 2 * half + 1):
+                        nc.vector.tensor_copy(out=picked[:, t, :], in_=pages[t][:].indirect(list3[:]))
+            if g == 1:
+                w3_w.append(at(AT_W3_LATE, "w3_w1", [P, BANK], I32))
+                deal_words(nc.gpsimd.tensor_copy, w3_w[1][:], w3_raw_w[1][:])
+            if g == 2:
+                woven = at(AT_W2_LATE, "w2_woven_late", [P, BANK, PACK], BF16)
+                weave_on_scalar(woven[:], raw_late[:])
                 quantize(woven[:], w2_w[1][:], w2_s[1][:])
-        z0 = at(AT_Z, "z0", [P, PACK, PM], F32)
-        h_last = ring_state()
-        make_state(pairs[7], part_of(AT_WEIGHTED, "weighted7", 10), h_last)
-        token_major(8)
-        token_major(9)
-        for t in (0, 1):
-            fetch(z0[:, t, :], own, t, 0, PM)
-        h = ring_state()
-        make_state(pairs[9], own[0][:, 1, 0:BANK], h)
-        put_state(pairs[7], h_last)
-        for t in (2, 3):
-            fetch(z0[:, t, :], own, t, 0, PM)
-        put_state(pairs[9], h)
-        token_major(10)
-        token_major(11)
-        woven_w4 = [at(AT_SECOND_WOVEN + 4 * KIB * a, f"w4_woven{a}", [P, BANK, PACK], BF16) for a in range(2)]
-        weave_halves(woven_w4[1], raw_w4[1])
-        h = ring_state()
-        make_state(pairs[8], own[1][:, 1, 0:BANK], h, part_of(AT_LATE_WEIGHTED, "third_size8", 4))
-        put_state(pairs[8], h)
-        own = [load_ctx(1, half) for half in range(2)]
-        weave_halves(woven_w4[0], raw_w4[0])
-        token_major(12)
-        token_major(13)
-        late = pairs[10:12] + [(1, BANK, BANK, t, 1) for t in range(PACK)]
-        woven_z = []
-        for i, unit in enumerate(late):
-            third_size = part_of(AT_Z0_WOVEN + 2 * KIB * i, f"late_third_size{i}", 2) if i < 4 else None
-            h = part_of(AT_Z, "last_h", 26) if i == len(late) - 1 else ring_state()
-            make_state(unit, part_of(AT_LATE_WEIGHTED + 2 * KIB * (i % 2), f"late_weighted{i}", 2), h, third_size)
-            put_state(unit, h)
-            if i < 2:
-                token_major(14 + i)
-            if i < 4:
-                woven_z.append(at(AT_Z0_WOVEN + 2 * KIB * i, f"z0_woven{i}", [P, QUARTER, PACK], BF16))
-                interleave(nc.scalar.copy, woven_z[i][:], z0[:, :, QUARTER * i : QUARTER * (i + 1)])
+                raw_w4.append(load_rows(at(AT_W2_RAW, "w4_raw1", [P, PACK, N], F32), w4[BANK : 2 * BANK, :]))
+            if g in (5, 6):
+                for c in (2 * (g - 5), 2 * (g - 5) + 1):
+                    own = at(AT_CTX + 4 * KIB * c, f"early_ctx{c}", [P, PACK, GROUP], F32)
+                    early_ctx.append(load_rows(own, ctx[0:BANK, GROUP * c : GROUP * (c + 1)]))
+
+        woven_z = at(AT_RELU, "z0_woven", [P, PM, PACK], BF16)
+        for c in range(4):
+            cols = slice(GROUP * c, GROUP * (c + 1))
+            nc.gpsimd.tensor_tensor(out=picked[:, :, cols], in0=picked[:, :, cols], in1=early_ctx[c][:], op=ALU.add)
+            interleave(nc.scalar.copy, woven_z[:, cols, :], picked[:, :, cols])
+        woven_w4 = at(AT_SECOND, "w4_woven", [P, 2 * N, PACK], BF16)
+        for a in range(2):
+            weave_on_scalar(woven_w4[:, N * a : N * (a + 1), :], raw_w4[a][:])
+        quantize(woven_w4[:], w4_w[:], w4_s[:])
+        quantize(woven_z[:], z_w[0][:], z_s[0][:])
 
         chunks = ((0, 256), (256, 256), (512, 256), (768, 128), (896, 128))
-        tags = (("first", "second"), ("first", "second"), ("sum", "third"), ("sum",), ("third", "first"))
-        banks, woven_late = {}, {}
+        chunk_banks = ((0, 1), (4, 5), (6, 7), (2,), (3, 0))
+        out_rows = out.rearrange("(nt p) m -> p nt m", p=P)
+        sums, woven_late = {}, {}
 
-        def last_passes(c, a):
+        def last_pass(c, b, a):
             m0, width = chunks[c]
-            share = 4 // len(tags[c])
-            words = z1_w[:, m0 : m0 + width] if a else z0_w[m0 // QUARTER][:, m0 % QUARTER : m0 % QUARTER + width]
-            for b, tag in enumerate(tags[c]):
-                if a == 0:
-                    banks[c, b] = psum.tile([P, share, width], F32, name="acc", tag=tag)
-                for i in range(share):
-                    nt = share * b + i
-                    nc.tensor.matmul_mx(
-                        out=banks[c, b][:, i, :],
-                        lhsT=w4_w[a][:, P * nt : P * (nt + 1)].bitcast(FP8X4),
-                        lhsT_scale=w4_s[a][:, P * nt : P * (nt + 1)],
-                        rhs=words.bitcast(FP8X4),
-                        rhs_scale=z_s[a][:, m0 : m0 + width],
-                        start=(a == 0 and i == 0),
-                        stop=(a == 1 and i == share - 1),
-                    )
+            share = 4 // len(chunk_banks[c])
+            if a == 0:
+                sums[c, b] = in_bank(chunk_banks[c][b], [P, share, width])
+            for i in range(share):
+                cols = slice(N * a + P * (share * b + i), N * a + P * (share * b + i + 1))
+                nc.tensor.matmul_mx(
+                    out=sums[c, b][:, i, :],
+                    lhsT=w4_w[:, cols].bitcast(FP8X4),
+                    lhsT_scale=w4_s[:, cols],
+                    rhs=z_w[a][:, m0 : m0 + width].bitcast(FP8X4),
+                    rhs_scale=z_s[a][:, m0 : m0 + width],
+                    start=(a == 0 and i == 0),
+                    stop=(a == 1 and i == share - 1),
+                )
 
         def fetch_chunk(c):
             m0, width = chunks[c]
-            z = at(AT_Z + (0, 4, 8, 12, 8)[c] * KIB, f"z1_{c}", [P, PACK, width], F32)[:]
+            z = at(AT_RELU + 4 * KIB * (c % 2), f"z1_{c}", [P, PACK, width], F32)
             for t in range(PACK):
-                fetch(z[:, t, :], own, t, m0, width)
-            if c == 0:
-                woven_late[c] = at(AT_Z + 8 * KIB, "z1_woven0", [P, 11 * P, PACK], BF16)[:, 0:width, :]
-            else:
-                woven_late[c] = ring.tile([P, width, PACK], BF16, name="z1_woven", tag="s2", bufs=8, align_bytes=64)[:]
+                nc.vector.tensor_tensor(
+                    out=z[:, t, :],
+                    in0=pages[t][:].indirect(list3[:, m0 // 16 : (m0 + width) // 16]),
+                    in1=late_ctx[:, t, m0 : m0 + width],
+                    op=ALU.add,
+                )
             return z
 
         def weave_chunk(c, z, copy):
-            interleave(copy, woven_late[c], z)
-
-        def quantize_z0(i):
-            quantize(woven_z[i][:], z0_w[i][:], z_s[0][:, QUARTER * i : QUARTER * (i + 1)])
+            woven_late[c] = at(AT_TABLE + 8 * min(chunks[c][0], 768), f"z1_woven{c}", [P, chunks[c][1], PACK], BF16)
+            interleave(copy, woven_late[c][:], z[:])
 
         def finish(c):
             m0, width = chunks[c]
-            quantize(woven_late[c], z1_w[:, m0 : m0 + width], z_s[1][:, m0 : m0 + width])
-            last_passes(c, 1)
-            share = 4 // len(tags[c])
-            for b in range(len(tags[c])):
-                result = ring.tile([P, share, width], F32, name="result", tag="d", bufs=8, align_bytes=64)
+            quantize(woven_late[c][:], z_w[1][:, m0 : m0 + width], z_s[1][:, m0 : m0 + width])
+            share = 4 // len(chunk_banks[c])
+            for a in range(2):
+                for b in range(len(chunk_banks[c])):
+                    last_pass(c, b, a)
+            for b in range(len(chunk_banks[c])):
+                result = at(AT_CTX + 16 * m0 + 4 * share * width * b, f"result{c}_{b}", [P, share, width], F32)
                 copy = nc.vector.tensor_copy if (c, b) == (len(chunks) - 1, 1) else nc.scalar.copy
-                copy(out=result[:], in_=banks[c, b][:])
+                copy(out=result[:], in_=sums[c, b][:])
                 nc.sync.dma_start(out=out_rows[:, share * b : share * (b + 1), m0 : m0 + width], in_=result[:])
 
         for c in range(2):
             weave_chunk(c, fetch_chunk(c), nc.scalar.copy)
-        quantize(woven_w4[0][:], w4_w[0][:], w4_s[0][:])
-        quantize_z0(0)
-        last_passes(0, 0)
-        quantize(woven_w4[1][:], w4_w[1][:], w4_s[1][:])
         finish(0)
-        for i in range(1, 4):
-            quantize_z0(i)
-            last_passes(i, 0)
-        last_passes(4, 0)
-        finish(1)
         weave_chunk(2, fetch_chunk(2), nc.scalar.copy)
+        finish(1)
         weave_chunk(3, fetch_chunk(3), nc.scalar.copy)
         finish(2)
         z = fetch_chunk(4)

@@ -22,17 +22,18 @@ PACK = 4
 BANK = 512
 GROUP = 256
 KIB = 1024
+HALF = 512
 AT_TABLE = 0
-AT_W2_RAW = 8 * KIB
-AT_W3_RAW = 68 * KIB
-AT_W2_WOVEN = 19 * KIB
-AT_RELU = 24 * KIB
-AT_SECOND = 32 * KIB
-AT_GATE = 40 * KIB
-AT_CTX = 48 * KIB
-AT_W2_LATE = 64 * KIB
-AT_W3_LATE = 72 * KIB
-AT_W2_RAW_LATE = 74 * KIB
+AT_W2_RAW = (8 * KIB, 12 * KIB, 16 * KIB)
+AT_PICKED = (26 * KIB, 33 * KIB, 16 * KIB, 20 * KIB)
+AT_W2_WOVEN = (24 * KIB, 29 * KIB + HALF, 31 * KIB + HALF)
+AT_LAST_GATE = 30 * KIB
+AT_RELU = 38 * KIB
+AT_SECOND = 46 * KIB
+AT_GATE = 54 * KIB
+AT_STATES = 62 * KIB
+AT_ROWS = 78 * KIB
+AT_CTX = 94 * KIB
 
 
 def tile_list_byte_patch_slots_kernel(
@@ -60,37 +61,37 @@ def tile_list_byte_patch_slots_kernel(
         tab_s = kept("tab_s", [P, T], U8)
         w1_w = [kept(f"w1_w{a}", [P, 2 * BANK], U8) for a in range(2)]
         w1_s = kept("w1_s", [P, H], U8)
-        w3_raw_w = [at(AT_W3_RAW, "w3_raw_w0", [P, BANK], I32), kept("w3_raw_w1", [P, BANK], I32)]
-        w3_raw_s = kept("w3_raw_s", [P, H], U8)
-        w2_w = [kept(f"w2_w{a}", [P, BANK], U32) for a in range(2)]
-        w2_s = [kept(f"w2_s{a}", [P, BANK], U8) for a in range(2)]
+        w3_early_w = [kept(f"w3_early_w{h}", [P, GROUP], I32) for h in range(2)]
+        w3_early_s = kept("w3_early_s", [P, BANK], U8)
+        w3_raw_w = kept("w3_raw_w", [P, BANK], I32)
+        w3_raw_s = kept("w3_raw_s", [P, BANK], U8)
+        w2_w = [kept(f"w2_w{i}", [P, width], U32) for i, width in enumerate((GROUP, GROUP, BANK))]
+        w2_s = [kept(f"w2_s{i}", [P, width], U8) for i, width in enumerate((GROUP, GROUP, BANK))]
         w4_w = kept("w4_w", [P, 2 * N], U32)
         w4_s = kept("w4_s", [P, 2 * N], U8)
         z_w = [kept(f"z_w{a}", [P, PM], U32) for a in range(2)]
         z_s = [kept(f"z_s{a}", [P, PM], U8) for a in range(2)]
-        slot_w = {j0: kept(f"slot_w{j0}", [P, PACK, width], F32) for j0, width in ((0, 256), (256, 256), (512, 512))}
-        states = [kept(f"states{a}", [P, PACK * S], F32) for a in range(2)]
+        early_w = [kept("early_w0", [P, GROUP], F32), kept("early_w1", [P, S - GROUP], F32)]
+        late_w = kept("late_w", [P, PACK, S], F32)
+        late_states = kept("late_states", [P, PACK * S], F32)
         late_ctx = kept("late_ctx", [P, PACK, PM], F32)
         pages = [kept(f"page{t}", [P, T2], F32) for t in range(PACK)]
         ident = kept("ident", [P, P], F32)
 
-        def load_scales(plane, rows, quadrants):
-            for q in quadrants:
-                nc.sync.dma_start(out=plane[32 * q : 32 * q + 4, :].bitcast(I32), in_=rows[0, 4 * q : 4 * q + 4, :].bitcast(I32))
-
-        def load_slot_weights(j0):
-            rows = wgs.rearrange("(m t) j -> m t j", t=PACK)
-            width = slot_w[j0].shape[2]
+        def load_scales(plane, rows, c0):
+            width = plane.shape[1]
             for q in range(4):
-                nc.sync.dma_start(out=slot_w[j0][32 * q : 32 * q + 32], in_=rows[:, :, j0 : j0 + width])
+                nc.sync.dma_start(
+                    out=plane[32 * q : 32 * q + 4, :].bitcast(I32), in_=rows[0, 4 * q : 4 * q + 4, c0 : c0 + width].bitcast(I32)
+                )
 
         def load_rows(tile, rows):
             nc.sync.dma_start(out=tile[:], in_=rows.rearrange("(p t) c -> p t c", t=PACK))
             return tile
 
-        def load_w3_words(a):
+        def load_w3_words(tile, c0):
             words = w3_words[0].rearrange("p c i -> p (c i)").bitcast(I32)
-            nc.sync.dma_start(out=w3_raw_w[a][:], in_=words[:, BANK * a : BANK * (a + 1)])
+            nc.sync.dma_start(out=tile[:], in_=words[:, c0 : c0 + tile.shape[1]])
 
         def load_w1_words(a):
             nc.sync.dma_start(out=w1_w[a][:].bitcast(I32), in_=w1_words[0, :, 2 * BANK * a : 2 * BANK * (a + 1)].bitcast(I32))
@@ -105,6 +106,14 @@ def tile_list_byte_patch_slots_kernel(
         def quantize(woven, words, scales):
             nc.vector.quantize_mx(out=words.bitcast(FP8X4), scales=scales, in_=woven.rearrange("p c t -> p (c t)"))
 
+        def quantize_w2(i):
+            woven = at(AT_W2_WOVEN[i], f"w2_woven{i}", [P, w2_w[i].shape[1], PACK], BF16)
+            if i == 0:
+                interleave(nc.vector.tensor_copy, woven[:], w2_raw[i][:])
+            else:
+                weave_on_scalar(woven[:], w2_raw[i][:])
+            quantize(woven[:], w2_w[i][:], w2_s[i][:])
+
         v_w, v_s = {}, {}
 
         def gather_table(j0, words, scales):
@@ -116,16 +125,10 @@ def tile_list_byte_patch_slots_kernel(
                 v_w[(j0 + c0) // GROUP] = words[:, c0 : c0 + GROUP]
                 v_s[(j0 + c0) // GROUP] = scales[:, c0 : c0 + GROUP]
 
-        def deal_words(copy, dealt, raw):
-            copy(out=dealt.rearrange("p (t c i) -> p c t i", t=PACK, i=4), in_=raw.rearrange("p (c i t) -> p c t i", t=PACK, i=4))
-
-        relu_t, second_t, second_bank = {}, {}, {}
-
-        def token_product(e, bank, words, scales):
-            g, cols = e % 8 // 2, slice(P * (e % 2), P * (e % 2 + 1))
-            acc = in_bank(bank, [P, BANK])
+        def token_product(acc, e, words, scales):
+            g, cols = e // 2, slice(P * (e % 2), P * (e % 2 + 1))
             nc.tensor.matmul_mx(
-                out=acc[:],
+                out=acc,
                 lhsT=v_w[g][:, cols].bitcast(FP8X4),
                 lhsT_scale=v_s[g][:, cols],
                 rhs=words,
@@ -133,65 +136,45 @@ def tile_list_byte_patch_slots_kernel(
                 start=True,
                 stop=True,
             )
-            return acc[:].rearrange("j (m t) -> j t m", t=PACK)
 
-        def first_product(e):
-            a = e // 8
-            by_slice = token_product(e, e % 2, w1_w[a][:].bitcast(FP4X4), w1_s[:, BANK * a : BANK * (a + 1)])
-            relu_t[e] = at((AT_W2_RAW - 4 * KIB if e in (2, 3) else AT_RELU) + 2 * KIB * (e % 4), f"relu{e}", [P, PACK, P], F32)
-            nc.scalar.activation(out=relu_t[e][:], in_=by_slice, func=ACT.Relu)
+        turn = {"relu": 0, "second": 0, "gate": 0, "bank": 0}
 
-        def second_product(e):
-            a = e // 8
-            second_bank[e] = token_product(e, (2, 6)[a] + e % 2, w2_w[a][:].bitcast(FP8X4), w2_s[a][:])
+        def next_slot(kind, count):
+            turn[kind] = turn[kind] + 1
+            return (turn[kind] - 1) % count
 
-        def empty_second(e, t0, count, offset):
-            part = at(offset, f"second{e}_{t0}", [P, count, P], F32)
-            nc.scalar.copy(out=part[:], in_=second_bank[e][:, t0 : t0 + count, :])
-            for i in range(count):
-                second_t[e, t0 + i] = part[:, i, :]
-
-        def state_of(g, t0, count):
-            start = PACK * GROUP * (g % 4) + GROUP * t0
-            return states[g // 4][:, start : start + GROUP * count]
-
-        def weigh_third(g, t0, count, bank):
-            a, j0 = g // 4, GROUP * (g % 4)
-            third = in_bank(bank, [P, GROUP * count])
-            for i in range(count):
-                cols = slice(P * (t0 + i), P * (t0 + i + 1))
+        def weigh_third(g, stationary, h, weights, bank):
+            third = in_bank(bank, [P, len(stationary), GROUP])
+            for i, (words, scales) in enumerate(stationary):
                 nc.tensor.matmul_mx(
-                    out=third[:, GROUP * i : GROUP * (i + 1)],
-                    lhsT=w3_w[a][:, cols].bitcast(FP8X4),
-                    lhsT_scale=w3_s[:, a, cols],
-                    rhs=v_w[g % 4].bitcast(FP8X4),
-                    rhs_scale=v_s[g % 4],
+                    out=third[:, i, :],
+                    lhsT=words.bitcast(FP8X4),
+                    lhsT_scale=scales,
+                    rhs=v_w[g].bitcast(FP8X4),
+                    rhs_scale=v_s[g],
                     start=True,
                     stop=True,
                 )
-            h = state_of(g, t0, count)
             nc.scalar.activation(out=h, in_=third[:], func=ACT.Abs)
-            start = min(j0, BANK)
-            by_slice = h.rearrange("p (t j) -> p t j", j=GROUP)
-            weights = slot_w[start][:, t0 : t0 + count, j0 - start : j0 - start + GROUP]
-            nc.gpsimd.tensor_tensor(out=by_slice, in0=by_slice, in1=weights, op=ALU.mult)
+            nc.gpsimd.tensor_tensor(out=h, in0=h, in1=weights, op=ALU.mult)
 
-        def gate_state(g, t0, count, bank, gate_at):
-            q = in_bank(bank, [P, GROUP * count])
-            for i in range(2 * count):
-                t, e, cols = t0 + i // 2, 2 * g + i % 2, slice(P * i, P * (i + 1))
-                nc.tensor.matmul(q[:, cols], lhsT=relu_t[e][:, t, :], rhs=ident[:], is_transpose=True, start=True, stop=False)
-                nc.tensor.matmul(q[:, cols], lhsT=second_t[e, t], rhs=ident[:], is_transpose=True, start=False, stop=True)
-            gate = at(gate_at, f"gate{g}_{t0}", [P, GROUP * count], F32)
+        def gate_state(name, addends, h, gate_at, bank):
+            count = len(addends) // 2
+            q = in_bank(bank, [P, count, GROUP])
+            for i, (relu, second) in enumerate(addends):
+                cols = q[:, i // 2, P * (i % 2) : P * (i % 2 + 1)]
+                nc.tensor.matmul(cols, lhsT=relu, rhs=ident[:], is_transpose=True, start=True, stop=False)
+                nc.tensor.matmul(cols, lhsT=second, rhs=ident[:], is_transpose=True, start=False, stop=True)
+            if gate_at is None:
+                gate_at = AT_GATE + 2 * KIB * next_slot("gate", 4)
+            gate = at(gate_at, name, [P, count, GROUP], F32)
             nc.scalar.activation(out=gate[:], in_=q[:], func=ACT.Silu)
             nc.scalar.activation(out=gate[:], in_=gate[:], func=ACT.Abs)
-            h = state_of(g, t0, count)
             nc.gpsimd.tensor_tensor(out=h, in0=h, in1=gate[:], op=ALU.mult)
 
-        def put_state(g, t0, count):
-            picks = list2[:, GROUP * (g % 4) // 16 : GROUP * (g % 4 + 1) // 16]
-            for t in range(t0, t0 + count):
-                nc.vector.tensor_copy(out=pages[t][:].indirect(picks), in_=state_of(g, t, 1))
+        def put_state(page, g, state):
+            picks = list2[:, GROUP * g // 16 : GROUP * (g + 1) // 16]
+            nc.vector.tensor_copy(out=pages[page][:].indirect(picks), in_=state)
 
         nc.gpsimd.memset(tab_s[:].bitcast(I32), 0)
         nc.gpsimd.memset(w3_raw_s[:].bitcast(I32), 0)
@@ -205,103 +188,150 @@ def tile_list_byte_patch_slots_kernel(
         for t in range(2, PACK):
             nc.gpsimd.memset(pages[t][:].bitcast(I32), 0)
         nc.sync.dma_start(list1[:], offs)
-        load_scales(w1_s, w1_scales, range(4))
         nc.sync.dma_start(out=tab_w[:], in_=tab_words[0].rearrange("p c i -> p (c i)").bitcast(I32))
+        load_scales(tab_s, tab_scales, 0)
+        w2_raw = [load_rows(at(AT_W2_RAW[0], "w2_raw0", [P, PACK, GROUP], F32), w2[:, 0:GROUP])]
         load_w1_words(0)
+        load_w3_words(w3_early_w[0], 0)
+        load_scales(w1_s, w1_scales, 0)
+        load_scales(w3_early_s, w3_scales, 0)
+        nc.sync.dma_start(out=early_w[0][:], in_=wgs[:, 0:GROUP])
         nc.sync.dma_start(list2[:], offs2)
-        load_scales(tab_s, tab_scales, range(4))
-        raw = [load_rows(at(AT_W2_RAW, "w2_raw0", [P, PACK, 384], F32), w2[:, 0:384])]
-        raw.append(load_rows(at(AT_W2_RAW + 6 * KIB, "w2_raw1", [P, PACK, P], F32), w2[:, 384:BANK]))
-        load_scales(w3_raw_s, w3_scales, range(4))
-        load_w3_words(0)
-        load_slot_weights(0)
-        load_slot_weights(256)
+        nc.sync.dma_start(out=early_w[1][:], in_=wgs[:, GROUP:S])
+        load_w3_words(w3_early_w[1], GROUP)
+        w2_raw.append(load_rows(at(AT_W2_RAW[1], "w2_raw1", [P, PACK, GROUP], F32), w2[:, GROUP:BANK]))
+        w2_raw.append(load_rows(at(AT_W2_RAW[2], "w2_raw2", [P, PACK, BANK], F32), w2[:, BANK : 2 * BANK]))
+        nc.sync.dma_start(list3[:], offs3)
+        load_scales(w3_raw_s, w3_scales, BANK)
+        load_w3_words(w3_raw_w, BANK)
+        early_ctx = [at(AT_CTX + 4 * KIB * s, f"early_ctx{s}", [P, PM], F32) for s in range(4)]
+        for s in range(2):
+            nc.sync.dma_start(out=early_ctx[s][:], in_=ctx[P * s : P * (s + 1), :])
         load_w1_words(1)
+        for q in range(4):
+            nc.sync.dma_start(out=late_w[32 * q : 32 * q + 32], in_=wgs.rearrange("(m t) j -> m t j", t=PACK))
+        for s in range(2, 4):
+            nc.sync.dma_start(out=early_ctx[s][:], in_=ctx[P * s : P * (s + 1), :])
 
         gather_table(0, kept("v_w0", [P, GROUP], U32), kept("v_s0", [P, GROUP], U8))
-        first_product(0)
-        first_product(1)
-        gather_table(GROUP, kept("v_w1", [P, GROUP], U32), kept("v_s1", [P, GROUP], U8))
-        woven = at(AT_W2_WOVEN, "w2_woven", [P, BANK, PACK], BF16)
-        interleave(nc.scalar.copy, woven[:, 0:P, :], raw[0][:, :, 0:P])
-        interleave(nc.vector.tensor_copy, woven[:, P:384, :], raw[0][:, :, P:384])
-        interleave(nc.vector.tensor_copy, woven[:, 384:BANK, :], raw[1][:])
-        first_product(2)
-        first_product(3)
-        quantize(woven[:], w2_w[0][:], w2_s[0][:])
-        raw_late = load_rows(at(AT_W2_RAW_LATE, "w2_raw_late", [P, PACK, BANK], F32), w2[:, BANK : 2 * BANK])
-        load_slot_weights(512)
-        load_w3_words(1)
-        nc.sync.dma_start(list3[:], offs3)
-        load_rows(late_ctx, ctx[BANK : 2 * BANK, :])
+        quantize_w2(0)
+        gather_table(GROUP, at(AT_W2_WOVEN[0], "v_w1", [P, GROUP], U32), at(AT_W2_RAW[0] + 3 * KIB, "v_s1", [P, GROUP], U8))
 
-        w3_s = at(AT_W2_WOVEN + KIB, "w3_s", [P, 2, BANK], U8)
-        nc.vector.tensor_copy(
-            out=w3_s[:].rearrange("p a (t m) -> p a t m", t=PACK),
-            in_=w3_raw_s[:].rearrange("p (a m t) -> p a t m", a=2, t=PACK),
-        )
-        w3_w = [at(AT_W2_WOVEN - KIB, "w3_w0", [P, BANK], I32)]
-        deal_words(nc.vector.tensor_copy, w3_w[0][:], w3_raw_w[0][:])
-        gather_table(2 * GROUP, at(AT_W3_RAW + 3 * BANK, "v_w2", [P, BANK], U32), at(AT_W3_RAW + KIB, "v_s2", [P, BANK], U8))
+        early_rows = at(AT_ROWS, "early_rows", [P, PACK, PM], F32)
+        picked = {}
+
+        def early_unit(pair, g, states, parts, gate_at):
+            first, second = in_bank(g % 2, [P, 2, GROUP]), in_bank(2 + g % 2, [P, 2, GROUP])
+            c0 = GROUP * pair
+            for i in range(2):
+                token_product(first[:, i, :], 2 * g + i, w1_w[0][:, 2 * c0 : 2 * (c0 + GROUP)].bitcast(FP4X4), w1_s[:, c0 : c0 + GROUP])
+            relu = at(AT_RELU + 2 * KIB * next_slot("relu", 4), f"relu{pair}_{g}", [P, 2, GROUP], F32)
+            if (pair, g) == (0, 1):
+                nc.vector.tensor_scalar(out=relu[:], in0=first[:], scalar1=0.0, scalar2=None, op0=ALU.max)
+            else:
+                nc.scalar.activation(out=relu[:], in_=first[:], func=ACT.Relu)
+            for i in range(2):
+                token_product(second[:, i, :], 2 * g + i, w2_w[pair][:].bitcast(FP8X4), w2_s[pair][:])
+            second_at = AT_SECOND + 2 * KIB * next_slot("second", 4)
+            weights = early_w[0][:] if g == 0 else early_w[1][:, GROUP * (g - 1) : GROUP * g]
+            for i0, count in parts:
+                h = states[:, i0 : i0 + count, GROUP * g : GROUP * (g + 1)]
+                stationary = [
+                    (w3_early_w[pair][:, P * i : P * (i + 1)], w3_early_s[:, c0 + P * i : c0 + P * (i + 1)]) for i in range(i0, i0 + count)
+                ]
+                bank = 4 + next_slot("bank", 4)
+                weigh_third(g, stationary, h, weights.unsqueeze(1).to_broadcast([P, count, GROUP]), bank)
+                copied = at(AT_W2_RAW[0] + 2 * KIB if (pair, g, i0) == (0, 0, 0) else second_at + KIB * i0, f"second{pair}_{g}_{i0}", [P, 2, P * count], F32)
+                copy = nc.vector.tensor_copy if (pair, g) == (0, 1) else nc.scalar.copy
+                copy(out=copied[:], in_=second[:, :, P * i0 : P * (i0 + count)])
+                addends = [
+                    (relu[:, e, P * (i0 + i) : P * (i0 + i + 1)], copied[:, e, P * i : P * (i + 1)]) for i in range(count) for e in range(2)
+                ]
+                gate_state(f"gate{pair}_{g}_{i0}", addends, h, gate_at, bank)
+                for i in range(i0, i0 + count):
+                    put_state(2 * pair + i, g, states[:, i, GROUP * g : GROUP * (g + 1)])
+
+        def fetch_slice(s):
+            picked[s] = at(AT_PICKED[s], f"picked{s}", [P, PM], F32)
+            nc.vector.tensor_copy(out=picked[s][:], in_=pages[s][:].indirect(list3[:]))
+
+        def add_and_regroup(s):
+            summed = at(AT_STATES + 4 * KIB * s, f"summed{s}", [P, PM], F32)
+            for c0 in range(0, PM, HALF):
+                cols = slice(c0, c0 + HALF)
+                nc.gpsimd.tensor_tensor(out=summed[:, cols], in0=picked[s][:, cols], in1=early_ctx[s][:, cols], op=ALU.add)
+            for t in range(PACK):
+                nc.sync.dma_start(out=early_rows[32 * s : 32 * (s + 1), t, :], in_=summed[t:P:PACK, :])
+
+        states = at(AT_STATES, "states0", [P, 2, S], F32)
+        early_unit(0, 0, states, ((0, 1), (1, 1)), None)
+        gather_table(2 * GROUP, at(AT_W2_RAW[0], "v_w2", [P, BANK], U32), at(AT_W2_RAW[0] + 2 * KIB, "v_s2", [P, BANK], U8))
         raw_w4 = [load_rows(at(AT_TABLE, "w4_raw0", [P, PACK, N], F32), w4[0:BANK, :])]
-
-        second_product(0)
-        second_product(1)
-        firsts = (
-            (0, 1, 4, 4, (AT_SECOND + BANK, AT_SECOND + KIB)),
-            (1, 1, 5, 0, (AT_W3_RAW, AT_W3_RAW + BANK)),
-            (2, 2, 6, 1, (AT_SECOND, AT_SECOND + KIB)),
+        load_rows(late_ctx, ctx[BANK : 2 * BANK, :])
+        for g in range(1, 4):
+            early_unit(0, g, states, ((0, 2),), AT_LAST_GATE if g == 3 else None)
+        quantize_w2(1)
+        w3_late_s = at(AT_LAST_GATE, "w3_late_s", [P, BANK], U8)
+        nc.gpsimd.tensor_copy(
+            out=w3_late_s[:].rearrange("p (t m) -> p t m", t=PACK), in_=w3_raw_s[:].rearrange("p (m t) -> p t m", t=PACK)
         )
-        for i, (t0, count, third_bank, sum_bank, offset) in enumerate(firsts):
-            weigh_third(0, t0, count, third_bank)
-            empty_second(0, t0, count, offset[0])
-            empty_second(1, t0, count, offset[1])
-            gate_state(0, t0, count, sum_bank, AT_GATE + 2 * KIB * i)
-            put_state(0, t0, count)
+        fetch_slice(0)
+        quantize_w2(2)
+        fetch_slice(1)
 
-        picked = states[0][:].rearrange("p (t m) -> p t m", t=PACK)
-        early_ctx = []
-        for g in range(1, 8):
-            for e in (2 * g, 2 * g + 1):
-                if g > 1:
-                    first_product(e)
-            for e in (2 * g, 2 * g + 1):
-                second_product(e)
-                empty_second(e, 0, PACK, AT_W2_LATE if e == 5 else AT_SECOND + 2 * KIB * (e % 4))
-            for half in range(2):
-                weigh_third(g, 2 * half, 2, 4 + half)
-            for half in range(2):
-                gate_at = AT_GATE + 2 * KIB * ((2 * g + half + 1) % 4)
-                if (g, half) == (1, 0):
-                    gate_at = AT_W3_LATE
-                if half == 1 and g in (5, 6):
-                    gate_at = AT_CTX + 8 * KIB * (g - 5) + 3 * KIB
-                gate_state(g, 2 * half, 2, (6, 2)[g // 4] + half, gate_at)
-                put_state(g, 2 * half, 2)
-                if g == 3:
-                    for t in (2 * half, 2 * half + 1):
-                        nc.vector.tensor_copy(out=picked[:, t, :], in_=pages[t][:].indirect(list3[:]))
-            if g == 1:
-                w3_w.append(at(AT_W3_LATE, "w3_w1", [P, BANK], I32))
-                deal_words(nc.gpsimd.tensor_copy, w3_w[1][:], w3_raw_w[1][:])
-            if g == 2:
-                woven = at(AT_W2_LATE, "w2_woven_late", [P, BANK, PACK], BF16)
-                weave_on_scalar(woven[:], raw_late[:])
-                quantize(woven[:], w2_w[1][:], w2_s[1][:])
-                raw_w4.append(load_rows(at(AT_W2_RAW, "w4_raw1", [P, PACK, N], F32), w4[BANK : 2 * BANK, :]))
-            if g in (5, 6):
-                for c in (2 * (g - 5), 2 * (g - 5) + 1):
-                    own = at(AT_CTX + 4 * KIB * c, f"early_ctx{c}", [P, PACK, GROUP], F32)
-                    early_ctx.append(load_rows(own, ctx[0:BANK, GROUP * c : GROUP * (c + 1)]))
+        states = at(AT_STATES + 8 * KIB, "states1", [P, 2, S], F32)
+        for g in range(4):
+            early_unit(1, g, states, ((0, 2),), AT_STATES + 3 * KIB if g == 3 else None)
+        w3_late_w = at(AT_W2_RAW[1], "w3_late_w", [P, BANK], U32)
+        nc.scalar.copy(
+            out=w3_late_w[:].rearrange("p (t c i) -> p c t i", t=PACK, i=4),
+            in_=w3_raw_w[:].bitcast(U32).rearrange("p (c i t) -> p c t i", t=PACK, i=4),
+        )
+        add_and_regroup(0)
+        add_and_regroup(1)
+        raw_w4.append(load_rows(at(AT_CTX, "w4_raw1", [P, PACK, N], F32), w4[BANK : 2 * BANK, :]))
+        fetch_slice(2)
+        fetch_slice(3)
 
-        woven_z = at(AT_RELU, "z0_woven", [P, PM, PACK], BF16)
-        for c in range(4):
-            cols = slice(GROUP * c, GROUP * (c + 1))
-            nc.gpsimd.tensor_tensor(out=picked[:, :, cols], in0=picked[:, :, cols], in1=early_ctx[c][:], op=ALU.add)
-            interleave(nc.scalar.copy, woven_z[:, cols, :], picked[:, :, cols])
+        def late_group(g, parts, last_gate_at):
+            relu, second, second_at = [], [], []
+            for e in range(2):
+                first = in_bank(e, [P, BANK])
+                token_product(first[:], 2 * g + e, w1_w[1][:].bitcast(FP4X4), w1_s[:, BANK : 2 * BANK])
+                relu.append(at(AT_RELU + 2 * KIB * next_slot("relu", 4), f"late_relu{g}_{e}", [P, PACK, P], F32))
+                nc.scalar.activation(out=relu[e][:], in_=first[:].rearrange("j (m t) -> j t m", t=PACK), func=ACT.Relu)
+            for e in range(2):
+                second.append(in_bank(2 + e, [P, BANK]))
+                token_product(second[e][:], 2 * g + e, w2_w[2][:].bitcast(FP8X4), w2_s[2][:])
+                second_at.append(AT_SECOND + 2 * KIB * next_slot("second", 4))
+            copied = {}
+            for t0, count, c0, c1 in parts:
+                start = PACK * GROUP * g + GROUP * t0
+                h = late_states[:, start : start + GROUP * count].rearrange("p (t j) -> p t j", j=GROUP)
+                stationary = [(w3_late_w[:, P * t : P * (t + 1)], w3_late_s[:, P * t : P * (t + 1)]) for t in range(t0, t0 + count)]
+                if c1 > c0:
+                    for e in range(2):
+                        part = at(second_at[e] + 4 * P * c0, f"late_second{g}_{e}_{c0}", [P, c1 - c0, P], F32)
+                        nc.scalar.copy(out=part[:], in_=second[e][:].rearrange("j (m t) -> j t m", t=PACK)[:, c0:c1, :])
+                        for t in range(c0, c1):
+                            copied[e, t] = part[:, t - c0, :]
+                bank = 4 + next_slot("bank", 4)
+                weigh_third(g, stationary, h, late_w[:, t0 : t0 + count, GROUP * g : GROUP * (g + 1)], bank)
+                addends = [(relu[e][:, t, :], copied[e, t]) for t in range(t0, t0 + count) for e in range(2)]
+                gate_state(f"late_gate{g}_{t0}", addends, h, last_gate_at if t0 + count == PACK else None, bank)
+                for i in range(count):
+                    put_state(t0 + i, g, h[:, i, :])
+
+        for g in range(4):
+            late_group(g, ((0, 2, 0, 4), (2, 2, 4, 4)), AT_STATES + 4 * KIB * g if g >= 2 else None)
+            if g >= 2:
+                add_and_regroup(g)
+
         woven_w4 = at(AT_SECOND, "w4_woven", [P, 2 * N, PACK], BF16)
         for a in range(2):
             weave_on_scalar(woven_w4[:, N * a : N * (a + 1), :], raw_w4[a][:])
+        woven_z = at(AT_CTX, "z0_woven", [P, PM, PACK], BF16)
+        weave_on_scalar(woven_z[:], early_rows[:])
         quantize(woven_w4[:], w4_w[:], w4_s[:])
         quantize(woven_z[:], z_w[0][:], z_s[0][:])
 
@@ -340,7 +370,7 @@ def tile_list_byte_patch_slots_kernel(
             return z
 
         def weave_chunk(c, z, copy):
-            woven_late[c] = at(AT_TABLE + 8 * min(chunks[c][0], 768), f"z1_woven{c}", [P, chunks[c][1], PACK], BF16)
+            woven_late[c] = at(AT_ROWS + 8 * min(chunks[c][0], 768), f"z1_woven{c}", [P, chunks[c][1], PACK], BF16)
             interleave(copy, woven_late[c][:], z[:])
 
         def finish(c):
@@ -351,7 +381,7 @@ def tile_list_byte_patch_slots_kernel(
                 for b in range(len(chunk_banks[c])):
                     last_pass(c, b, a)
             for b in range(len(chunk_banks[c])):
-                result = at(AT_CTX + 16 * m0 + 4 * share * width * b, f"result{c}_{b}", [P, share, width], F32)
+                result = at(AT_STATES + 16 * m0 + 4 * share * width * b, f"result{c}_{b}", [P, share, width], F32)
                 copy = nc.vector.tensor_copy if (c, b) == (len(chunks) - 1, 1) else nc.scalar.copy
                 copy(out=result[:], in_=sums[c, b][:])
                 nc.sync.dma_start(out=out_rows[:, share * b : share * (b + 1), m0 : m0 + width], in_=result[:])

@@ -25,15 +25,16 @@ KIB = 1024
 HALF = 512
 AT_TABLE = 0
 AT_W2_RAW = (8 * KIB, 12 * KIB, 16 * KIB)
-AT_PICKED = (26 * KIB, 33 * KIB, 16 * KIB, 20 * KIB)
-AT_W2_WOVEN = (24 * KIB, 29 * KIB + HALF, 31 * KIB + HALF)
-AT_LAST_GATE = 30 * KIB
-AT_RELU = 38 * KIB
-AT_SECOND = 46 * KIB
-AT_GATE = 54 * KIB
-AT_STATES = 62 * KIB
-AT_ROWS = 78 * KIB
-AT_CTX = 94 * KIB
+AT_PICKED = (26 * KIB, 30 * KIB + HALF, 16 * KIB, 20 * KIB)
+AT_W2_WOVEN = (24 * KIB, 26 * KIB, 28 * KIB)
+AT_W2_WORDS = (40 * KIB, 41 * KIB, 42 * KIB)
+AT_RELU = 44 * KIB
+AT_SECOND = 52 * KIB
+AT_GATE = 60 * KIB
+AT_STATES = 68 * KIB
+AT_ROWS = 84 * KIB
+AT_CTX = 100 * KIB
+AT_LAST_WORDS = 116 * KIB
 
 
 def tile_list_byte_patch_slots_kernel(
@@ -65,11 +66,9 @@ def tile_list_byte_patch_slots_kernel(
         w3_early_s = kept("w3_early_s", [P, BANK], U8)
         w3_raw_w = kept("w3_raw_w", [P, BANK], I32)
         w3_raw_s = kept("w3_raw_s", [P, BANK], U8)
-        w2_w = [kept(f"w2_w{i}", [P, width], U32) for i, width in enumerate((GROUP, GROUP, BANK))]
+        w2_w = []
         w2_s = [kept(f"w2_s{i}", [P, width], U8) for i, width in enumerate((GROUP, GROUP, BANK))]
-        w4_w = kept("w4_w", [P, 2 * N], U32)
         w4_s = kept("w4_s", [P, 2 * N], U8)
-        z_w = [kept(f"z_w{a}", [P, PM], U32) for a in range(2)]
         z_s = [kept(f"z_s{a}", [P, PM], U8) for a in range(2)]
         early_w = [kept("early_w0", [P, GROUP], F32), kept("early_w1", [P, S - GROUP], F32)]
         late_w = kept("late_w", [P, PACK, S], F32)
@@ -107,11 +106,10 @@ def tile_list_byte_patch_slots_kernel(
             nc.vector.quantize_mx(out=words.bitcast(FP8X4), scales=scales, in_=woven.rearrange("p c t -> p (c t)"))
 
         def quantize_w2(i):
-            woven = at(AT_W2_WOVEN[i], f"w2_woven{i}", [P, w2_w[i].shape[1], PACK], BF16)
-            if i == 0:
-                interleave(nc.vector.tensor_copy, woven[:], w2_raw[i][:])
-            else:
-                weave_on_scalar(woven[:], w2_raw[i][:])
+            width = w2_s[i].shape[1]
+            woven = at(AT_W2_WOVEN[i], f"w2_woven{i}", [P, width, PACK], BF16)
+            weave_on_scalar(woven[:], w2_raw[i][:])
+            w2_w.append(at(AT_W2_WORDS[i], f"w2_w{i}", [P, width], U32))
             quantize(woven[:], w2_w[i][:], w2_s[i][:])
 
         v_w, v_s = {}, {}
@@ -143,7 +141,7 @@ def tile_list_byte_patch_slots_kernel(
             turn[kind] = turn[kind] + 1
             return (turn[kind] - 1) % count
 
-        def weigh_third(g, stationary, h, weights, bank):
+        def weigh_third(g, stationary, h, weights, bank, func):
             third = in_bank(bank, [P, len(stationary), GROUP])
             for i, (words, scales) in enumerate(stationary):
                 nc.tensor.matmul_mx(
@@ -155,10 +153,10 @@ def tile_list_byte_patch_slots_kernel(
                     start=True,
                     stop=True,
                 )
-            nc.scalar.activation(out=h, in_=third[:], func=ACT.Abs)
+            nc.scalar.activation(out=h, in_=third[:], func=func)
             nc.gpsimd.tensor_tensor(out=h, in0=h, in1=weights, op=ALU.mult)
 
-        def gate_state(name, addends, h, gate_at, bank):
+        def gate_state(name, addends, h, gate_at, bank, absolute):
             count = len(addends) // 2
             q = in_bank(bank, [P, count, GROUP])
             for i, (relu, second) in enumerate(addends):
@@ -169,7 +167,8 @@ def tile_list_byte_patch_slots_kernel(
                 gate_at = AT_GATE + 2 * KIB * next_slot("gate", 4)
             gate = at(gate_at, name, [P, count, GROUP], F32)
             nc.scalar.activation(out=gate[:], in_=q[:], func=ACT.Silu)
-            nc.scalar.activation(out=gate[:], in_=gate[:], func=ACT.Abs)
+            if absolute:
+                nc.scalar.activation(out=gate[:], in_=gate[:], func=ACT.Abs)
             nc.gpsimd.tensor_tensor(out=h, in0=h, in1=gate[:], op=ALU.mult)
 
         def put_state(page, g, state):
@@ -215,21 +214,18 @@ def tile_list_byte_patch_slots_kernel(
 
         gather_table(0, kept("v_w0", [P, GROUP], U32), kept("v_s0", [P, GROUP], U8))
         quantize_w2(0)
-        gather_table(GROUP, at(AT_W2_WOVEN[0], "v_w1", [P, GROUP], U32), at(AT_W2_RAW[0] + 3 * KIB, "v_s1", [P, GROUP], U8))
+        gather_table(GROUP, kept("v_w1", [P, GROUP], U32), at(AT_W2_RAW[0] + 3 * KIB, "v_s1", [P, GROUP], U8))
 
         early_rows = at(AT_ROWS, "early_rows", [P, PACK, PM], F32)
         picked = {}
 
-        def early_unit(pair, g, states, parts, gate_at):
+        def early_unit(pair, g, states, parts, gate_at, ring):
             first, second = in_bank(g % 2, [P, 2, GROUP]), in_bank(2 + g % 2, [P, 2, GROUP])
             c0 = GROUP * pair
             for i in range(2):
                 token_product(first[:, i, :], 2 * g + i, w1_w[0][:, 2 * c0 : 2 * (c0 + GROUP)].bitcast(FP4X4), w1_s[:, c0 : c0 + GROUP])
             relu = at(AT_RELU + 2 * KIB * next_slot("relu", 4), f"relu{pair}_{g}", [P, 2, GROUP], F32)
-            if (pair, g) == (0, 1):
-                nc.vector.tensor_scalar(out=relu[:], in0=first[:], scalar1=0.0, scalar2=None, op0=ALU.max)
-            else:
-                nc.scalar.activation(out=relu[:], in_=first[:], func=ACT.Relu)
+            nc.scalar.activation(out=relu[:], in_=first[:], func=ACT.Relu)
             for i in range(2):
                 token_product(second[:, i, :], 2 * g + i, w2_w[pair][:].bitcast(FP8X4), w2_s[pair][:])
             second_at = AT_SECOND + 2 * KIB * next_slot("second", 4)
@@ -239,15 +235,14 @@ def tile_list_byte_patch_slots_kernel(
                 stationary = [
                     (w3_early_w[pair][:, P * i : P * (i + 1)], w3_early_s[:, c0 + P * i : c0 + P * (i + 1)]) for i in range(i0, i0 + count)
                 ]
-                bank = 4 + next_slot("bank", 4)
-                weigh_third(g, stationary, h, weights.unsqueeze(1).to_broadcast([P, count, GROUP]), bank)
+                bank = 4 + next_slot("bank", ring)
+                weigh_third(g, stationary, h, weights.unsqueeze(1).to_broadcast([P, count, GROUP]), bank, ACT.Copy)
                 copied = at(AT_W2_RAW[0] + 2 * KIB if (pair, g, i0) == (0, 0, 0) else second_at + KIB * i0, f"second{pair}_{g}_{i0}", [P, 2, P * count], F32)
-                copy = nc.vector.tensor_copy if (pair, g) == (0, 1) else nc.scalar.copy
-                copy(out=copied[:], in_=second[:, :, P * i0 : P * (i0 + count)])
+                nc.scalar.copy(out=copied[:], in_=second[:, :, P * i0 : P * (i0 + count)])
                 addends = [
                     (relu[:, e, P * (i0 + i) : P * (i0 + i + 1)], copied[:, e, P * i : P * (i + 1)]) for i in range(count) for e in range(2)
                 ]
-                gate_state(f"gate{pair}_{g}_{i0}", addends, h, gate_at, bank)
+                gate_state(f"gate{pair}_{g}_{i0}", addends, h, gate_at, bank, False)
                 for i in range(i0, i0 + count):
                     put_state(2 * pair + i, g, states[:, i, GROUP * g : GROUP * (g + 1)])
 
@@ -259,29 +254,30 @@ def tile_list_byte_patch_slots_kernel(
             summed = at(AT_STATES + 4 * KIB * s, f"summed{s}", [P, PM], F32)
             for c0 in range(0, PM, HALF):
                 cols = slice(c0, c0 + HALF)
-                nc.gpsimd.tensor_tensor(out=summed[:, cols], in0=picked[s][:, cols], in1=early_ctx[s][:, cols], op=ALU.add)
+                nc.scalar.activation(out=summed[:, cols], in_=picked[s][:, cols], func=ACT.Abs)
+                nc.gpsimd.tensor_tensor(out=summed[:, cols], in0=summed[:, cols], in1=early_ctx[s][:, cols], op=ALU.add)
             for t in range(PACK):
                 nc.sync.dma_start(out=early_rows[32 * s : 32 * (s + 1), t, :], in_=summed[t:P:PACK, :])
 
         states = at(AT_STATES, "states0", [P, 2, S], F32)
-        early_unit(0, 0, states, ((0, 1), (1, 1)), None)
+        early_unit(0, 0, states, ((0, 1), (1, 1)), None, 4)
         gather_table(2 * GROUP, at(AT_W2_RAW[0], "v_w2", [P, BANK], U32), at(AT_W2_RAW[0] + 2 * KIB, "v_s2", [P, BANK], U8))
         raw_w4 = [load_rows(at(AT_TABLE, "w4_raw0", [P, PACK, N], F32), w4[0:BANK, :])]
         load_rows(late_ctx, ctx[BANK : 2 * BANK, :])
         for g in range(1, 4):
-            early_unit(0, g, states, ((0, 2),), AT_LAST_GATE if g == 3 else None)
+            early_unit(0, g, states, ((0, 2),), {2: AT_W2_WOVEN[1] + KIB, 3: AT_W2_WORDS[1]}.get(g), 4)
         quantize_w2(1)
-        w3_late_s = at(AT_LAST_GATE, "w3_late_s", [P, BANK], U8)
+        quantize_w2(2)
+        w3_late_s = at(AT_W2_WOVEN[2] + 2 * KIB, "w3_late_s", [P, BANK], U8)
         nc.gpsimd.tensor_copy(
             out=w3_late_s[:].rearrange("p (t m) -> p t m", t=PACK), in_=w3_raw_s[:].rearrange("p (m t) -> p t m", t=PACK)
         )
         fetch_slice(0)
-        quantize_w2(2)
         fetch_slice(1)
 
         states = at(AT_STATES + 8 * KIB, "states1", [P, 2, S], F32)
         for g in range(4):
-            early_unit(1, g, states, ((0, 2),), AT_STATES + 3 * KIB if g == 3 else None)
+            early_unit(1, g, states, ((0, 2),), AT_STATES + 3 * KIB if g == 3 else None, 2)
         w3_late_w = at(AT_W2_RAW[1], "w3_late_w", [P, BANK], U32)
         nc.scalar.copy(
             out=w3_late_w[:].rearrange("p (t c i) -> p c t i", t=PACK, i=4),
@@ -316,22 +312,24 @@ def tile_list_byte_patch_slots_kernel(
                         for t in range(c0, c1):
                             copied[e, t] = part[:, t - c0, :]
                 bank = 4 + next_slot("bank", 4)
-                weigh_third(g, stationary, h, late_w[:, t0 : t0 + count, GROUP * g : GROUP * (g + 1)], bank)
+                weigh_third(g, stationary, h, late_w[:, t0 : t0 + count, GROUP * g : GROUP * (g + 1)], bank, ACT.Abs)
                 addends = [(relu[e][:, t, :], copied[e, t]) for t in range(t0, t0 + count) for e in range(2)]
-                gate_state(f"late_gate{g}_{t0}", addends, h, last_gate_at if t0 + count == PACK else None, bank)
+                gate_state(f"late_gate{g}_{t0}", addends, h, last_gate_at if t0 + count == PACK else None, bank, True)
                 for i in range(count):
                     put_state(t0 + i, g, h[:, i, :])
 
         for g in range(4):
-            late_group(g, ((0, 2, 0, 4), (2, 2, 4, 4)), AT_STATES + 4 * KIB * g if g >= 2 else None)
-            if g >= 2:
-                add_and_regroup(g)
+            late_group(g, ((0, 2, 0, 4), (2, 2, 4, 4)), (None, AT_STATES + 8 * KIB, AT_STATES + 12 * KIB, AT_LAST_WORDS + 3 * KIB)[g])
+            if g in (1, 2):
+                add_and_regroup(1 + g)
 
         woven_w4 = at(AT_SECOND, "w4_woven", [P, 2 * N, PACK], BF16)
         for a in range(2):
             weave_on_scalar(woven_w4[:, N * a : N * (a + 1), :], raw_w4[a][:])
         woven_z = at(AT_CTX, "z0_woven", [P, PM, PACK], BF16)
         weave_on_scalar(woven_z[:], early_rows[:])
+        w4_w = at(AT_LAST_WORDS, "w4_w", [P, 2 * N], U32)
+        z_w = [at(AT_LAST_WORDS + 4 * KIB, "z_w0", [P, PM], U32), kept("z_w1", [P, PM], U32)]
         quantize(woven_w4[:], w4_w[:], w4_s[:])
         quantize(woven_z[:], z_w[0][:], z_s[0][:])
 

@@ -216,7 +216,7 @@ def tile_list_byte_patch_slots_kernel(
         quantize_w2(0)
         gather_table(GROUP, kept("v_w1", [P, GROUP], U32), at(AT_W2_RAW[0] + 3 * KIB, "v_s1", [P, GROUP], U8))
 
-        early_rows = at(AT_ROWS, "early_rows", [P, PACK, PM], F32)
+        turned = at(AT_ROWS, "turned", [P, PM // P, 2, P, 2], BF16)
         picked = {}
 
         def early_unit(pair, g, states, parts, gate_at, ring):
@@ -231,7 +231,7 @@ def tile_list_byte_patch_slots_kernel(
             second_at = AT_SECOND + 2 * KIB * next_slot("second", 4)
             weights = early_w[0][:] if g == 0 else early_w[1][:, GROUP * (g - 1) : GROUP * g]
             for i0, count in parts:
-                h = states[:, i0 : i0 + count, GROUP * g : GROUP * (g + 1)]
+                h = states[:, g, i0 : i0 + count, :]
                 stationary = [
                     (w3_early_w[pair][:, P * i : P * (i + 1)], w3_early_s[:, c0 + P * i : c0 + P * (i + 1)]) for i in range(i0, i0 + count)
                 ]
@@ -244,22 +244,28 @@ def tile_list_byte_patch_slots_kernel(
                 ]
                 gate_state(f"gate{pair}_{g}_{i0}", addends, h, gate_at, bank, False)
                 for i in range(i0, i0 + count):
-                    put_state(2 * pair + i, g, states[:, i, GROUP * g : GROUP * (g + 1)])
+                    put_state(2 * pair + i, g, states[:, g, i, :])
 
         def fetch_slice(s):
             picked[s] = at(AT_PICKED[s], f"picked{s}", [P, PM], F32)
             nc.vector.tensor_copy(out=picked[s][:], in_=pages[s][:].indirect(list3[:]))
 
-        def add_and_regroup(s):
-            summed = at(AT_STATES + 4 * KIB * s, f"summed{s}", [P, PM], F32)
-            for c0 in range(0, PM, HALF):
-                cols = slice(c0, c0 + HALF)
-                nc.scalar.activation(out=summed[:, cols], in_=picked[s][:, cols], func=ACT.Abs)
-                nc.gpsimd.tensor_tensor(out=summed[:, cols], in0=summed[:, cols], in1=early_ctx[s][:, cols], op=ALU.add)
-            for t in range(PACK):
-                nc.sync.dma_start(out=early_rows[32 * s : 32 * (s + 1), t, :], in_=summed[t:P:PACK, :])
+        def add_and_turn(s, banks):
+            size = at(AT_STATES + 4 * KIB * s, f"size{s}", [P, PM], F32)
+            for half, bank in enumerate(banks):
+                cols = slice(HALF * half, HALF * (half + 1))
+                nc.scalar.activation(out=size[:, cols], in_=picked[s][:, cols], func=ACT.Abs)
+                total = in_bank(bank, [P, 4, P])
+                for i in range(4):
+                    tile_cols = slice(HALF * half + P * i, HALF * half + P * (i + 1))
+                    nc.tensor.matmul(total[:, i, :], lhsT=early_ctx[s][:, tile_cols], rhs=ident[:], is_transpose=True, start=True, stop=False)
+                    nc.tensor.matmul(total[:, i, :], lhsT=size[:, tile_cols], rhs=ident[:], is_transpose=True, start=False, stop=True)
+                nc.scalar.copy(
+                    out=turned[:, 4 * half : 4 * (half + 1), :, 32 * s : 32 * (s + 1), :],
+                    in_=total[:].rearrange("m i (q u e) -> m i u q e", u=2, e=2),
+                )
 
-        states = at(AT_STATES, "states0", [P, 2, S], F32)
+        states = at(AT_STATES, "states0", [P, 4, 2, GROUP], F32)
         early_unit(0, 0, states, ((0, 1), (1, 1)), None, 4)
         gather_table(2 * GROUP, at(AT_W2_RAW[0], "v_w2", [P, BANK], U32), at(AT_W2_RAW[0] + 2 * KIB, "v_s2", [P, BANK], U8))
         raw_w4 = [load_rows(at(AT_TABLE, "w4_raw0", [P, PACK, N], F32), w4[0:BANK, :])]
@@ -275,16 +281,16 @@ def tile_list_byte_patch_slots_kernel(
         fetch_slice(0)
         fetch_slice(1)
 
-        states = at(AT_STATES + 8 * KIB, "states1", [P, 2, S], F32)
+        states = at(AT_STATES + 8 * KIB, "states1", [P, 4, 2, GROUP], F32)
         for g in range(4):
-            early_unit(1, g, states, ((0, 2),), AT_STATES + 3 * KIB if g == 3 else None, 2)
+            early_unit(1, g, states, ((0, 2),), AT_STATES + 3 * KIB if g == 2 else None, 2)
         w3_late_w = at(AT_W2_RAW[1], "w3_late_w", [P, BANK], U32)
         nc.scalar.copy(
             out=w3_late_w[:].rearrange("p (t c i) -> p c t i", t=PACK, i=4),
             in_=w3_raw_w[:].bitcast(U32).rearrange("p (c i t) -> p c t i", t=PACK, i=4),
         )
-        add_and_regroup(0)
-        add_and_regroup(1)
+        add_and_turn(0, (6, 7))
+        add_and_turn(1, (6, 7))
         raw_w4.append(load_rows(at(AT_CTX, "w4_raw1", [P, PACK, N], F32), w4[BANK : 2 * BANK, :]))
         fetch_slice(2)
         fetch_slice(3)
@@ -319,19 +325,24 @@ def tile_list_byte_patch_slots_kernel(
                     put_state(t0 + i, g, h[:, i, :])
 
         for g in range(4):
-            late_group(g, ((0, 2, 0, 4), (2, 2, 4, 4)), (None, AT_STATES + 8 * KIB, AT_STATES + 12 * KIB, AT_LAST_WORDS + 3 * KIB)[g])
-            if g in (1, 2):
-                add_and_regroup(1 + g)
+            late_group(g, ((0, 2, 0, 4), (2, 2, 4, 4)), (None, AT_STATES + 11 * KIB, None, AT_LAST_WORDS + 3 * KIB)[g])
+        add_and_turn(2, (0, 1))
+        add_and_turn(3, (2, 3))
 
         woven_w4 = at(AT_SECOND, "w4_woven", [P, 2 * N, PACK], BF16)
         for a in range(2):
             weave_on_scalar(woven_w4[:, N * a : N * (a + 1), :], raw_w4[a][:])
         woven_z = at(AT_CTX, "z0_woven", [P, PM, PACK], BF16)
-        weave_on_scalar(woven_z[:], early_rows[:])
+        pairs = turned[:].rearrange("m i u p e -> m (i u p e)").bitcast(F32).rearrange("m (i u p) -> m i u p", u=2, p=P)
+        woven_pairs = woven_z[:].rearrange("p m t -> p (m t)").bitcast(F32).rearrange("p (i m u) -> p i m u", m=P, u=2)
+        for i0 in range(0, PM // P, 2):
+            back = in_bank(i0 // 2, [P, 2, 2, P])
+            for i in range(2):
+                for u in range(2):
+                    nc.tensor.transpose(back[:, i, u, :], pairs[:, i0 + i, u, :], ident[:])
+            nc.scalar.copy(out=woven_pairs[:, i0 : i0 + 2], in_=back[:].rearrange("p i u m -> p i m u"))
         w4_w = at(AT_LAST_WORDS, "w4_w", [P, 2 * N], U32)
         z_w = [at(AT_LAST_WORDS + 4 * KIB, "z_w0", [P, PM], U32), kept("z_w1", [P, PM], U32)]
-        quantize(woven_w4[:], w4_w[:], w4_s[:])
-        quantize(woven_z[:], z_w[0][:], z_s[0][:])
 
         chunks = ((0, 256), (256, 256), (512, 256), (768, 128), (896, 128))
         chunk_banks = ((0, 1), (4, 5), (6, 7), (2,), (3, 0))
@@ -386,6 +397,8 @@ def tile_list_byte_patch_slots_kernel(
 
         for c in range(2):
             weave_chunk(c, fetch_chunk(c), nc.scalar.copy)
+        quantize(woven_w4[:], w4_w[:], w4_s[:])
+        quantize(woven_z[:], z_w[0][:], z_s[0][:])
         finish(0)
         weave_chunk(2, fetch_chunk(2), nc.scalar.copy)
         finish(1)

@@ -26,7 +26,7 @@ HALF = 512
 AT_TABLE = 0
 AT_W2_RAW = (8 * KIB, 12 * KIB, 16 * KIB)
 AT_PICKED = (26 * KIB, 30 * KIB + HALF, 16 * KIB, 20 * KIB)
-AT_W2_WOVEN = (24 * KIB, 26 * KIB, 28 * KIB)
+AT_W2_WOVEN = (24 * KIB, 76 * KIB, 28 * KIB)
 AT_W2_WORDS = (40 * KIB, 41 * KIB, 42 * KIB)
 AT_RELU = 44 * KIB
 AT_SECOND = 52 * KIB
@@ -72,7 +72,7 @@ def tile_list_byte_patch_slots_kernel(
         z_s = [kept(f"z_s{a}", [P, PM], U8) for a in range(2)]
         early_w = [kept("early_w0", [P, GROUP], F32), kept("early_w1", [P, S - GROUP], F32)]
         late_w = kept("late_w", [P, PACK, S], F32)
-        late_states = kept("late_states", [P, PACK * S], F32)
+        late_states = kept("late_states", [P, PACK, S], F32)
         late_ctx = kept("late_ctx", [P, PACK, PM], F32)
         pages = [kept(f"page{t}", [P, T2], F32) for t in range(PACK)]
         ident = kept("ident", [P, P], F32)
@@ -171,8 +171,8 @@ def tile_list_byte_patch_slots_kernel(
                 nc.scalar.activation(out=gate[:], in_=gate[:], func=ACT.Abs)
             nc.gpsimd.tensor_tensor(out=h, in0=h, in1=gate[:], op=ALU.mult)
 
-        def put_state(page, g, state):
-            picks = list2[:, GROUP * g // 16 : GROUP * (g + 1) // 16]
+        def put_state(page, j0, state):
+            picks = list2[:, j0 // 16 : (j0 + state.shape[1]) // 16]
             nc.vector.tensor_copy(out=pages[page][:].indirect(picks), in_=state)
 
         nc.gpsimd.memset(tab_s[:].bitcast(I32), 0)
@@ -219,7 +219,7 @@ def tile_list_byte_patch_slots_kernel(
         turned = at(AT_ROWS, "turned", [P, PM // P, 2, P, 2], BF16)
         picked = {}
 
-        def early_unit(pair, g, states, parts, gate_at, ring):
+        def early_unit(pair, g, states, parts, gate_at, ring, pieces=()):
             first, second = in_bank(g % 2, [P, 2, GROUP]), in_bank(2 + g % 2, [P, 2, GROUP])
             c0 = GROUP * pair
             for i in range(2):
@@ -244,14 +244,17 @@ def tile_list_byte_patch_slots_kernel(
                 ]
                 gate_state(f"gate{pair}_{g}_{i0}", addends, h, gate_at, bank, False)
                 for i in range(i0, i0 + count):
-                    put_state(2 * pair + i, g, states[:, g, i, :])
+                    put_state(2 * pair + i, GROUP * g, states[:, g, i, :])
+                    if i == 0:
+                        for piece in pieces:
+                            quantize_w2(piece)
 
         def fetch_slice(s):
             picked[s] = at(AT_PICKED[s], f"picked{s}", [P, PM], F32)
             nc.vector.tensor_copy(out=picked[s][:], in_=pages[s][:].indirect(list3[:]))
 
         def add_and_turn(s, banks):
-            size = at(AT_STATES + 4 * KIB * s, f"size{s}", [P, PM], F32)
+            size = at(AT_RELU + 4 * KIB * (s % 2), f"size{s}", [P, PM], F32)
             for half, bank in enumerate(banks):
                 cols = slice(HALF * half, HALF * (half + 1))
                 nc.scalar.activation(out=size[:, cols], in_=picked[s][:, cols], func=ACT.Abs)
@@ -269,11 +272,10 @@ def tile_list_byte_patch_slots_kernel(
         early_unit(0, 0, states, ((0, 1), (1, 1)), None, 4)
         gather_table(2 * GROUP, at(AT_W2_RAW[0], "v_w2", [P, BANK], U32), at(AT_W2_RAW[0] + 2 * KIB, "v_s2", [P, BANK], U8))
         raw_w4 = [load_rows(at(AT_TABLE, "w4_raw0", [P, PACK, N], F32), w4[0:BANK, :])]
+        raw_w4.append(load_rows(at(AT_ROWS + 8 * KIB, "w4_raw1", [P, PACK, N], F32), w4[BANK : 2 * BANK, :]))
         load_rows(late_ctx, ctx[BANK : 2 * BANK, :])
         for g in range(1, 4):
-            early_unit(0, g, states, ((0, 2),), {2: AT_W2_WOVEN[1] + KIB, 3: AT_W2_WORDS[1]}.get(g), 4)
-        quantize_w2(1)
-        quantize_w2(2)
+            early_unit(0, g, states, ((0, 2),), {1: AT_W2_WOVEN[1], 2: AT_W2_WOVEN[2], 3: AT_W2_WORDS[1]}.get(g), 4, (1, 2) if g == 3 else ())
         w3_late_s = at(AT_W2_WOVEN[2] + 2 * KIB, "w3_late_s", [P, BANK], U8)
         nc.gpsimd.tensor_copy(
             out=w3_late_s[:].rearrange("p (t m) -> p t m", t=PACK), in_=w3_raw_s[:].rearrange("p (m t) -> p t m", t=PACK)
@@ -283,15 +285,12 @@ def tile_list_byte_patch_slots_kernel(
 
         states = at(AT_STATES + 8 * KIB, "states1", [P, 4, 2, GROUP], F32)
         for g in range(4):
-            early_unit(1, g, states, ((0, 2),), AT_STATES + 3 * KIB if g == 2 else None, 2)
+            early_unit(1, g, states, ((0, 2),), None, 2)
         w3_late_w = at(AT_W2_RAW[1], "w3_late_w", [P, BANK], U32)
         nc.scalar.copy(
             out=w3_late_w[:].rearrange("p (t c i) -> p c t i", t=PACK, i=4),
             in_=w3_raw_w[:].bitcast(U32).rearrange("p (c i t) -> p c t i", t=PACK, i=4),
         )
-        add_and_turn(0, (6, 7))
-        add_and_turn(1, (6, 7))
-        raw_w4.append(load_rows(at(AT_CTX, "w4_raw1", [P, PACK, N], F32), w4[BANK : 2 * BANK, :]))
         fetch_slice(2)
         fetch_slice(3)
 
@@ -308,8 +307,7 @@ def tile_list_byte_patch_slots_kernel(
                 second_at.append(AT_SECOND + 2 * KIB * next_slot("second", 4))
             copied = {}
             for t0, count, c0, c1 in parts:
-                start = PACK * GROUP * g + GROUP * t0
-                h = late_states[:, start : start + GROUP * count].rearrange("p (t j) -> p t j", j=GROUP)
+                h = late_states[:, t0 : t0 + count, GROUP * g : GROUP * (g + 1)]
                 stationary = [(w3_late_w[:, P * t : P * (t + 1)], w3_late_s[:, P * t : P * (t + 1)]) for t in range(t0, t0 + count)]
                 if c1 > c0:
                     for e in range(2):
@@ -321,18 +319,19 @@ def tile_list_byte_patch_slots_kernel(
                 weigh_third(g, stationary, h, late_w[:, t0 : t0 + count, GROUP * g : GROUP * (g + 1)], bank, ACT.Abs)
                 addends = [(relu[e][:, t, :], copied[e, t]) for t in range(t0, t0 + count) for e in range(2)]
                 gate_state(f"late_gate{g}_{t0}", addends, h, last_gate_at if t0 + count == PACK else None, bank, True)
-                for i in range(count):
-                    put_state(t0 + i, g, h[:, i, :])
+                if g % 2 == 1:
+                    for t in range(t0, t0 + count):
+                        put_state(t, GROUP * (g - 1), late_states[:, t, GROUP * (g - 1) : GROUP * (g + 1)])
 
         for g in range(4):
-            late_group(g, ((0, 2, 0, 4), (2, 2, 4, 4)), (None, AT_STATES + 11 * KIB, None, AT_LAST_WORDS + 3 * KIB)[g])
-        add_and_turn(2, (0, 1))
-        add_and_turn(3, (2, 3))
+            late_group(g, ((0, 2, 0, 4), (2, 2, 4, 4)), (None, None, None, AT_LAST_WORDS + 3 * KIB)[g])
+        for s in range(4):
+            add_and_turn(s, (2 * (s % 2), 2 * (s % 2) + 1))
 
         woven_w4 = at(AT_SECOND, "w4_woven", [P, 2 * N, PACK], BF16)
         for a in range(2):
             weave_on_scalar(woven_w4[:, N * a : N * (a + 1), :], raw_w4[a][:])
-        woven_z = at(AT_CTX, "z0_woven", [P, PM, PACK], BF16)
+        woven_z = at(AT_ROWS + 8 * KIB, "z0_woven", [P, PM, PACK], BF16)
         pairs = turned[:].rearrange("m i u p e -> m (i u p e)").bitcast(F32).rearrange("m (i u p) -> m i u p", u=2, p=P)
         woven_pairs = woven_z[:].rearrange("p m t -> p (m t)").bitcast(F32).rearrange("p (i m u) -> p i m u", m=P, u=2)
         for i0 in range(0, PM // P, 2):
@@ -344,7 +343,11 @@ def tile_list_byte_patch_slots_kernel(
         w4_w = at(AT_LAST_WORDS, "w4_w", [P, 2 * N], U32)
         z_w = [at(AT_LAST_WORDS + 4 * KIB, "z_w0", [P, PM], U32), kept("z_w1", [P, PM], U32)]
 
+        quantize(woven_w4[:], w4_w[:], w4_s[:])
+        quantize(woven_z[:], z_w[0][:], z_s[0][:])
         chunks = ((0, 256), (256, 256), (512, 256), (768, 128), (896, 128))
+        fetched_at = (AT_SECOND, AT_SECOND + 4 * KIB, AT_GATE, AT_ROWS, AT_ROWS + 2 * KIB)
+        woven_at = (AT_GATE, AT_ROWS, AT_ROWS + 2 * KIB, AT_ROWS + 4 * KIB, AT_ROWS + 4 * KIB)
         chunk_banks = ((0, 1), (4, 5), (6, 7), (2,), (3, 0))
         out_rows = out.rearrange("(nt p) m -> p nt m", p=P)
         sums, woven_late = {}, {}
@@ -368,7 +371,7 @@ def tile_list_byte_patch_slots_kernel(
 
         def fetch_chunk(c):
             m0, width = chunks[c]
-            z = at(AT_RELU + 4 * KIB * (c % 2), f"z1_{c}", [P, PACK, width], F32)
+            z = at(fetched_at[c], f"z1_{c}", [P, PACK, width], F32)
             for t in range(PACK):
                 nc.vector.tensor_tensor(
                     out=z[:, t, :],
@@ -379,7 +382,7 @@ def tile_list_byte_patch_slots_kernel(
             return z
 
         def weave_chunk(c, z, copy):
-            woven_late[c] = at(AT_ROWS + 8 * min(chunks[c][0], 768), f"z1_woven{c}", [P, chunks[c][1], PACK], BF16)
+            woven_late[c] = at(woven_at[c], f"z1_woven{c}", [P, chunks[c][1], PACK], BF16)
             interleave(copy, woven_late[c][:], z[:])
 
         def finish(c):
@@ -397,8 +400,6 @@ def tile_list_byte_patch_slots_kernel(
 
         for c in range(2):
             weave_chunk(c, fetch_chunk(c), nc.scalar.copy)
-        quantize(woven_w4[:], w4_w[:], w4_s[:])
-        quantize(woven_z[:], z_w[0][:], z_s[0][:])
         finish(0)
         weave_chunk(2, fetch_chunk(2), nc.scalar.copy)
         finish(1)

@@ -35,6 +35,7 @@ AT_STATES = 68 * KIB
 AT_ROWS = 84 * KIB
 AT_CTX = 100 * KIB
 AT_LAST_WORDS = 116 * KIB
+AT_LAST_PAGE = 124 * KIB
 
 
 def tile_list_byte_patch_slots_kernel(
@@ -70,17 +71,17 @@ def tile_list_byte_patch_slots_kernel(
         w2_s = [kept(f"w2_s{i}", [P, width], U8) for i, width in enumerate((GROUP, GROUP, BANK))]
         w4_s = kept("w4_s", [P, 2 * N], U8)
         z_s = [kept(f"z_s{a}", [P, PM], U8) for a in range(2)]
-        early_w = [kept("early_w0", [P, GROUP], F32), kept("early_w1", [P, S - GROUP], F32)]
+        early_w = [kept(f"early_w{i}", [P, HALF], F32) for i in range(2)]
         late_w = kept("late_w", [P, PACK, S], F32)
         late_states = kept("late_states", [P, PACK, S], F32)
         late_ctx = kept("late_ctx", [P, PACK, PM], F32)
-        pages = [kept(f"page{t}", [P, T2], F32) for t in range(PACK)]
+        pages = [kept(f"page{t}", [P, T2], F32) for t in range(PACK - 1)]
         ident = kept("ident", [P, P], F32)
 
-        def load_scales(plane, rows, c0):
+        def load_scales(plane, rows, c0, quadrants=range(4), queue=nc.sync):
             width = plane.shape[1]
-            for q in range(4):
-                nc.sync.dma_start(
+            for q in quadrants:
+                queue.dma_start(
                     out=plane[32 * q : 32 * q + 4, :].bitcast(I32), in_=rows[0, 4 * q : 4 * q + 4, c0 : c0 + width].bitcast(I32)
                 )
 
@@ -102,13 +103,20 @@ def tile_list_byte_patch_slots_kernel(
             for c0 in range(0, woven.shape[1], GROUP):
                 interleave(nc.scalar.copy, woven[:, c0 : c0 + GROUP, :], planes[:, :, c0 : c0 + GROUP])
 
+        def round_on_gpsimd(out, in_):
+            nc.gpsimd.tensor_scalar(out=out, in0=in_, scalar1=1.0, scalar2=0.0, op0=ALU.mult, op1=ALU.add)
+
         def quantize(woven, words, scales):
             nc.vector.quantize_mx(out=words.bitcast(FP8X4), scales=scales, in_=woven.rearrange("p c t -> p (c t)"))
 
         def quantize_w2(i):
             width = w2_s[i].shape[1]
             woven = at(AT_W2_WOVEN[i], f"w2_woven{i}", [P, width, PACK], BF16)
-            weave_on_scalar(woven[:], w2_raw[i][:])
+            if i == 0:
+                interleave(nc.scalar.copy, woven[:, 0:P, :], w2_raw[0][:, :, 0:P])
+                interleave(nc.vector.tensor_copy, woven[:, P:GROUP, :], w2_raw[0][:, :, P:GROUP])
+            else:
+                weave_on_scalar(woven[:], w2_raw[i][:])
             w2_w.append(at(AT_W2_WORDS[i], f"w2_w{i}", [P, width], U32))
             quantize(woven[:], w2_w[i][:], w2_s[i][:])
 
@@ -135,7 +143,7 @@ def tile_list_byte_patch_slots_kernel(
                 stop=True,
             )
 
-        turn = {"relu": 0, "second": 0, "gate": 0, "bank": 0}
+        turn = {"relu": 1, "second": 0, "gate": 0, "bank": 2}
 
         def next_slot(kind, count):
             turn[kind] = turn[kind] + 1
@@ -176,6 +184,7 @@ def tile_list_byte_patch_slots_kernel(
             nc.vector.tensor_copy(out=pages[page][:].indirect(picks), in_=state)
 
         nc.gpsimd.memset(tab_s[:].bitcast(I32), 0)
+        load_scales(w1_s, w1_scales, 0, range(2, 4), nc.gpsimd)
         nc.gpsimd.memset(w3_raw_s[:].bitcast(I32), 0)
         make_identity(nc, ident[:])
         warm = keep.tile([P, 2], F32, name="warm")
@@ -184,19 +193,18 @@ def tile_list_byte_patch_slots_kernel(
         for t in range(2):
             nc.vector.memset(pages[t][:, 0 : S - 1].bitcast(I32), 0)
             nc.vector.memset(pages[t][:, S - 1 : T2].bitcast(I32), 0)
-        for t in range(2, PACK):
-            nc.gpsimd.memset(pages[t][:].bitcast(I32), 0)
+        nc.gpsimd.memset(pages[2][:].bitcast(I32), 0)
         nc.sync.dma_start(list1[:], offs)
         nc.sync.dma_start(out=tab_w[:], in_=tab_words[0].rearrange("p c i -> p (c i)").bitcast(I32))
         load_scales(tab_s, tab_scales, 0)
-        w2_raw = [load_rows(at(AT_W2_RAW[0], "w2_raw0", [P, PACK, GROUP], F32), w2[:, 0:GROUP])]
         load_w1_words(0)
+        w2_raw = [load_rows(at(AT_W2_RAW[0], "w2_raw0", [P, PACK, GROUP], F32), w2[:, 0:GROUP])]
         load_w3_words(w3_early_w[0], 0)
-        load_scales(w1_s, w1_scales, 0)
         load_scales(w3_early_s, w3_scales, 0)
-        nc.sync.dma_start(out=early_w[0][:], in_=wgs[:, 0:GROUP])
+        load_scales(w1_s, w1_scales, 0, range(2))
+        nc.sync.dma_start(out=early_w[0][:], in_=wgs[:, 0:HALF])
         nc.sync.dma_start(list2[:], offs2)
-        nc.sync.dma_start(out=early_w[1][:], in_=wgs[:, GROUP:S])
+        nc.sync.dma_start(out=early_w[1][:], in_=wgs[:, HALF:S])
         load_w3_words(w3_early_w[1], GROUP)
         w2_raw.append(load_rows(at(AT_W2_RAW[1], "w2_raw1", [P, PACK, GROUP], F32), w2[:, GROUP:BANK]))
         w2_raw.append(load_rows(at(AT_W2_RAW[2], "w2_raw2", [P, PACK, BANK], F32), w2[:, BANK : 2 * BANK]))
@@ -219,8 +227,8 @@ def tile_list_byte_patch_slots_kernel(
         turned = at(AT_ROWS, "turned", [P, PM // P, 2, P, 2], BF16)
         picked = {}
 
-        def early_unit(pair, g, states, parts, gate_at, ring, pieces=()):
-            first, second = in_bank(g % 2, [P, 2, GROUP]), in_bank(2 + g % 2, [P, 2, GROUP])
+        def early_unit(pair, g, states, banks, gate_at, pieces=()):
+            first, second = in_bank(banks[0], [P, 2, GROUP]), in_bank(banks[1], [P, 2, GROUP])
             c0 = GROUP * pair
             for i in range(2):
                 token_product(first[:, i, :], 2 * g + i, w1_w[0][:, 2 * c0 : 2 * (c0 + GROUP)].bitcast(FP4X4), w1_s[:, c0 : c0 + GROUP])
@@ -229,29 +237,49 @@ def tile_list_byte_patch_slots_kernel(
             for i in range(2):
                 token_product(second[:, i, :], 2 * g + i, w2_w[pair][:].bitcast(FP8X4), w2_s[pair][:])
             second_at = AT_SECOND + 2 * KIB * next_slot("second", 4)
-            weights = early_w[0][:] if g == 0 else early_w[1][:, GROUP * (g - 1) : GROUP * g]
-            for i0, count in parts:
+            weights = early_w[g // 2][:, GROUP * (g % 2) : GROUP * (g % 2 + 1)]
+            for i0, count in ((0, 2),):
                 h = states[:, g, i0 : i0 + count, :]
                 stationary = [
                     (w3_early_w[pair][:, P * i : P * (i + 1)], w3_early_s[:, c0 + P * i : c0 + P * (i + 1)]) for i in range(i0, i0 + count)
                 ]
-                bank = 4 + next_slot("bank", ring)
-                weigh_third(g, stationary, h, weights.unsqueeze(1).to_broadcast([P, count, GROUP]), bank, ACT.Copy)
-                copied = at(AT_W2_RAW[0] + 2 * KIB if (pair, g, i0) == (0, 0, 0) else second_at + KIB * i0, f"second{pair}_{g}_{i0}", [P, 2, P * count], F32)
+                weigh_third(g, stationary, h, weights.unsqueeze(1).to_broadcast([P, count, GROUP]), banks[2], ACT.Copy)
+                copied = at(second_at + KIB * i0, f"second{pair}_{g}_{i0}", [P, 2, P * count], F32)
                 nc.scalar.copy(out=copied[:], in_=second[:, :, P * i0 : P * (i0 + count)])
                 addends = [
                     (relu[:, e, P * (i0 + i) : P * (i0 + i + 1)], copied[:, e, P * i : P * (i + 1)]) for i in range(count) for e in range(2)
                 ]
-                gate_state(f"gate{pair}_{g}_{i0}", addends, h, gate_at, bank, False)
+                gate_state(f"gate{pair}_{g}_{i0}", addends, h, gate_at, banks[3], False)
                 for i in range(i0, i0 + count):
-                    put_state(2 * pair + i, GROUP * g, states[:, g, i, :])
+                    put_state(i, GROUP * g, states[:, g, i, :])
                     if i == 0:
                         for piece in pieces:
                             quantize_w2(piece)
 
+        def opening_slice(i, h):
+            cols = slice(P * i, P * (i + 1))
+            sums = []
+            for bank, words, scales in (
+                (i, w1_w[0][:, 2 * P * i : 2 * P * (i + 1)].bitcast(FP4X4), w1_s[:, cols]),
+                (2 + i, w2_w[0][:, cols].bitcast(FP8X4), w2_s[0][:, cols]),
+            ):
+                acc = in_bank(bank, [P, GROUP])
+                nc.tensor.matmul_mx(
+                    out=acc[:], lhsT=words, lhsT_scale=scales, rhs=v_w[0].bitcast(FP8X4), rhs_scale=v_s[0], start=True, stop=True
+                )
+                sums.append(acc)
+            relu = at(AT_W2_RAW[0] + 2 * KIB if i == 1 else AT_RELU, f"opening_relu{i}", [P, GROUP], F32)
+            nc.scalar.activation(out=relu[:], in_=sums[0][:], func=ACT.Relu)
+            gate = at(AT_GATE + 2 * KIB * next_slot("gate", 4), f"opening_gate{i}", [P, 1, GROUP], F32)
+            nc.vector.tensor_tensor(out=gate[:, 0, :], in0=sums[1][:], in1=relu[:], op=ALU.add)
+            weigh_third(0, [(w3_early_w[0][:, cols], w3_early_s[:, cols])], h, early_w[0][:, 0:GROUP].unsqueeze(1), 4 + i, ACT.Copy)
+            nc.scalar.activation(out=gate[:], in_=gate[:], func=ACT.Silu)
+            nc.gpsimd.tensor_tensor(out=h, in0=h, in1=gate[:], op=ALU.mult)
+            put_state(i, 0, h[:, 0, :])
+
         def fetch_slice(s):
             picked[s] = at(AT_PICKED[s], f"picked{s}", [P, PM], F32)
-            nc.vector.tensor_copy(out=picked[s][:], in_=pages[s][:].indirect(list3[:]))
+            nc.vector.tensor_copy(out=picked[s][:], in_=pages[s % 2][:].indirect(list3[:]))
 
         def add_and_turn(s, banks):
             size = at(AT_RELU + 4 * KIB * (s % 2), f"size{s}", [P, PM], F32)
@@ -269,13 +297,16 @@ def tile_list_byte_patch_slots_kernel(
                 )
 
         states = at(AT_STATES, "states0", [P, 4, 2, GROUP], F32)
-        early_unit(0, 0, states, ((0, 1), (1, 1)), None, 4)
+        for i in range(2):
+            opening_slice(i, states[:, 0, i : i + 1, :])
         gather_table(2 * GROUP, at(AT_W2_RAW[0], "v_w2", [P, BANK], U32), at(AT_W2_RAW[0] + 2 * KIB, "v_s2", [P, BANK], U8))
         raw_w4 = [load_rows(at(AT_TABLE, "w4_raw0", [P, PACK, N], F32), w4[0:BANK, :])]
         raw_w4.append(load_rows(at(AT_ROWS + 8 * KIB, "w4_raw1", [P, PACK, N], F32), w4[BANK : 2 * BANK, :]))
         load_rows(late_ctx, ctx[BANK : 2 * BANK, :])
         for g in range(1, 4):
-            early_unit(0, g, states, ((0, 2),), {1: AT_W2_WOVEN[1], 2: AT_W2_WOVEN[2], 3: AT_W2_WORDS[1]}.get(g), 4, (1, 2) if g == 3 else ())
+            banks = {1: (6, 7, 2, 4), 2: (0, 1, 4, 6), 3: (7, 3, 6, 5)}[g]
+            gate_at = {1: AT_W2_WOVEN[1], 2: AT_W2_WOVEN[2], 3: AT_W2_WORDS[1]}[g]
+            early_unit(0, g, states, banks, gate_at, (1, 2) if g == 3 else ())
         w3_late_s = at(AT_W2_WOVEN[2] + 2 * KIB, "w3_late_s", [P, BANK], U8)
         nc.gpsimd.tensor_copy(
             out=w3_late_s[:].rearrange("p (t m) -> p t m", t=PACK), in_=w3_raw_s[:].rearrange("p (m t) -> p t m", t=PACK)
@@ -285,7 +316,7 @@ def tile_list_byte_patch_slots_kernel(
 
         states = at(AT_STATES + 8 * KIB, "states1", [P, 4, 2, GROUP], F32)
         for g in range(4):
-            early_unit(1, g, states, ((0, 2),), None, 2)
+            early_unit(1, g, states, (g % 2, 2 + g % 2, 4 + g % 2, 4 + g % 2), None)
         w3_late_w = at(AT_W2_RAW[1], "w3_late_w", [P, BANK], U32)
         nc.scalar.copy(
             out=w3_late_w[:].rearrange("p (t c i) -> p c t i", t=PACK, i=4),
@@ -294,7 +325,7 @@ def tile_list_byte_patch_slots_kernel(
         fetch_slice(2)
         fetch_slice(3)
 
-        def late_group(g, parts, last_gate_at):
+        def late_group(g, parts, gates_at):
             relu, second, second_at = [], [], []
             for e in range(2):
                 first = in_bank(e, [P, BANK])
@@ -318,20 +349,23 @@ def tile_list_byte_patch_slots_kernel(
                 bank = 4 + next_slot("bank", 4)
                 weigh_third(g, stationary, h, late_w[:, t0 : t0 + count, GROUP * g : GROUP * (g + 1)], bank, ACT.Abs)
                 addends = [(relu[e][:, t, :], copied[e, t]) for t in range(t0, t0 + count) for e in range(2)]
-                gate_state(f"late_gate{g}_{t0}", addends, h, last_gate_at if t0 + count == PACK else None, bank, True)
+                gate_state(f"late_gate{g}_{t0}", addends, h, gates_at[t0 // 2], bank, True)
+                if (g, t0) == (1, 0):
+                    pages.append(at(AT_LAST_PAGE, "page3", [P, T2], F32))
+                    nc.gpsimd.memset(pages[3][:].bitcast(I32), 0)
                 if g % 2 == 1:
                     for t in range(t0, t0 + count):
                         put_state(t, GROUP * (g - 1), late_states[:, t, GROUP * (g - 1) : GROUP * (g + 1)])
 
         for g in range(4):
-            late_group(g, ((0, 2, 0, 4), (2, 2, 4, 4)), (None, None, None, AT_LAST_WORDS + 3 * KIB)[g])
+            late_group(g, ((0, 2, 0, 4), (2, 2, 4, 4)), (AT_LAST_PAGE if g == 1 else None, AT_STATES if g == 3 else None))
         for s in range(4):
             add_and_turn(s, (2 * (s % 2), 2 * (s % 2) + 1))
 
-        woven_w4 = at(AT_SECOND, "w4_woven", [P, 2 * N, PACK], BF16)
-        for a in range(2):
-            weave_on_scalar(woven_w4[:, N * a : N * (a + 1), :], raw_w4[a][:])
-        woven_z = at(AT_ROWS + 8 * KIB, "z0_woven", [P, PM, PACK], BF16)
+        woven_w4 = at(AT_STATES, "w4_woven", [P, 2 * N, PACK], BF16)
+        interleave(round_on_gpsimd, woven_w4[:, 0:N, :], raw_w4[0][:])
+        weave_on_scalar(woven_w4[:, N : 2 * N, :], raw_w4[1][:])
+        woven_z = at(AT_SECOND, "z0_woven", [P, PM, PACK], BF16)
         pairs = turned[:].rearrange("m i u p e -> m (i u p e)").bitcast(F32).rearrange("m (i u p) -> m i u p", u=2, p=P)
         woven_pairs = woven_z[:].rearrange("p m t -> p (m t)").bitcast(F32).rearrange("p (i m u) -> p i m u", m=P, u=2)
         for i0 in range(0, PM // P, 2):
@@ -341,12 +375,12 @@ def tile_list_byte_patch_slots_kernel(
                     nc.tensor.transpose(back[:, i, u, :], pairs[:, i0 + i, u, :], ident[:])
             nc.scalar.copy(out=woven_pairs[:, i0 : i0 + 2], in_=back[:].rearrange("p i u m -> p i m u"))
         w4_w = at(AT_LAST_WORDS, "w4_w", [P, 2 * N], U32)
-        z_w = [at(AT_LAST_WORDS + 4 * KIB, "z_w0", [P, PM], U32), kept("z_w1", [P, PM], U32)]
+        z_w = [at(AT_TABLE, "z_w0", [P, PM], U32), kept("z_w1", [P, PM], U32)]
 
-        quantize(woven_w4[:], w4_w[:], w4_s[:])
         quantize(woven_z[:], z_w[0][:], z_s[0][:])
+        quantize(woven_w4[:], w4_w[:], w4_s[:])
         chunks = ((0, 256), (256, 256), (512, 256), (768, 128), (896, 128))
-        fetched_at = (AT_SECOND, AT_SECOND + 4 * KIB, AT_GATE, AT_ROWS, AT_ROWS + 2 * KIB)
+        fetched_at = (AT_STATES, AT_STATES + 4 * KIB, AT_GATE, AT_ROWS, AT_ROWS + 2 * KIB)
         woven_at = (AT_GATE, AT_ROWS, AT_ROWS + 2 * KIB, AT_ROWS + 4 * KIB, AT_ROWS + 4 * KIB)
         chunk_banks = ((0, 1), (4, 5), (6, 7), (2,), (3, 0))
         out_rows = out.rearrange("(nt p) m -> p nt m", p=P)

@@ -25,17 +25,22 @@ KIB = 1024
 HALF = 512
 AT_TABLE = 0
 AT_W2_RAW = (8 * KIB, 12 * KIB, 16 * KIB)
-AT_PICKED = (26 * KIB, 30 * KIB + HALF, 16 * KIB, 20 * KIB)
-AT_W2_WOVEN = (24 * KIB, 76 * KIB, 28 * KIB)
-AT_W2_WORDS = (40 * KIB, 41 * KIB, 42 * KIB)
-AT_RELU = 44 * KIB
-AT_SECOND = 52 * KIB
-AT_GATE = 60 * KIB
-AT_STATES = 68 * KIB
-AT_ROWS = 84 * KIB
-AT_CTX = 100 * KIB
-AT_LAST_WORDS = 116 * KIB
-AT_LAST_PAGE = 124 * KIB
+AT_FIRST_W = 24 * KIB
+AT_PAGE2 = 26 * KIB
+AT_W2_WORDS = (34 * KIB, 35 * KIB, 37 * KIB)
+AT_PICKED = (92 * KIB, 8 * KIB, 16 * KIB, 12 * KIB)
+AT_W2_WOVEN = (AT_PAGE2, 44 * KIB, 48 * KIB)
+AT_W3_LATE_S = AT_W2_WOVEN[1] + 768
+AT_HELD_STATES = (AT_W3_LATE_S - 2 * KIB, AT_W3_LATE_S + HALF, AT_W2_WOVEN[2], 41 * KIB)
+AT_W3_LATE_W = 39 * KIB
+AT_PAGE3 = 52 * KIB
+AT_RELU = 60 * KIB
+AT_SECOND = 68 * KIB
+AT_GATE = 76 * KIB
+AT_STATES = 84 * KIB
+AT_ROWS = 100 * KIB
+AT_CTX = 116 * KIB
+AT_LAST_WORDS = 132 * KIB
 
 
 def tile_list_byte_patch_slots_kernel(
@@ -61,21 +66,22 @@ def tile_list_byte_patch_slots_kernel(
         list3 = keep.tile([P, PM // 16], U16, name="list3")
         tab_w = at(AT_TABLE, "tab_w", [P, T], I32)
         tab_s = kept("tab_s", [P, T], U8)
+        v_s = kept("v_s", [P, S], U8)
         w1_w = [kept(f"w1_w{a}", [P, 2 * BANK], U8) for a in range(2)]
         w1_s = kept("w1_s", [P, H], U8)
         w3_early_w = [kept(f"w3_early_w{h}", [P, GROUP], I32) for h in range(2)]
         w3_early_s = kept("w3_early_s", [P, BANK], U8)
         w3_raw_w = kept("w3_raw_w", [P, BANK], I32)
         w3_raw_s = kept("w3_raw_s", [P, BANK], U8)
-        w2_w = []
         w2_s = [kept(f"w2_s{i}", [P, width], U8) for i, width in enumerate((GROUP, GROUP, BANK))]
         w4_s = kept("w4_s", [P, 2 * N], U8)
         z_s = [kept(f"z_s{a}", [P, PM], U8) for a in range(2)]
+        first_w = at(AT_FIRST_W, "first_w", [P, GROUP], F32)
         early_w = [kept(f"early_w{i}", [P, HALF], F32) for i in range(2)]
         late_w = kept("late_w", [P, PACK, S], F32)
         late_states = kept("late_states", [P, PACK, S], F32)
         late_ctx = kept("late_ctx", [P, PACK, PM], F32)
-        pages = [kept(f"page{t}", [P, T2], F32) for t in range(PACK - 1)]
+        pages = [kept(f"page{t}", [P, T2], F32) for t in range(2)]
         ident = kept("ident", [P, P], F32)
 
         def load_scales(plane, rows, c0, quadrants=range(4), queue=nc.sync):
@@ -99,9 +105,9 @@ def tile_list_byte_patch_slots_kernel(
         def interleave(copy, woven, planes):
             copy(out=woven.rearrange("p (c i) t -> p c t i", i=4), in_=planes.rearrange("p t (c i) -> p c t i", i=4))
 
-        def weave_on_scalar(woven, planes):
-            for c0 in range(0, woven.shape[1], GROUP):
-                interleave(nc.scalar.copy, woven[:, c0 : c0 + GROUP, :], planes[:, :, c0 : c0 + GROUP])
+        def weave_on_scalar(woven, planes, step=GROUP):
+            for c0 in range(0, woven.shape[1], step):
+                interleave(nc.scalar.copy, woven[:, c0 : c0 + step, :], planes[:, :, c0 : c0 + step])
 
         def round_on_gpsimd(out, in_):
             nc.gpsimd.tensor_scalar(out=out, in0=in_, scalar1=1.0, scalar2=0.0, op0=ALU.mult, op1=ALU.add)
@@ -109,60 +115,47 @@ def tile_list_byte_patch_slots_kernel(
         def quantize(woven, words, scales):
             nc.vector.quantize_mx(out=words.bitcast(FP8X4), scales=scales, in_=woven.rearrange("p c t -> p (c t)"))
 
+        w2_woven, w2_w, v_w = {}, {}, {}
+
+        def weave_w2(i):
+            w2_woven[i] = at(AT_W2_WOVEN[i], f"w2_woven{i}", [P, w2_s[i].shape[1], PACK], BF16)
+            weave_on_scalar(w2_woven[i][:], w2_raw[i][:], P if i > 0 else GROUP)
+
         def quantize_w2(i):
-            width = w2_s[i].shape[1]
-            woven = at(AT_W2_WOVEN[i], f"w2_woven{i}", [P, width, PACK], BF16)
-            if i == 0:
-                interleave(nc.scalar.copy, woven[:, 0:P, :], w2_raw[0][:, :, 0:P])
-                interleave(nc.vector.tensor_copy, woven[:, P:GROUP, :], w2_raw[0][:, :, P:GROUP])
-            else:
-                weave_on_scalar(woven[:], w2_raw[i][:])
-            w2_w.append(at(AT_W2_WORDS[i], f"w2_w{i}", [P, width], U32))
-            quantize(woven[:], w2_w[i][:], w2_s[i][:])
+            w2_w[i] = at(AT_W2_WORDS[i], f"w2_w{i}", [P, w2_s[i].shape[1]], U32)
+            quantize(w2_woven[i][:], w2_w[i][:], w2_s[i][:])
 
-        v_w, v_s = {}, {}
-
-        def gather_table(j0, words, scales):
+        def gather_words(j0, words):
             width = words.shape[1]
-            picks = list1[:, j0 // 16 : (j0 + width) // 16]
-            nc.vector.tensor_copy(out=words[:], in_=tab_w[:].bitcast(U32).indirect(picks))
-            nc.vector.tensor_copy(out=scales[:], in_=tab_s[:].indirect(picks))
+            nc.vector.tensor_copy(out=words[:], in_=tab_w[:].bitcast(U32).indirect(list1[:, j0 // 16 : (j0 + width) // 16]))
             for c0 in range(0, width, GROUP):
                 v_w[(j0 + c0) // GROUP] = words[:, c0 : c0 + GROUP]
-                v_s[(j0 + c0) // GROUP] = scales[:, c0 : c0 + GROUP]
 
-        def token_product(acc, e, words, scales):
-            g, cols = e // 2, slice(P * (e % 2), P * (e % 2 + 1))
+        def product(acc, lhs_words, lhs_scales, rhs_words, rhs_scales):
             nc.tensor.matmul_mx(
-                out=acc,
-                lhsT=v_w[g][:, cols].bitcast(FP8X4),
-                lhsT_scale=v_s[g][:, cols],
-                rhs=words,
-                rhs_scale=scales,
-                start=True,
-                stop=True,
+                out=acc, lhsT=lhs_words, lhsT_scale=lhs_scales, rhs=rhs_words, rhs_scale=rhs_scales, start=True, stop=True
             )
 
-        turn = {"relu": 1, "second": 0, "gate": 0, "bank": 2}
+        def token_product(acc, e, words, scales):
+            cols = slice(P * (e % 2), P * (e % 2 + 1))
+            product(acc, v_w[e // 2][:, cols].bitcast(FP8X4), v_s[:, P * e : P * (e + 1)], words, scales)
+
+        def row_product(acc, g, words, scales):
+            product(acc, words, scales, v_w[g].bitcast(FP8X4), v_s[:, GROUP * g : GROUP * (g + 1)])
+
+        turn = {"relu": 1, "second": 1, "gate": 0, "bank": 2}
 
         def next_slot(kind, count):
             turn[kind] = turn[kind] + 1
             return (turn[kind] - 1) % count
 
-        def weigh_third(g, stationary, h, weights, bank, func):
+        def weigh_third(g, stationary, h, weights, bank, func, plain=None):
             third = in_bank(bank, [P, len(stationary), GROUP])
             for i, (words, scales) in enumerate(stationary):
-                nc.tensor.matmul_mx(
-                    out=third[:, i, :],
-                    lhsT=words.bitcast(FP8X4),
-                    lhsT_scale=scales,
-                    rhs=v_w[g].bitcast(FP8X4),
-                    rhs_scale=v_s[g],
-                    start=True,
-                    stop=True,
-                )
-            nc.scalar.activation(out=h, in_=third[:], func=func)
-            nc.gpsimd.tensor_tensor(out=h, in0=h, in1=weights, op=ALU.mult)
+                row_product(third[:, i, :], g, words.bitcast(FP8X4), scales)
+            plain = h if plain is None else plain
+            nc.scalar.activation(out=plain, in_=third[:], func=func)
+            nc.gpsimd.tensor_tensor(out=h, in0=plain, in1=weights, op=ALU.mult)
 
         def gate_state(name, addends, h, gate_at, bank, absolute):
             count = len(addends) // 2
@@ -183,33 +176,35 @@ def tile_list_byte_patch_slots_kernel(
             picks = list2[:, j0 // 16 : (j0 + state.shape[1]) // 16]
             nc.vector.tensor_copy(out=pages[page][:].indirect(picks), in_=state)
 
-        nc.gpsimd.memset(tab_s[:].bitcast(I32), 0)
-        load_scales(w1_s, w1_scales, 0, range(2, 4), nc.gpsimd)
-        nc.gpsimd.memset(w3_raw_s[:].bitcast(I32), 0)
+        load_scales(w3_early_s, w3_scales, 0, range(1, 4), nc.gpsimd)
+        nc.gpsimd.memset(pages[1][:].bitcast(I32), 0)
         make_identity(nc, ident[:])
+        nc.gpsimd.memset(w3_raw_s[:].bitcast(I32), 0)
         warm = keep.tile([P, 2], F32, name="warm")
         nc.vector.memset(warm[:, 0:1], 0.0)
         nc.scalar.activation(out=warm[:, 1:2], in_=warm[:, 0:1], func=ACT.Silu)
-        for t in range(2):
-            nc.vector.memset(pages[t][:, 0 : S - 1].bitcast(I32), 0)
-            nc.vector.memset(pages[t][:, S - 1 : T2].bitcast(I32), 0)
-        nc.gpsimd.memset(pages[2][:].bitcast(I32), 0)
+        nc.vector.memset(pages[0][:, 0 : S - 1].bitcast(I32), 0)
+        nc.vector.memset(pages[0][:, S - 1 : T2].bitcast(I32), 0)
         nc.sync.dma_start(list1[:], offs)
-        nc.sync.dma_start(out=tab_w[:], in_=tab_words[0].rearrange("p c i -> p (c i)").bitcast(I32))
-        load_scales(tab_s, tab_scales, 0)
-        load_w1_words(0)
+        for q in range(4):
+            rows = tab_scales[0, 4 * q : 4 * q + 4, :].bitcast(I32)
+            nc.sync.dma_start(out=tab_s[32 * q : 32 * q + 32, :].bitcast(I32), in_=rows.unsqueeze(0).to_broadcast([8, 4, T // 4]))
         w2_raw = [load_rows(at(AT_W2_RAW[0], "w2_raw0", [P, PACK, GROUP], F32), w2[:, 0:GROUP])]
+        load_scales(w1_s, w1_scales, 0, range(1))
+        nc.sync.dma_start(out=tab_w[:], in_=tab_words[0].rearrange("p c i -> p (c i)").bitcast(I32))
+        load_w1_words(0)
+        load_scales(w1_s, w1_scales, 0, range(1, 4))
         load_w3_words(w3_early_w[0], 0)
-        load_scales(w3_early_s, w3_scales, 0)
-        load_scales(w1_s, w1_scales, 0, range(2))
-        nc.sync.dma_start(out=early_w[0][:], in_=wgs[:, 0:HALF])
+        load_scales(w3_early_s, w3_scales, 0, range(1))
+        nc.sync.dma_start(out=first_w[:], in_=wgs[:, 0:GROUP])
         nc.sync.dma_start(list2[:], offs2)
+        nc.sync.dma_start(out=early_w[0][:], in_=wgs[:, 0:HALF])
+        w2_raw.append(load_rows(at(AT_W2_RAW[1], "w2_raw1", [P, PACK, GROUP], F32), w2[:, GROUP:BANK]))
         nc.sync.dma_start(out=early_w[1][:], in_=wgs[:, HALF:S])
         load_w3_words(w3_early_w[1], GROUP)
-        w2_raw.append(load_rows(at(AT_W2_RAW[1], "w2_raw1", [P, PACK, GROUP], F32), w2[:, GROUP:BANK]))
-        w2_raw.append(load_rows(at(AT_W2_RAW[2], "w2_raw2", [P, PACK, BANK], F32), w2[:, BANK : 2 * BANK]))
         nc.sync.dma_start(list3[:], offs3)
         load_scales(w3_raw_s, w3_scales, BANK)
+        w2_raw.append(load_rows(at(AT_W2_RAW[2], "w2_raw2", [P, PACK, BANK], F32), w2[:, BANK : 2 * BANK]))
         load_w3_words(w3_raw_w, BANK)
         early_ctx = [at(AT_CTX + 4 * KIB * s, f"early_ctx{s}", [P, PM], F32) for s in range(4)]
         for s in range(2):
@@ -220,14 +215,34 @@ def tile_list_byte_patch_slots_kernel(
         for s in range(2, 4):
             nc.sync.dma_start(out=early_ctx[s][:], in_=ctx[P * s : P * (s + 1), :])
 
-        gather_table(0, kept("v_w0", [P, GROUP], U32), kept("v_s0", [P, GROUP], U8))
+        nc.vector.tensor_copy(out=v_s[:], in_=tab_s[:].indirect(list1[:]))
+        weave_w2(0)
         quantize_w2(0)
-        gather_table(GROUP, kept("v_w1", [P, GROUP], U32), at(AT_W2_RAW[0] + 3 * KIB, "v_s1", [P, GROUP], U8))
+        pages.append(at(AT_PAGE2, "page2", [P, T2], F32))
+        nc.gpsimd.memset(pages[2][:].bitcast(I32), 0)
+        for g in range(3):
+            gather_words(GROUP * g, kept(f"v_w{g}", [P, GROUP], U32))
 
         turned = at(AT_ROWS, "turned", [P, PM // P, 2, P, 2], BF16)
         picked = {}
 
-        def early_unit(pair, g, states, banks, gate_at, pieces=()):
+        def opening_slice(i, h, banks):
+            cols = slice(P * i, P * (i + 1))
+            first = in_bank(banks[0], [P, GROUP])
+            row_product(first[:], 0, w1_w[0][:, 2 * P * i : 2 * P * (i + 1)].bitcast(FP4X4), w1_s[:, cols])
+            relu = at(AT_RELU + KIB * i, f"opening_relu{i}", [P, GROUP], F32)
+            nc.scalar.activation(out=relu[:], in_=first[:], func=ACT.Relu)
+            second = in_bank(banks[1], [P, GROUP])
+            row_product(second[:], 0, w2_w[0][:, cols].bitcast(FP8X4), w2_s[0][:, cols])
+            gate = at(AT_GATE + 2 * KIB * next_slot("gate", 4), f"opening_gate{i}", [P, GROUP], F32)
+            nc.vector.tensor_tensor(out=gate[:], in0=second[:], in1=relu[:], op=ALU.add)
+            nc.scalar.activation(out=gate[:], in_=gate[:], func=ACT.Silu)
+            third = in_bank(banks[2], [P, GROUP])
+            row_product(third[:], 0, w3_early_w[0][:, cols].bitcast(FP8X4), w3_early_s[:, cols])
+            nc.vector.tensor_tensor(out=h, in0=third[:], in1=first_w[:], op=ALU.mult)
+            nc.gpsimd.tensor_tensor(out=h, in0=h, in1=gate[:], op=ALU.mult)
+
+        def early_unit(pair, g, states, banks):
             first, second = in_bank(banks[0], [P, 2, GROUP]), in_bank(banks[1], [P, 2, GROUP])
             c0 = GROUP * pair
             for i in range(2):
@@ -237,52 +252,31 @@ def tile_list_byte_patch_slots_kernel(
             for i in range(2):
                 token_product(second[:, i, :], 2 * g + i, w2_w[pair][:].bitcast(FP8X4), w2_s[pair][:])
             second_at = AT_SECOND + 2 * KIB * next_slot("second", 4)
+            gate_at = {(0, 3): AT_W2_WORDS[1], (1, 1): AT_W2_WORDS[2], (1, 2): AT_W3_LATE_W + KIB, (1, 3): AT_PAGE3}.get((pair, g))
+            copied = at(AT_W2_WOVEN[g - 1] if pair == 0 and g > 1 else second_at, f"second{pair}_{g}", [P, 2, GROUP], F32)
+            nc.scalar.copy(out=copied[:], in_=second[:])
             weights = early_w[g // 2][:, GROUP * (g % 2) : GROUP * (g % 2 + 1)]
-            for i0, count in ((0, 2),):
-                h = states[:, g, i0 : i0 + count, :]
-                stationary = [
-                    (w3_early_w[pair][:, P * i : P * (i + 1)], w3_early_s[:, c0 + P * i : c0 + P * (i + 1)]) for i in range(i0, i0 + count)
-                ]
-                weigh_third(g, stationary, h, weights.unsqueeze(1).to_broadcast([P, count, GROUP]), banks[2], ACT.Copy)
-                copied = at(second_at + KIB * i0, f"second{pair}_{g}_{i0}", [P, 2, P * count], F32)
-                nc.scalar.copy(out=copied[:], in_=second[:, :, P * i0 : P * (i0 + count)])
-                addends = [
-                    (relu[:, e, P * (i0 + i) : P * (i0 + i + 1)], copied[:, e, P * i : P * (i + 1)]) for i in range(count) for e in range(2)
-                ]
-                gate_state(f"gate{pair}_{g}_{i0}", addends, h, gate_at, banks[3], False)
-                for i in range(i0, i0 + count):
-                    put_state(i, GROUP * g, states[:, g, i, :])
-                    if i == 0:
-                        for piece in pieces:
-                            quantize_w2(piece)
+            stationary = [(w3_early_w[pair][:, P * i : P * (i + 1)], w3_early_s[:, c0 + P * i : c0 + P * (i + 1)]) for i in range(2)]
+            plain = at(AT_STATES + 2 * KIB * (4 + g), f"third{g}", [P, 2, GROUP], F32)[:] if pair == 1 and g > 1 else None
+            weigh_third(g, stationary, states[:], weights.unsqueeze(1).to_broadcast([P, 2, GROUP]), banks[2], ACT.Copy, plain)
+            addends = [(relu[:, e, P * i : P * (i + 1)], copied[:, e, P * i : P * (i + 1)]) for i in range(2) for e in range(2)]
+            gate_state(f"gate{pair}_{g}", addends, states[:], gate_at, banks[3], False)
+            if pair == 0 and g > 1:
+                weave_w2(g - 1)
+            if (pair, g) in ((0, 3), (1, 1)):
+                quantize_w2(pair + 1)
+            put_unit(g, states)
 
-        def opening_slice(i, h):
-            cols = slice(P * i, P * (i + 1))
-            sums = []
-            for bank, words, scales in (
-                (i, w1_w[0][:, 2 * P * i : 2 * P * (i + 1)].bitcast(FP4X4), w1_s[:, cols]),
-                (2 + i, w2_w[0][:, cols].bitcast(FP8X4), w2_s[0][:, cols]),
-            ):
-                acc = in_bank(bank, [P, GROUP])
-                nc.tensor.matmul_mx(
-                    out=acc[:], lhsT=words, lhsT_scale=scales, rhs=v_w[0].bitcast(FP8X4), rhs_scale=v_s[0], start=True, stop=True
-                )
-                sums.append(acc)
-            relu = at(AT_W2_RAW[0] + 2 * KIB if i == 1 else AT_RELU, f"opening_relu{i}", [P, GROUP], F32)
-            nc.scalar.activation(out=relu[:], in_=sums[0][:], func=ACT.Relu)
-            gate = at(AT_GATE + 2 * KIB * next_slot("gate", 4), f"opening_gate{i}", [P, 1, GROUP], F32)
-            nc.vector.tensor_tensor(out=gate[:, 0, :], in0=sums[1][:], in1=relu[:], op=ALU.add)
-            weigh_third(0, [(w3_early_w[0][:, cols], w3_early_s[:, cols])], h, early_w[0][:, 0:GROUP].unsqueeze(1), 4 + i, ACT.Copy)
-            nc.scalar.activation(out=gate[:], in_=gate[:], func=ACT.Silu)
-            nc.gpsimd.tensor_tensor(out=h, in0=h, in1=gate[:], op=ALU.mult)
-            put_state(i, 0, h[:, 0, :])
+        def put_unit(g, states):
+            for i in range(2):
+                put_state(i, GROUP * g, states[:, i, :])
 
         def fetch_slice(s):
             picked[s] = at(AT_PICKED[s], f"picked{s}", [P, PM], F32)
             nc.vector.tensor_copy(out=picked[s][:], in_=pages[s % 2][:].indirect(list3[:]))
 
-        def add_and_turn(s, banks):
-            size = at(AT_RELU + 4 * KIB * (s % 2), f"size{s}", [P, PM], F32)
+        def add_and_turn(s, size_at, banks):
+            size = at(size_at, f"size{s}", [P, PM], F32)
             for half, bank in enumerate(banks):
                 cols = slice(HALF * half, HALF * (half + 1))
                 nc.scalar.activation(out=size[:, cols], in_=picked[s][:, cols], func=ACT.Abs)
@@ -296,71 +290,68 @@ def tile_list_byte_patch_slots_kernel(
                     in_=total[:].rearrange("m i (q u e) -> m i u q e", u=2, e=2),
                 )
 
-        states = at(AT_STATES, "states0", [P, 4, 2, GROUP], F32)
-        for i in range(2):
-            opening_slice(i, states[:, 0, i : i + 1, :])
-        gather_table(2 * GROUP, at(AT_W2_RAW[0], "v_w2", [P, BANK], U32), at(AT_W2_RAW[0] + 2 * KIB, "v_s2", [P, BANK], U8))
+        states = at(AT_STATES, "states0_0", [P, 2, GROUP], F32)
+        for i, banks in enumerate(((0, 1, 2), (3, 0, 4))):
+            opening_slice(i, states[:, i, :], banks)
+        gather_words(3 * GROUP, at(AT_FIRST_W, "v_w3", [P, GROUP], U32))
+        put_unit(0, states)
         raw_w4 = [load_rows(at(AT_TABLE, "w4_raw0", [P, PACK, N], F32), w4[0:BANK, :])]
         raw_w4.append(load_rows(at(AT_ROWS + 8 * KIB, "w4_raw1", [P, PACK, N], F32), w4[BANK : 2 * BANK, :]))
         load_rows(late_ctx, ctx[BANK : 2 * BANK, :])
         for g in range(1, 4):
-            banks = {1: (6, 7, 2, 4), 2: (0, 1, 4, 6), 3: (7, 3, 6, 5)}[g]
-            gate_at = {1: AT_W2_WOVEN[1], 2: AT_W2_WOVEN[2], 3: AT_W2_WORDS[1]}[g]
-            early_unit(0, g, states, banks, gate_at, (1, 2) if g == 3 else ())
-        w3_late_s = at(AT_W2_WOVEN[2] + 2 * KIB, "w3_late_s", [P, BANK], U8)
+            banks = {1: (5, 2, 1, 4), 2: (1, 2, 4, 3), 3: (2, 1, 4, 5)}[g]
+            states = at(AT_STATES + 2 * KIB * g, f"states0_{g}", [P, 2, GROUP], F32)
+            early_unit(0, g, states, banks)
+        w3_late_s = at(AT_W3_LATE_S, "w3_late_s", [P, BANK], U8)
         nc.gpsimd.tensor_copy(
             out=w3_late_s[:].rearrange("p (t m) -> p t m", t=PACK), in_=w3_raw_s[:].rearrange("p (m t) -> p t m", t=PACK)
         )
         fetch_slice(0)
         fetch_slice(1)
 
-        states = at(AT_STATES + 8 * KIB, "states1", [P, 4, 2, GROUP], F32)
         for g in range(4):
-            early_unit(1, g, states, (g % 2, 2 + g % 2, 4 + g % 2, 4 + g % 2), None)
-        w3_late_w = at(AT_W2_RAW[1], "w3_late_w", [P, BANK], U32)
+            banks = (g % 2, 2 + g % 2, 4 + g % 2, 4 + g % 2)
+            states = at(AT_HELD_STATES[g], f"states1_{g}", [P, 2, GROUP], F32)
+            early_unit(1, g, states, banks)
+        w3_late_w = at(AT_W3_LATE_W, "w3_late_w", [P, BANK], U32)
         nc.scalar.copy(
             out=w3_late_w[:].rearrange("p (t c i) -> p c t i", t=PACK, i=4),
             in_=w3_raw_w[:].bitcast(U32).rearrange("p (c i t) -> p c t i", t=PACK, i=4),
         )
+        pages.append(at(AT_PAGE3, "page3", [P, T2], F32))
+        nc.gpsimd.memset(pages[3][:].bitcast(I32), 0)
         fetch_slice(2)
         fetch_slice(3)
 
-        def late_group(g, parts, gates_at):
-            relu, second, second_at = [], [], []
+        def late_group(g, last_gate_at):
+            relu, copied = [], []
             for e in range(2):
                 first = in_bank(e, [P, BANK])
                 token_product(first[:], 2 * g + e, w1_w[1][:].bitcast(FP4X4), w1_s[:, BANK : 2 * BANK])
                 relu.append(at(AT_RELU + 2 * KIB * next_slot("relu", 4), f"late_relu{g}_{e}", [P, PACK, P], F32))
                 nc.scalar.activation(out=relu[e][:], in_=first[:].rearrange("j (m t) -> j t m", t=PACK), func=ACT.Relu)
             for e in range(2):
-                second.append(in_bank(2 + e, [P, BANK]))
-                token_product(second[e][:], 2 * g + e, w2_w[2][:].bitcast(FP8X4), w2_s[2][:])
-                second_at.append(AT_SECOND + 2 * KIB * next_slot("second", 4))
-            copied = {}
-            for t0, count, c0, c1 in parts:
-                h = late_states[:, t0 : t0 + count, GROUP * g : GROUP * (g + 1)]
-                stationary = [(w3_late_w[:, P * t : P * (t + 1)], w3_late_s[:, P * t : P * (t + 1)]) for t in range(t0, t0 + count)]
-                if c1 > c0:
-                    for e in range(2):
-                        part = at(second_at[e] + 4 * P * c0, f"late_second{g}_{e}_{c0}", [P, c1 - c0, P], F32)
-                        nc.scalar.copy(out=part[:], in_=second[e][:].rearrange("j (m t) -> j t m", t=PACK)[:, c0:c1, :])
-                        for t in range(c0, c1):
-                            copied[e, t] = part[:, t - c0, :]
+                second = in_bank(2 + e, [P, BANK])
+                token_product(second[:], 2 * g + e, w2_w[2][:].bitcast(FP8X4), w2_s[2][:])
+                copied.append(at(AT_SECOND + 2 * KIB * next_slot("second", 4), f"late_second{g}_{e}", [P, PACK, P], F32))
+                nc.scalar.copy(out=copied[e][:], in_=second[:].rearrange("j (m t) -> j t m", t=PACK))
+            for t0 in range(0, PACK, 2):
+                h = late_states[:, t0 : t0 + 2, GROUP * g : GROUP * (g + 1)]
+                stationary = [(w3_late_w[:, P * t : P * (t + 1)], w3_late_s[:, P * t : P * (t + 1)]) for t in range(t0, t0 + 2)]
                 bank = 4 + next_slot("bank", 4)
-                weigh_third(g, stationary, h, late_w[:, t0 : t0 + count, GROUP * g : GROUP * (g + 1)], bank, ACT.Abs)
-                addends = [(relu[e][:, t, :], copied[e, t]) for t in range(t0, t0 + count) for e in range(2)]
-                gate_state(f"late_gate{g}_{t0}", addends, h, gates_at[t0 // 2], bank, True)
-                if (g, t0) == (1, 0):
-                    pages.append(at(AT_LAST_PAGE, "page3", [P, T2], F32))
-                    nc.gpsimd.memset(pages[3][:].bitcast(I32), 0)
-                if g % 2 == 1:
-                    for t in range(t0, t0 + count):
-                        put_state(t, GROUP * (g - 1), late_states[:, t, GROUP * (g - 1) : GROUP * (g + 1)])
+                weigh_third(g, stationary, h, late_w[:, t0 : t0 + 2, GROUP * g : GROUP * (g + 1)], bank, ACT.Abs)
+                addends = [(relu[e][:, t, :], copied[e][:, t, :]) for t in range(t0, t0 + 2) for e in range(2)]
+                gate_state(f"late_gate{g}_{t0}", addends, h, last_gate_at if t0 == 2 else None, bank, True)
+                for t in range(t0, t0 + 2):
+                    if g < 2:
+                        put_state(t, GROUP * g, late_states[:, t, GROUP * g : GROUP * (g + 1)])
+                    if g == 3:
+                        put_state(t, HALF, late_states[:, t, HALF:S])
 
         for g in range(4):
-            late_group(g, ((0, 2, 0, 4), (2, 2, 4, 4)), (AT_LAST_PAGE if g == 1 else None, AT_STATES if g == 3 else None))
+            late_group(g, AT_STATES if g == 3 else None)
         for s in range(4):
-            add_and_turn(s, (2 * (s % 2), 2 * (s % 2) + 1))
+            add_and_turn(s, AT_RELU + 4 * KIB * (s % 2), (2 * (s % 2), 2 * (s % 2) + 1))
 
         woven_w4 = at(AT_STATES, "w4_woven", [P, 2 * N, PACK], BF16)
         interleave(round_on_gpsimd, woven_w4[:, 0:N, :], raw_w4[0][:])

@@ -310,7 +310,7 @@ def tile_list_byte_patch_slots_kernel(
         fetch_slice(1)
 
         for g in range(4):
-            banks = (g % 2, 2 + g % 2, 4 + g % 2, 4 + g % 2)
+            banks = (5, 2 + g % 2, 4 + 2 * (g % 2), 4 + 2 * (g % 2))
             states = at(AT_HELD_STATES[g], f"states1_{g}", [P, 2, GROUP], F32)
             early_unit(1, g, states, banks)
         w3_late_w = at(AT_W3_LATE_W, "w3_late_w", [P, BANK], U32)
@@ -343,10 +343,7 @@ def tile_list_byte_patch_slots_kernel(
                 addends = [(relu[e][:, t, :], copied[e][:, t, :]) for t in range(t0, t0 + 2) for e in range(2)]
                 gate_state(f"late_gate{g}_{t0}", addends, h, last_gate_at if t0 == 2 else None, bank, True)
                 for t in range(t0, t0 + 2):
-                    if g < 2:
-                        put_state(t, GROUP * g, late_states[:, t, GROUP * g : GROUP * (g + 1)])
-                    if g == 3:
-                        put_state(t, HALF, late_states[:, t, HALF:S])
+                    put_state(t, GROUP * g, late_states[:, t, GROUP * g : GROUP * (g + 1)])
 
         for g in range(4):
             late_group(g, AT_STATES if g == 3 else None)
@@ -366,13 +363,15 @@ def tile_list_byte_patch_slots_kernel(
                     nc.tensor.transpose(back[:, i, u, :], pairs[:, i0 + i, u, :], ident[:])
             nc.scalar.copy(out=woven_pairs[:, i0 : i0 + 2], in_=back[:].rearrange("p i u m -> p i m u"))
         w4_w = at(AT_LAST_WORDS, "w4_w", [P, 2 * N], U32)
-        z_w = [at(AT_TABLE, "z_w0", [P, PM], U32), kept("z_w1", [P, PM], U32)]
+        early_words = at(AT_TABLE, "early_words", [P, PM], U32)
+        late_words = {}
 
-        quantize(woven_z[:], z_w[0][:], z_s[0][:])
         quantize(woven_w4[:], w4_w[:], w4_s[:])
+        quantize(woven_z[:], early_words[:], z_s[0][:])
         chunks = ((0, 256), (256, 256), (512, 256), (768, 128), (896, 128))
-        fetched_at = (AT_STATES, AT_STATES + 4 * KIB, AT_GATE, AT_ROWS, AT_ROWS + 2 * KIB)
-        woven_at = (AT_GATE, AT_ROWS, AT_ROWS + 2 * KIB, AT_ROWS + 4 * KIB, AT_ROWS + 4 * KIB)
+        fetched_at = [AT_STATES + 4 * KIB * (c % 2) for c in range(5)]
+        woven_at = [AT_RELU + 2 * KIB * c for c in range(4)] + [fetched_at[3]]
+        words_at = [AT_GATE + KIB * c for c in range(5)]
         chunk_banks = ((0, 1), (4, 5), (6, 7), (2,), (3, 0))
         out_rows = out.rearrange("(nt p) m -> p nt m", p=P)
         sums, woven_late = {}, {}
@@ -388,7 +387,7 @@ def tile_list_byte_patch_slots_kernel(
                     out=sums[c, b][:, i, :],
                     lhsT=w4_w[:, cols].bitcast(FP8X4),
                     lhsT_scale=w4_s[:, cols],
-                    rhs=z_w[a][:, m0 : m0 + width].bitcast(FP8X4),
+                    rhs=(late_words[c][:] if a == 1 else early_words[:, m0 : m0 + width]).bitcast(FP8X4),
                     rhs_scale=z_s[a][:, m0 : m0 + width],
                     start=(a == 0 and i == 0),
                     stop=(a == 1 and i == share - 1),
@@ -412,13 +411,14 @@ def tile_list_byte_patch_slots_kernel(
 
         def finish(c):
             m0, width = chunks[c]
-            quantize(woven_late[c][:], z_w[1][:, m0 : m0 + width], z_s[1][:, m0 : m0 + width])
+            late_words[c] = at(words_at[c], f"late_words{c}", [P, width], U32)
+            quantize(woven_late[c][:], late_words[c][:], z_s[1][:, m0 : m0 + width])
             share = 4 // len(chunk_banks[c])
             for a in range(2):
                 for b in range(len(chunk_banks[c])):
                     last_pass(c, b, a)
             for b in range(len(chunk_banks[c])):
-                result = at(AT_STATES + 16 * m0 + 4 * share * width * b, f"result{c}_{b}", [P, share, width], F32)
+                result = at(AT_CTX + 16 * m0 + 4 * share * width * b, f"result{c}_{b}", [P, share, width], F32)
                 copy = nc.vector.tensor_copy if (c, b) == (len(chunks) - 1, 1) else nc.scalar.copy
                 copy(out=result[:], in_=sums[c, b][:])
                 nc.sync.dma_start(out=out_rows[:, share * b : share * (b + 1), m0 : m0 + width], in_=result[:])

@@ -220,7 +220,7 @@ def tile_list_byte_patch_slots_kernel(
         quantize_w2(0)
         pages.append(at(AT_PAGE2, "page2", [P, T2], F32))
         nc.gpsimd.memset(pages[2][:].bitcast(I32), 0)
-        for g in range(3):
+        for g in range(4):
             gather_words(GROUP * g, kept(f"v_w{g}", [P, GROUP], U32))
 
         turned = at(AT_ROWS, "turned", [P, PM // P, 2, P, 2], BF16)
@@ -260,7 +260,11 @@ def tile_list_byte_patch_slots_kernel(
             plain = at(AT_STATES + 2 * KIB * (4 + g), f"third{g}", [P, 2, GROUP], F32)[:] if pair == 1 and g > 1 else None
             weigh_third(g, stationary, states[:], weights.unsqueeze(1).to_broadcast([P, 2, GROUP]), banks[2], ACT.Copy, plain)
             addends = [(relu[:, e, P * i : P * (i + 1)], copied[:, e, P * i : P * (i + 1)]) for i in range(2) for e in range(2)]
-            gate_state(f"gate{pair}_{g}", addends, states[:], gate_at, banks[3], False)
+            if (pair, g) == (0, 1):
+                for i, bank in enumerate((banks[3], 6)):
+                    gate_state(f"gate{pair}_{g}_{i}", addends[2 * i : 2 * i + 2], states[:, i : i + 1, :], None, bank, False)
+            else:
+                gate_state(f"gate{pair}_{g}", addends, states[:], gate_at, banks[3], False)
             if pair == 0 and g > 1:
                 weave_w2(g - 1)
             if (pair, g) in ((0, 3), (1, 1)):
@@ -293,7 +297,6 @@ def tile_list_byte_patch_slots_kernel(
         states = at(AT_STATES, "states0_0", [P, 2, GROUP], F32)
         for i, banks in enumerate(((0, 1, 2), (3, 0, 4))):
             opening_slice(i, states[:, i, :], banks)
-        gather_words(3 * GROUP, at(AT_FIRST_W, "v_w3", [P, GROUP], U32))
         put_unit(0, states)
         raw_w4 = [load_rows(at(AT_TABLE, "w4_raw0", [P, PACK, N], F32), w4[0:BANK, :])]
         raw_w4.append(load_rows(at(AT_ROWS + 8 * KIB, "w4_raw1", [P, PACK, N], F32), w4[BANK : 2 * BANK, :]))

from contextlib import ExitStack

import concourse.mybir as mybir
from concourse.masks import make_identity

K, T, S, T2, PM, H, N = 512, 2048, 1024, 2048, 1024, 1024, 512
FLOPS = 2 * (3 * K * H * S + H * N * PM)

F32 = mybir.dt.float32
BF16 = mybir.dt.bfloat16
I32 = mybir.dt.int32
U32 = mybir.dt.uint32
U16 = mybir.dt.uint16
U8 = mybir.dt.uint8
FP8X4 = mybir.dt.float8_e4m3fn_x4
FP4X4 = mybir.dt.float4_e2m1fn_x4
ALU = mybir.AluOpType
ACT = mybir.ActivationFunctionType

P = 128
PACK = 4
BANK = 512
GROUP = 256
KIB = 1024
HALF = 512
AT_TABLE = 0
AT_W2_RAW = (8 * KIB, 12 * KIB, 16 * KIB)
AT_FIRST_W = 24 * KIB
AT_PAGE2 = 26 * KIB
AT_W2_WORDS = (34 * KIB, 35 * KIB, 37 * KIB)
AT_PICKED = (92 * KIB, 8 * KIB, 16 * KIB, 12 * KIB)
AT_W2_WOVEN = (AT_PAGE2, 44 * KIB, 48 * KIB)
AT_W3_LATE_S = AT_W2_WOVEN[1] + 768
AT_HELD_STATES = (AT_W3_LATE_S - 2 * KIB, AT_W3_LATE_S + HALF, AT_W2_WOVEN[2], 41 * KIB)
AT_W3_LATE_W = 39 * KIB
AT_PAGE3 = 52 * KIB
AT_RELU = 60 * KIB
AT_SECOND = 68 * KIB
AT_GATE = 76 * KIB
AT_STATES = 84 * KIB
AT_ROWS = 100 * KIB
AT_CTX = 116 * KIB
AT_LAST_WORDS = 132 * KIB


def tile_list_byte_patch_slots_kernel(
    tc, tab_words, tab_scales, offs, w1_words, w1_scales, w2, w3_words, w3_scales, wgs, offs2, offs3, ctx, w4, out
):
    nc = tc.nc
    with ExitStack() as stack:
        keep = stack.enter_context(tc.tile_pool(name="keep", bufs=1))
        shared = stack.enter_context(tc.tile_pool(name="shared", bufs=1))
        psum = stack.enter_context(tc.psum_pool(name="psum", bufs=1))

        def at(offset, name, shape, dtype):
            return shared.tile(shape, dtype, name=name, align_bytes=64, offset=offset)

        def kept(name, shape, dtype):
            return keep.tile(shape, dtype, name=name, align_bytes=64)

        def in_bank(b, shape):
            return psum.tile(shape, F32, name="bank", tag=f"bank{b}")

        list1 = keep.tile([P, S // 16], U16, name="list1")
        list2 = keep.tile([P, S // 16], U16, name="list2")
        list3 = keep.tile([P, PM // 16], U16, name="list3")
        tab_w = at(AT_TABLE, "tab_w", [P, T], I32)
        tab_s = kept("tab_s", [P, T], U8)
        v_s = kept("v_s", [P, S], U8)
        w1_w = [kept(f"w1_w{a}", [P, 2 * BANK], U8) for a in range(2)]
        w1_s = kept("w1_s", [P, H], U8)
        w3_early_w = [kept(f"w3_early_w{h}", [P, GROUP], I32) for h in range(2)]
        w3_early_s = kept("w3_early_s", [P, BANK], U8)
        w3_raw_w = kept("w3_raw_w", [P, BANK], I32)
        w3_raw_s = kept("w3_raw_s", [P, BANK], U8)
        w2_s = [kept(f"w2_s{i}", [P, width], U8) for i, width in enumerate((GROUP, GROUP, BANK))]
        w4_s = kept("w4_s", [P, 2 * N], U8)
        z_s = [kept(f"z_s{a}", [P, PM], U8) for a in range(2)]
        first_w = at(AT_FIRST_W, "first_w", [P, GROUP], F32)
        early_w = [kept(f"early_w{i}", [P, HALF], F32) for i in range(2)]
        late_w = kept("late_w", [P, PACK, S], F32)
        late_states = kept("late_states", [P, PACK, S], F32)
        late_ctx = kept("late_ctx", [P, PACK, PM], F32)
        pages = [kept(f"page{t}", [P, T2], F32) for t in range(2)]
        ident = kept("ident", [P, P], F32)

        def load_scales(plane, rows, c0, quadrants=range(4), queue=nc.sync):
            width = plane.shape[1]
            for q in quadrants:
                queue.dma_start(
                    out=plane[32 * q : 32 * q + 4, :].bitcast(I32), in_=rows[0, 4 * q : 4 * q + 4, c0 : c0 + width].bitcast(I32)
                )

        def load_rows(tile, rows):
            nc.sync.dma_start(out=tile[:], in_=rows.rearrange("(p t) c -> p t c", t=PACK))
            return tile

        def load_w3_words(tile, c0):
            words = w3_words[0].rearrange("p c i -> p (c i)").bitcast(I32)
            nc.sync.dma_start(out=tile[:], in_=words[:, c0 : c0 + tile.shape[1]])

        def load_w1_words(a):
            nc.sync.dma_start(out=w1_w[a][:].bitcast(I32), in_=w1_words[0, :, 2 * BANK * a : 2 * BANK * (a + 1)].bitcast(I32))

        def interleave(copy, woven, planes):
            copy(out=woven.rearrange("p (c i) t -> p c t i", i=4), in_=planes.rearrange("p t (c i) -> p c t i", i=4))

        def weave_on_scalar(woven, planes, step=GROUP):
            for c0 in range(0, woven.shape[1], step):
                interleave(nc.scalar.copy, woven[:, c0 : c0 + step, :], planes[:, :, c0 : c0 + step])

        def round_on_gpsimd(out, in_):
            nc.gpsimd.tensor_scalar(out=out, in0=in_, scalar1=1.0, scalar2=0.0, op0=ALU.mult, op1=ALU.add)

        def quantize(woven, words, scales):
            nc.vector.quantize_mx(out=words.bitcast(FP8X4), scales=scales, in_=woven.rearrange("p c t -> p (c t)"))

        w2_woven, w2_w, v_w = {}, {}, {}

        def weave_w2(i):
            w2_woven[i] = at(AT_W2_WOVEN[i], f"w2_woven{i}", [P, w2_s[i].shape[1], PACK], BF16)
            weave_on_scalar(w2_woven[i][:], w2_raw[i][:], P if i > 0 else GROUP)

        def quantize_w2(i):
            w2_w[i] = at(AT_W2_WORDS[i], f"w2_w{i}", [P, w2_s[i].shape[1]], U32)
            quantize(w2_woven[i][:], w2_w[i][:], w2_s[i][:])

        def gather_words(j0, words):
            width = words.shape[1]
            nc.vector.tensor_copy(out=words[:], in_=tab_w[:].bitcast(U32).indirect(list1[:, j0 // 16 : (j0 + width) // 16]))
            for c0 in range(0, width, GROUP):
                v_w[(j0 + c0) // GROUP] = words[:, c0 : c0 + GROUP]

        def product(acc, lhs_words, lhs_scales, rhs_words, rhs_scales):
            nc.tensor.matmul_mx(
                out=acc, lhsT=lhs_words, lhsT_scale=lhs_scales, rhs=rhs_words, rhs_scale=rhs_scales, start=True, stop=True
            )

        def token_product(acc, e, words, scales):
            cols = slice(P * (e % 2), P * (e % 2 + 1))
            product(acc, v_w[e // 2][:, cols].bitcast(FP8X4), v_s[:, P * e : P * (e + 1)], words, scales)

        def row_product(acc, g, words, scales):
            product(acc, words, scales, v_w[g].bitcast(FP8X4), v_s[:, GROUP * g : GROUP * (g + 1)])

        turn = {"relu": 1, "second": 1, "gate": 0, "bank": 2}

        def next_slot(kind, count):
            turn[kind] = turn[kind] + 1
            return (turn[kind] - 1) % count

        def weigh_third(g, stationary, h, weights, bank, func, plain=None):
            third = in_bank(bank, [P, len(stationary), GROUP])
            for i, (words, scales) in enumerate(stationary):
                row_product(third[:, i, :], g, words.bitcast(FP8X4), scales)
            plain = h if plain is None else plain
            nc.scalar.activation(out=plain, in_=third[:], func=func)
            nc.gpsimd.tensor_tensor(out=h, in0=plain, in1=weights, op=ALU.mult)

        def gate_state(name, addends, h, gate_at, bank, absolute):
            count = len(addends) // 2
            q = in_bank(bank, [P, count, GROUP])
            for i, (relu, second) in enumerate(addends):
                cols = q[:, i // 2, P * (i % 2) : P * (i % 2 + 1)]
                nc.tensor.matmul(cols, lhsT=relu, rhs=ident[:], is_transpose=True, start=True, stop=False)
                nc.tensor.matmul(cols, lhsT=second, rhs=ident[:], is_transpose=True, start=False, stop=True)
            if gate_at is None:
                gate_at = AT_GATE + 2 * KIB * next_slot("gate", 4)
            gate = at(gate_at, name, [P, count, GROUP], F32)
            nc.scalar.activation(out=gate[:], in_=q[:], func=ACT.Silu)
            if absolute:
                nc.scalar.activation(out=gate[:], in_=gate[:], func=ACT.Abs)
            nc.gpsimd.tensor_tensor(out=h, in0=h, in1=gate[:], op=ALU.mult)

        def put_state(page, j0, state):
            picks = list2[:, j0 // 16 : (j0 + state.shape[1]) // 16]
            nc.vector.tensor_copy(out=pages[page][:].indirect(picks), in_=state)

        load_scales(w3_early_s, w3_scales, 0, range(1, 4), nc.gpsimd)
        nc.gpsimd.memset(pages[1][:].bitcast(I32), 0)
        make_identity(nc, ident[:])
        nc.gpsimd.memset(w3_raw_s[:].bitcast(I32), 0)
        warm = keep.tile([P, 2], F32, name="warm")
        nc.vector.memset(warm[:, 0:1], 0.0)
        nc.scalar.activation(out=warm[:, 1:2], in_=warm[:, 0:1], func=ACT.Silu)
        nc.vector.memset(pages[0][:, 0 : S - 1].bitcast(I32), 0)
        nc.vector.memset(pages[0][:, S - 1 : T2].bitcast(I32), 0)
        nc.sync.dma_start(list1[:], offs)
        for q in range(4):
            rows = tab_scales[0, 4 * q : 4 * q + 4, :].bitcast(I32)
            nc.sync.dma_start(out=tab_s[32 * q : 32 * q + 32, :].bitcast(I32), in_=rows.unsqueeze(0).to_broadcast([8, 4, T // 4]))
        w2_raw = [load_rows(at(AT_W2_RAW[0], "w2_raw0", [P, PACK, GROUP], F32), w2[:, 0:GROUP])]
        load_scales(w1_s, w1_scales, 0, range(1))
        nc.sync.dma_start(out=tab_w[:], in_=tab_words[0].rearrange("p c i -> p (c i)").bitcast(I32))
        load_w1_words(0)
        load_scales(w1_s, w1_scales, 0, range(1, 4))
        load_w3_words(w3_early_w[0], 0)
        load_scales(w3_early_s, w3_scales, 0, range(1))
        nc.sync.dma_start(out=first_w[:], in_=wgs[:, 0:GROUP])
        nc.sync.dma_start(list2[:], offs2)
        nc.sync.dma_start(out=early_w[0][:], in_=wgs[:, 0:HALF])
        w2_raw.append(load_rows(at(AT_W2_RAW[1], "w2_raw1", [P, PACK, GROUP], F32), w2[:, GROUP:BANK]))
        nc.sync.dma_start(out=early_w[1][:], in_=wgs[:, HALF:S])
        load_w3_words(w3_early_w[1], GROUP)
        nc.sync.dma_start(list3[:], offs3)
        load_scales(w3_raw_s, w3_scales, BANK)
        w2_raw.append(load_rows(at(AT_W2_RAW[2], "w2_raw2", [P, PACK, BANK], F32), w2[:, BANK : 2 * BANK]))
        load_w3_words(w3_raw_w, BANK)
        early_ctx = [at(AT_CTX + 4 * KIB * s, f"early_ctx{s}", [P, PM], F32) for s in range(4)]
        for s in range(2):
            nc.sync.dma_start(out=early_ctx[s][:], in_=ctx[P * s : P * (s + 1), :])
        load_w1_words(1)
        for q in range(4):
            nc.sync.dma_start(out=late_w[32 * q : 32 * q + 32], in_=wgs.rearrange("(m t) j -> m t j", t=PACK))
        for s in range(2, 4):
            nc.sync.dma_start(out=early_ctx[s][:], in_=ctx[P * s : P * (s + 1), :])

        nc.vector.tensor_copy(out=v_s[:], in_=tab_s[:].indirect(list1[:]))
        weave_w2(0)
        quantize_w2(0)
        pages.append(at(AT_PAGE2, "page2", [P, T2], F32))
        nc.gpsimd.memset(pages[2][:].bitcast(I32), 0)
        for g in range(4):
            gather_words(GROUP * g, kept(f"v_w{g}", [P, GROUP], U32))

        turned = at(AT_ROWS, "turned", [P, PM // P, 2, P, 2], BF16)
        picked = {}

        def opening_slice(i, h, banks):
            cols = slice(P * i, P * (i + 1))
            first = in_bank(banks[0], [P, GROUP])
            row_product(first[:], 0, w1_w[0][:, 2 * P * i : 2 * P * (i + 1)].bitcast(FP4X4), w1_s[:, cols])
            relu = at(AT_RELU + KIB * i, f"opening_relu{i}", [P, GROUP], F32)
            nc.scalar.activation(out=relu[:], in_=first[:], func=ACT.Relu)
            second = in_bank(banks[1], [P, GROUP])
            row_product(second[:], 0, w2_w[0][:, cols].bitcast(FP8X4), w2_s[0][:, cols])
            gate = at(AT_GATE + 2 * KIB * next_slot("gate", 4), f"opening_gate{i}", [P, GROUP], F32)
            nc.vector.tensor_tensor(out=gate[:], in0=second[:], in1=relu[:], op=ALU.add)
            nc.scalar.activation(out=gate[:], in_=gate[:], func=ACT.Silu)
            third = in_bank(banks[2], [P, GROUP])
            row_product(third[:], 0, w3_early_w[0][:, cols].bitcast(FP8X4), w3_early_s[:, cols])
            nc.vector.tensor_tensor(out=h, in0=third[:], in1=first_w[:], op=ALU.mult)
            nc.gpsimd.tensor_tensor(out=h, in0=h, in1=gate[:], op=ALU.mult)

        def early_unit(pair, g, states, banks):
            first, second = in_bank(banks[0], [P, 2, GROUP]), in_bank(banks[1], [P, 2, GROUP])
            c0 = GROUP * pair
            for i in range(2):
                token_product(first[:, i, :], 2 * g + i, w1_w[0][:, 2 * c0 : 2 * (c0 + GROUP)].bitcast(FP4X4), w1_s[:, c0 : c0 + GROUP])
            relu = at(AT_RELU + 2 * KIB * next_slot("relu", 4), f"relu{pair}_{g}", [P, 2, GROUP], F32)
            nc.scalar.activation(out=relu[:], in_=first[:], func=ACT.Relu)
            for i in range(2):
                token_product(second[:, i, :], 2 * g + i, w2_w[pair][:].bitcast(FP8X4), w2_s[pair][:])
            second_at = AT_SECOND + 2 * KIB * next_slot("second", 4)
            gate_at = {(0, 3): AT_W2_WORDS[1], (1, 1): AT_W2_WORDS[2], (1, 2): AT_W3_LATE_W + KIB, (1, 3): AT_PAGE3}.get((pair, g))
            copied = at(AT_W2_WOVEN[g - 1] if pair == 0 and g > 1 else second_at, f"second{pair}_{g}", [P, 2, GROUP], F32)
            nc.scalar.copy(out=copied[:], in_=second[:])
            weights = early_w[g // 2][:, GROUP * (g % 2) : GROUP * (g % 2 + 1)]
            stationary = [(w3_early_w[pair][:, P * i : P * (i + 1)], w3_early_s[:, c0 + P * i : c0 + P * (i + 1)]) for i in range(2)]
            plain = at(AT_STATES + 2 * KIB * (4 + g), f"third{g}", [P, 2, GROUP], F32)[:] if pair == 1 and g > 1 else None
            weigh_third(g, stationary, states[:], weights.unsqueeze(1).to_broadcast([P, 2, GROUP]), banks[2], ACT.Copy, plain)
            addends = [(relu[:, e, P * i : P * (i + 1)], copied[:, e, P * i : P * (i + 1)]) for i in range(2) for e in range(2)]
            if (pair, g) == (0, 1):
                for i, bank in enumerate((banks[3], 6)):
                    gate_state(f"gate{pair}_{g}_{i}", addends[2 * i : 2 * i + 2], states[:, i : i + 1, :], None, bank, False)
            else:
                gate_state(f"gate{pair}_{g}", addends, states[:], gate_at, banks[3], False)
            if pair == 0 and g > 1:
                weave_w2(g - 1)
            if (pair, g) in ((0, 3), (1, 1)):
                quantize_w2(pair + 1)
            put_unit(g, states)

        def put_unit(g, states):
            for i in range(2):
                put_state(i, GROUP * g, states[:, i, :])

        def fetch_slice(s):
            picked[s] = at(AT_PICKED[s], f"picked{s}", [P, PM], F32)
            nc.vector.tensor_copy(out=picked[s][:], in_=pages[s % 2][:].indirect(list3[:]))

        def add_and_turn(s, size_at, banks):
            size = at(size_at, f"size{s}", [P, PM], F32)
            for half, bank in enumerate(banks):
                cols = slice(HALF * half, HALF * (half + 1))
                nc.scalar.activation(out=size[:, cols], in_=picked[s][:, cols], func=ACT.Abs)
                total = in_bank(bank, [P, 4, P])
                for i in range(4):
                    tile_cols = slice(HALF * half + P * i, HALF * half + P * (i + 1))
                    nc.tensor.matmul(total[:, i, :], lhsT=early_ctx[s][:, tile_cols], rhs=ident[:], is_transpose=True, start=True, stop=False)
                    nc.tensor.matmul(total[:, i, :], lhsT=size[:, tile_cols], rhs=ident[:], is_transpose=True, start=False, stop=True)
                nc.scalar.copy(
                    out=turned[:, 4 * half : 4 * (half + 1), :, 32 * s : 32 * (s + 1), :],
                    in_=total[:].rearrange("m i (q u e) -> m i u q e", u=2, e=2),
                )

        states = at(AT_STATES, "states0_0", [P, 2, GROUP], F32)
        for i, banks in enumerate(((0, 1, 2), (3, 0, 4))):
            opening_slice(i, states[:, i, :], banks)
        put_unit(0, states)
        raw_w4 = [load_rows(at(AT_TABLE, "w4_raw0", [P, PACK, N], F32), w4[0:BANK, :])]
        raw_w4.append(load_rows(at(AT_ROWS + 8 * KIB, "w4_raw1", [P, PACK, N], F32), w4[BANK : 2 * BANK, :]))
        load_rows(late_ctx, ctx[BANK : 2 * BANK, :])
        for g in range(1, 4):
            banks = {1: (5, 2, 1, 4), 2: (1, 2, 4, 3), 3: (2, 1, 4, 5)}[g]
            states = at(AT_STATES + 2 * KIB * g, f"states0_{g}", [P, 2, GROUP], F32)
            early_unit(0, g, states, banks)
        w3_late_s = at(AT_W3_LATE_S, "w3_late_s", [P, BANK], U8)
        nc.gpsimd.tensor_copy(
            out=w3_late_s[:].rearrange("p (t m) -> p t m", t=PACK), in_=w3_raw_s[:].rearrange("p (m t) -> p t m", t=PACK)
        )
        fetch_slice(0)
        fetch_slice(1)

        for g in range(4):
            banks = (5, 2 + g % 2, 4 + 2 * (g % 2), 4 + 2 * (g % 2))
            states = at(AT_HELD_STATES[g], f"states1_{g}", [P, 2, GROUP], F32)
            early_unit(1, g, states, banks)
        w3_late_w = at(AT_W3_LATE_W, "w3_late_w", [P, BANK], U32)
        nc.scalar.copy(
            out=w3_late_w[:].rearrange("p (t c i) -> p c t i", t=PACK, i=4),
            in_=w3_raw_w[:].bitcast(U32).rearrange("p (c i t) -> p c t i", t=PACK, i=4),
        )
        pages.append(at(AT_PAGE3, "page3", [P, T2], F32))
        nc.gpsimd.memset(pages[3][:].bitcast(I32), 0)
        fetch_slice(2)
        fetch_slice(3)

        def late_group(g, last_gate_at):
            relu, copied = [], []
            for e in range(2):
                first = in_bank(e, [P, BANK])
                token_product(first[:], 2 * g + e, w1_w[1][:].bitcast(FP4X4), w1_s[:, BANK : 2 * BANK])
                relu.append(at(AT_RELU + 2 * KIB * next_slot("relu", 4), f"late_relu{g}_{e}", [P, PACK, P], F32))
                nc.scalar.activation(out=relu[e][:], in_=first[:].rearrange("j (m t) -> j t m", t=PACK), func=ACT.Relu)
            for e in range(2):
                second = in_bank(2 + e, [P, BANK])
                token_product(second[:], 2 * g + e, w2_w[2][:].bitcast(FP8X4), w2_s[2][:])
                copied.append(at(AT_SECOND + 2 * KIB * next_slot("second", 4), f"late_second{g}_{e}", [P, PACK, P], F32))
                nc.scalar.copy(out=copied[e][:], in_=second[:].rearrange("j (m t) -> j t m", t=PACK))
            for t0 in range(0, PACK, 2):
                h = late_states[:, t0 : t0 + 2, GROUP * g : GROUP * (g + 1)]
                stationary = [(w3_late_w[:, P * t : P * (t + 1)], w3_late_s[:, P * t : P * (t + 1)]) for t in range(t0, t0 + 2)]
                bank = 4 + next_slot("bank", 4)
                weigh_third(g, stationary, h, late_w[:, t0 : t0 + 2, GROUP * g : GROUP * (g + 1)], bank, ACT.Abs)
                addends = [(relu[e][:, t, :], copied[e][:, t, :]) for t in range(t0, t0 + 2) for e in range(2)]
                gate_state(f"late_gate{g}_{t0}", addends, h, last_gate_at if t0 == 2 else None, bank, True)
                for t in range(t0, t0 + 2):
                    put_state(t, GROUP * g, late_states[:, t, GROUP * g : GROUP * (g + 1)])

        for g in range(4):
            late_group(g, AT_STATES if g == 3 else None)
        for s in range(4):
            add_and_turn(s, AT_RELU + 4 * KIB * (s % 2), (2 * (s % 2), 2 * (s % 2) + 1))

        woven_w4 = at(AT_STATES, "w4_woven", [P, 2 * N, PACK], BF16)
        interleave(round_on_gpsimd, woven_w4[:, 0:N, :], raw_w4[0][:])
        weave_on_scalar(woven_w4[:, N : 2 * N, :], raw_w4[1][:])
        woven_z = at(AT_SECOND, "z0_woven", [P, PM, PACK], BF16)
        pairs = turned[:].rearrange("m i u p e -> m (i u p e)").bitcast(F32).rearrange("m (i u p) -> m i u p", u=2, p=P)
        woven_pairs = woven_z[:].rearrange("p m t -> p (m t)").bitcast(F32).rearrange("p (i m u) -> p i m u", m=P, u=2)
        for i0 in range(0, PM // P, 2):
            back = in_bank(i0 // 2, [P, 2, 2, P])
            for i in range(2):
                for u in range(2):
                    nc.tensor.transpose(back[:, i, u, :], pairs[:, i0 + i, u, :], ident[:])
            nc.scalar.copy(out=woven_pairs[:, i0 : i0 + 2], in_=back[:].rearrange("p i u m -> p i m u"))
        w4_w = at(AT_LAST_WORDS, "w4_w", [P, 2 * N], U32)
        early_words = at(AT_TABLE, "early_words", [P, PM], U32)
        late_words = {}

        quantize(woven_w4[:], w4_w[:], w4_s[:])
        quantize(woven_z[:], early_words[:], z_s[0][:])
        chunks = ((0, 256), (256, 256), (512, 256), (768, 128), (896, 128))
        fetched_at = [AT_STATES + 4 * KIB * (c % 2) for c in range(5)]
        woven_at = [AT_RELU + 2 * KIB * c for c in range(4)] + [fetched_at[3]]
        words_at = [AT_GATE + KIB * c for c in range(5)]
        chunk_banks = ((0, 1), (4, 5), (6, 7), (2,), (3, 0))
        out_rows = out.rearrange("(nt p) m -> p nt m", p=P)
        sums, woven_late = {}, {}

        def last_pass(c, b, a):
            m0, width = chunks[c]
            share = 4 // len(chunk_banks[c])
            if a == 0:
                sums[c, b] = in_bank(chunk_banks[c][b], [P, share, width])
            for i in range(share):
                cols = slice(N * a + P * (share * b + i), N * a + P * (share * b + i + 1))
                nc.tensor.matmul_mx(
                    out=sums[c, b][:, i, :],
                    lhsT=w4_w[:, cols].bitcast(FP8X4),
                    lhsT_scale=w4_s[:, cols],
                    rhs=(late_words[c][:] if a == 1 else early_words[:, m0 : m0 + width]).bitcast(FP8X4),
                    rhs_scale=z_s[a][:, m0 : m0 + width],
                    start=(a == 0 and i == 0),
                    stop=(a == 1 and i == share - 1),
                )

        def fetch_chunk(c):
            m0, width = chunks[c]
            z = at(fetched_at[c], f"z1_{c}", [P, PACK, width], F32)
            for t in range(PACK):
                nc.vector.tensor_tensor(
                    out=z[:, t, :],
                    in0=pages[t][:].indirect(list3[:, m0 // 16 : (m0 + width) // 16]),
                    in1=late_ctx[:, t, m0 : m0 + width],
                    op=ALU.add,
                )
            return z

        def weave_chunk(c, z, copy):
            woven_late[c] = at(woven_at[c], f"z1_woven{c}", [P, chunks[c][1], PACK], BF16)
            interleave(copy, woven_late[c][:], z[:])

        def finish(c):
            m0, width = chunks[c]
            late_words[c] = at(words_at[c], f"late_words{c}", [P, width], U32)
            quantize(woven_late[c][:], late_words[c][:], z_s[1][:, m0 : m0 + width])
            share = 4 // len(chunk_banks[c])
            for a in range(2):
                for b in range(len(chunk_banks[c])):
                    last_pass(c, b, a)
            for b in range(len(chunk_banks[c])):
                result = at(AT_CTX + 16 * m0 + 4 * share * width * b, f"result{c}_{b}", [P, share, width], F32)
                copy = nc.vector.tensor_copy if (c, b) == (len(chunks) - 1, 1) else nc.scalar.copy
                copy(out=result[:], in_=sums[c, b][:])
                nc.sync.dma_start(out=out_rows[:, share * b : share * (b + 1), m0 : m0 + width], in_=result[:])

        for c in range(2):
            weave_chunk(c, fetch_chunk(c), nc.scalar.copy)
        finish(0)
        weave_chunk(2, fetch_chunk(2), nc.scalar.copy)
        finish(1)
        weave_chunk(3, fetch_chunk(3), nc.scalar.copy)
        finish(2)
        z = fetch_chunk(4)
        finish(3)
        weave_chunk(4, z, nc.vector.tensor_copy)
        finish(4)
